import numpy as np
import ml_dtypes


def mxq(x, axis, fmt="e4m3"):
    dtype, down = {"e4m3": (ml_dtypes.float8_e4m3fn, 7), "e5m2": (ml_dtypes.float8_e5m2, 14)}[fmt]
    v = np.moveaxis(np.asarray(x, np.float32).astype(ml_dtypes.bfloat16).astype(np.float64), axis, -1)
    blocks = v.reshape(v.shape[:-1] + (-1, 32))
    amax = np.abs(blocks).max(-1, keepdims=True)
    byte = np.maximum(np.where(amax > 0, np.frexp(amax)[1] - 1 + 127, 0) - down, 1)
    scale = np.exp2(byte - 127.0)
    codes = (blocks / scale).astype(np.float32).astype(dtype).astype(np.float64)
    return np.moveaxis((codes * scale).reshape(v.shape), -1, axis)


WIDE = False


def mx_kscale(k):
    if not WIDE:
        return np.ones(k)
    levels = np.array([10, -10, 5, -5, 0])
    if k % 512:
        return np.exp2(np.random.permutation(np.resize(levels, k // 32))).repeat(32)
    a = np.empty((k // 512, 16))
    for p in range(k // 512):
        a[p, :8] = np.random.permutation(np.resize(levels, 8))
        for g in range(8):
            far = levels[np.abs(levels - a[p, g]) >= 10]
            a[p, g + 8] = far[np.random.randint(len(far))]
    return np.exp2(a.ravel()).repeat(32)


def f64(x):
    return np.asarray(x).astype(np.float64)


def striped(idx):
    return np.tile(idx.reshape(-1, 16).T, (8, 1)).astype(np.uint16)


def unstriped(offs):
    return offs[:16].T.reshape(-1).astype(np.int64)


E2M1 = np.array([0.0, 0.5, 1.0, 1.5, 2.0, 3.0, 4.0, 6.0, -0.0, -0.5, -1.0, -1.5, -2.0, -3.0, -4.0, -6.0])


def pack_weight(w, fmt):
    k, n = w.shape
    w = f64(np.asarray(w, np.float32).astype(ml_dtypes.bfloat16)).reshape(k // 32, 32, n)
    amax = np.abs(w).max(1)
    if fmt == "e4m3":
        byte = np.frexp(amax)[1] - 1 + 127 - 7
    else:
        mant, ex = np.frexp(amax / 6.0)
        byte = np.where(mant > 0.5, ex, ex - 1) + 127
    byte = np.clip(np.where(amax > 0, byte, 1), 1, 254)
    scaled = (w * np.exp2(127.0 - byte)[:, None, :]).reshape(k, n).astype(np.float32)
    by_word = np.ascontiguousarray(scaled.reshape(k // 512, 128, 4, n).transpose(0, 1, 3, 2))
    if fmt == "e4m3":
        words = by_word.astype(ml_dtypes.float8_e4m3fn).view(np.uint8)
    else:
        c = by_word.astype(ml_dtypes.float4_e2m1fn).view(np.uint8) & 0xF
        words = (c[..., 0::2] | (c[..., 1::2] << 4)).reshape(k // 512, 128, 2 * n)
    return np.ascontiguousarray(words), np.ascontiguousarray(byte.astype(np.uint8).reshape(k // 512, 16, n))


def unpack_weight(words, scales, fmt):
    g, _, n = scales.shape
    words = np.ascontiguousarray(words).reshape(g, 128, n, -1)
    if fmt == "e4m3":
        vals = words.view(ml_dtypes.float8_e4m3fn).astype(np.float64)
    else:
        nib = np.empty((g, 128, n, 4), np.uint8)
        nib[..., 0::2] = words & 0xF
        nib[..., 1::2] = words >> 4
        vals = E2M1[nib]
    vals = vals * np.repeat(np.exp2(scales.astype(np.float64) - 127.0), 8, axis=1)[..., None]
    return vals.transpose(0, 1, 3, 2).reshape(g * 512, n)


def gelu(v):
    return 0.5 * v * (1.0 + np.tanh(np.sqrt(2.0 / np.pi) * (v + 0.044715 * v**3)))


K, T, S, H, T2, P, N = 1024, 4096, 1024, 1024, 2048, 1024, 512

def setup_inputs():
    n = np.random.standard_normal
    s = mx_kscale(K)[:, None]
    u = mx_kscale(H)[:, None]
    tab_words, tab_scales = pack_weight(n((K, T)) * s, "e4m3")
    w4_words, w4_scales = pack_weight(0.7 * n((K, H)) / np.sqrt(K) / s, "e2m1")
    return {
        "tab_words": tab_words, "tab_scales": tab_scales,
        "offs": striped(np.random.permutation(T)[:S]),
        "w4_words": w4_words, "w4_scales": w4_scales,
        "cub": np.random.uniform(0.1, 0.3, H).astype(np.float32),
        "offs2": striped(np.random.permutation(T2)[:S]),
        "wgs": np.exp(0.3 * n((128, S))).astype(np.float32),
        "shelf": (np.exp(0.3 * n((H, T2))) * u).astype(np.float32),
        "w2": (1.2 * n((H, N)) / np.sqrt(H) / u).astype(np.float32),
        "offs3": striped(np.random.permutation(T2)[:P]),
        "base": (0.7 * n(N)).astype(np.float32),
        "offs4": striped(np.random.permutation(T2)[:P]),
        "wgo": np.exp(0.3 * n((128, P))).astype(np.float32),
    }

def reference(tab_words, tab_scales, offs, w4_words, w4_scales, cub, offs2, wgs, shelf, w2, offs3, base, offs4, wgo):
    v = unpack_weight(tab_words, tab_scales, "e4m3")[:, unstriped(offs)]
    w4 = unpack_weight(w4_words, w4_scales, "e2m1")
    p = w4.T @ v
    h = p + f64(cub)[:, None] * p ** 3
    page = np.zeros((H, T2))
    page[:, unstriped(offs2)] = np.tile(f64(wgs), (H // 128, 1)) * h
    z = page * f64(shelf)
    y = mxq(f64(w2), 0, "e4m3").T @ mxq(z, 0, "e4m3")
    x = y[:, unstriped(offs3)] + f64(base)[:, None]
    x = 1.0 / (1.0 + np.exp(-x))
    out = np.zeros((N, T2))
    out[:, unstriped(offs4)] = np.tile(f64(wgo), (N // 128, 1)) * x
    return out

@@ -1,0 +1,267 @@
+from contextlib import ExitStack
+
+import concourse.mybir as mybir
+
+K, T, S, H, T2, PICKS, N = 1024, 4096, 1024, 1024, 2048, 1024, 512
+FLOPS = 2 * K * H * S + 2 * H * N * T2
+
+F32 = mybir.dt.float32
+BF16 = mybir.dt.bfloat16
+I32 = mybir.dt.int32
+U32 = mybir.dt.uint32
+U16 = mybir.dt.uint16
+U8 = mybir.dt.uint8
+FP8X4 = mybir.dt.float8_e4m3fn_x4
+FP4X4 = mybir.dt.float4_e2m1fn_x4
+ACT = mybir.ActivationFunctionType
+MULT = mybir.AluOpType.mult
+
+P = 128
+PACK = 4
+BANK = 512
+K_PASSES = K // (P * PACK)
+H_PASSES = H // (P * PACK)
+N_TILES = N // P
+PER_COLUMN = 16
+
+
+def tile_list_audiobook_banner_scores_kernel(
+    tc, tab_words, tab_scales, offs, w4_words, w4_scales, cub, offs2, wgs, shelf, w2, offs3, base, offs4, wgo, out
+):
+    nc = tc.nc
+    with ExitStack() as ctx:
+        keep = ctx.enter_context(tc.tile_pool(name="keep", bufs=1))
+        ring2 = ctx.enter_context(tc.tile_pool(name="ring2", bufs=2))
+        ring3 = ctx.enter_context(tc.tile_pool(name="ring3", bufs=3))
+        ring4 = ctx.enter_context(tc.tile_pool(name="ring4", bufs=4))
+        psum = ctx.enter_context(tc.psum_pool(name="psum", bufs=4))
+
+        lists = []
+        for name, src in (("offs", offs), ("offs2", offs2), ("offs3", offs3), ("offs4", offs4)):
+            tile = keep.tile([P, S // PER_COLUMN], U16, name=name + "_sb")
+            nc.sync.dma_start(tile[:], src)
+            lists.append(tile)
+        picked, shelved, promoted, slots = lists
+
+        def part(tile, lo, hi):
+            return tile[:, lo // PER_COLUMN : hi // PER_COLUMN]
+
+        cub_sb = keep.tile([P, H_PASSES, PACK], F32)
+        nc.sync.dma_start(cub_sb[:], cub.rearrange("(b p t) -> p b t", b=H_PASSES, t=PACK))
+        base_sb = keep.tile([P, N_TILES], F32)
+        with nc.allow_non_contiguous_dma(reason="one bias value a partition"):
+            nc.sync.dma_start(base_sb[:], base.rearrange("(c p) -> p c", p=P))
+
+        tab_scale_sb = keep.tile([P, K_PASSES, T], U8, align_bytes=64)
+        nc.gpsimd.memset(tab_scale_sb[:].bitcast(I32), 0)
+        w4_scale_raw = keep.tile([P, K_PASSES, H], U8, align_bytes=64)
+        nc.gpsimd.memset(w4_scale_raw[:].bitcast(I32), 0)
+        for q in range(4):
+            nc.scalar.dma_start(
+                w4_scale_raw[32 * q : 32 * q + 4, :, :].bitcast(I32),
+                w4_scales[:, 4 * q : 4 * q + 4, :].rearrange("a r n -> r a n").bitcast(I32),
+            )
+        w4_raw = keep.tile([P, K_PASSES, 2 * H], U8, align_bytes=64)
+        nc.sync.dma_start(w4_raw[:].bitcast(I32), w4_words.rearrange("a p n -> p a n").bitcast(I32))
+        for q in range(4):
+            nc.sync.dma_start(
+                tab_scale_sb[32 * q : 32 * q + 4, :, :].bitcast(I32),
+                tab_scales[:, 4 * q : 4 * q + 4, :].rearrange("a r n -> r a n").bitcast(I32),
+            )
+        tab_sb = []
+        for a in range(K_PASSES):
+            words = keep.tile([P, T], U32, name="tab_sb%d" % a, align_bytes=64)
+            nc.sync.dma_start(words[:].bitcast(I32), tab_words[a].rearrange("p n t -> p (n t)").bitcast(I32))
+            tab_sb.append(words)
+
+        wgs_rows = wgs.rearrange("(p t) j -> p t j", t=PACK)
+        wgs_first = keep.tile([P, 1, S], F32)
+        wgs_rest = keep.tile([P, PACK - 1, S], F32)
+        for q in range(4):
+            nc.sync.dma_start(wgs_first[32 * q : 32 * q + 32, :, :], wgs_rows[:, 0:1, :])
+        shelf_rows = shelf.rearrange("(b p t) c -> b t p c", b=H_PASSES, t=PACK)
+
+        def load_shelf(i):
+            rows = ring3.tile([P, T2], F32, name="rows", tag="wide")
+            nc.sync.dma_start(rows[:], shelf_rows[i // PACK, i % PACK])
+            return rows
+
+        shelf_sb = {0: load_shelf(0)}
+        for q in range(4):
+            nc.sync.dma_start(wgs_rest[32 * q : 32 * q + 32, :, :], wgs_rows[:, 1:PACK, :])
+
+        def wgs_of(t):
+            return wgs_first[:, 0, :] if t == 0 else wgs_rest[:, t - 1, :]
+
+        pages = []
+        for i in range(2):
+            page = keep.tile([P, T2], F32, name="page%d" % i)
+            nc.gpsimd.memset(page[:], 0.0)
+            pages.append(page)
+        banners = []
+        for i in range(2):
+            banner = keep.tile([P, T2], F32, name="banner%d" % i)
+            nc.gpsimd.memset(banner[:], 0.0)
+            banners.append(banner)
+
+        w4_sb = keep.tile([P, K_PASSES, 2 * H], U8, align_bytes=64)
+        nc.vector.tensor_copy(
+            w4_sb[:].bitcast(U16).rearrange("p a (b t m) -> p (a b) t m", b=H_PASSES, t=PACK),
+            w4_raw[:].bitcast(U16).rearrange("p a (b m t) -> p (a b) t m", b=H_PASSES, t=PACK),
+        )
+        w4_scale_sb = keep.tile([P, K_PASSES, H], U8, align_bytes=64)
+        nc.vector.tensor_copy(
+            w4_scale_sb[:].rearrange("p a (b t m) -> p (a b) t m", b=H_PASSES, t=PACK),
+            w4_scale_raw[:].rearrange("p a (b m t) -> p (a b) t m", b=H_PASSES, t=PACK),
+        )
+
+        v_scale = keep.tile([P, K_PASSES, S], U8, align_bytes=64)
+        for a in range(K_PASSES):
+            nc.vector.tensor_copy(v_scale[:, a, :], tab_scale_sb[:, a, :].indirect(picked[:]))
+        v_codes = []
+        for a in range(K_PASSES):
+            codes = keep.tile([P, S], U32, name="v_codes%d" % a, align_bytes=64)
+            for lo in range(0, S, BANK):
+                nc.vector.tensor_copy(codes[:, lo : lo + BANK], tab_sb[a][:].indirect(part(picked, lo, lo + BANK)))
+            v_codes.append(codes)
+
+        def features(i):
+            b, t = divmod(i, PACK)
+            h = ring2.tile([P, S], F32, name="h", tag="h")
+            sq = ring2.tile([P, S], F32, name="sq", tag="sq")
+            u = ring2.tile([P, S], F32, name="u", tag="u")
+            for lo in range(0, S, BANK):
+                cols = slice(lo, lo + BANK)
+                acc = psum.tile([P, BANK], F32, name="acc", tag="p")
+                for a in range(K_PASSES):
+                    nc.tensor.matmul_mx(
+                        out=acc[:],
+                        lhsT=w4_sb[:, a, 2 * P * i : 2 * P * (i + 1)].bitcast(FP4X4),
+                        lhsT_scale=w4_scale_sb[:, a, P * i : P * (i + 1)],
+                        rhs=v_codes[a][:, cols].bitcast(FP8X4),
+                        rhs_scale=v_scale[:, a, cols],
+                        start=(a == 0),
+                        stop=(a == K_PASSES - 1),
+                    )
+                nc.scalar.activation(sq[:, cols], acc[:], ACT.Square)
+                nc.scalar.activation(u[:, cols], sq[:, cols], ACT.Identity, bias=1.0, scale=cub_sb[:, b, t : t + 1])
+                nc.vector.tensor_tensor(h[:, cols], acc[:], u[:, cols], MULT)
+            return h
+
+        def interleave(dst, src):
+            nc.scalar.copy(
+                dst.rearrange("p (c i) t -> p c t i", i=4),
+                src.rearrange("p t (c i) -> p c t i", i=4),
+            )
+
+        w2_codes = keep.tile([P, H_PASSES, N], U32, align_bytes=64)
+        w2_scale = keep.tile([P, H_PASSES, N], U8, align_bytes=64)
+
+        def quantize_w2(b):
+            raw = ring3.tile([P, PACK, N], F32, name="raw", tag="wide")
+            nc.sync.dma_start(raw[:], w2[P * PACK * b : P * PACK * (b + 1), :].rearrange("(p t) n -> p t n", t=PACK))
+            grouped = ring3.tile([P, N, PACK], BF16, name="grouped", tag="grouped", align_bytes=64)
+            interleave(grouped[:], raw[:])
+            nc.vector.quantize_mx(
+                out=w2_codes[:, b, :].bitcast(FP8X4),
+                scales=w2_scale[:, b, :],
+                in_=grouped[:].rearrange("p n t -> p (n t)"),
+            )
+
+        z_codes = keep.tile([P, H_PASSES, T2], U32, align_bytes=64)
+        z_scale = keep.tile([P, H_PASSES, T2], U8, align_bytes=64)
+        wgo_sb = keep.tile([P, PICKS], F32)
+
+        tiles = H_PASSES * PACK
+        h_next = features(0)
+        planes = pairs = None
+        for i in range(tiles):
+            b, t = divmod(i, PACK)
+            h = h_next
+            page = pages[i % 2]
+            if i == 0:
+                for lo in range(0, S, BANK):
+                    nc.vector.tensor_tensor(
+                        page[:].indirect(part(shelved, lo, lo + BANK)),
+                        h[:, lo : lo + BANK],
+                        wgs_of(t)[:, lo : lo + BANK],
+                        MULT,
+                    )
+            else:
+                nc.vector.tensor_tensor(page[:].indirect(shelved[:]), h[:], wgs_of(t), MULT)
+            if i + 1 < tiles:
+                h_next = features(i + 1)
+                shelf_sb[i + 1] = load_shelf(i + 1)
+            chunks = range(0, T2, BANK)
+            if t == 0:
+                pairs = [ring4.tile([P, 2, BANK, 2], BF16, name="pairs", tag="pairs") for lo in chunks]
+            if t % 2 == 0:
+                planes = ring2.tile([P, 2, T2], BF16, name="planes", tag="planes")
+            if i < tiles - 1:
+                nc.vector.tensor_tensor(planes[:, t % 2, :], page[:], shelf_sb[i][:], MULT)
+            if i == tiles - 2:
+                for c, lo in enumerate(chunks):
+                    nc.scalar.copy(
+                        pairs[c][:, 1, :, :], planes[:, 0, lo : lo + BANK].unsqueeze(2).to_broadcast([P, BANK, 2])
+                    )
+            elif i == tiles - 1:
+                for c, lo in enumerate(chunks):
+                    nc.vector.tensor_tensor(
+                        pairs[c][:, 1, :, 1], page[:, lo : lo + BANK], shelf_sb[i][:, lo : lo + BANK], MULT
+                    )
+            elif t % 2 == 1:
+                for c, lo in enumerate(chunks):
+                    nc.scalar.copy(
+                        pairs[c][:, t // 2, :, :].rearrange("p (c i) e -> p c e i", i=4),
+                        planes[:, :, lo : lo + BANK].rearrange("p e (c i) -> p c e i", i=4),
+                    )
+            if i in (1, 2):
+                quantize_w2(i - 1)
+            if i == 3:
+                nc.sync.dma_start(wgo_sb[:], wgo)
+            if t == PACK - 1:
+                for c, lo in enumerate(chunks):
+                    grouped = ring3.tile([P, BANK * PACK], BF16, name="grouped", tag="grouped", align_bytes=64)
+                    nc.scalar.copy(
+                        grouped[:].bitcast(F32).rearrange("p (c h) -> p c h", h=2),
+                        pairs[c][:].rearrange("p h c e -> p h (c e)").bitcast(F32).rearrange("p h c -> p c h"),
+                    )
+                    nc.vector.quantize_mx(
+                        out=z_codes[:, b, lo : lo + BANK].bitcast(FP8X4),
+                        scales=z_scale[:, b, lo : lo + BANK],
+                        in_=grouped[:],
+                    )
+
+        def scores(n):
+            y = ring3.tile([P, T2], F32, name="y", tag="wide")
+            for lo in range(0, T2, BANK):
+                cols = slice(lo, lo + BANK)
+                acc = psum.tile([P, BANK], F32, name="acc", tag="y")
+                for b in range(H_PASSES):
+                    nc.tensor.matmul_mx(
+                        out=acc[:],
+                        lhsT=w2_codes[:, b, P * n : P * (n + 1)].bitcast(FP8X4),
+                        lhsT_scale=w2_scale[:, b, P * n : P * (n + 1)],
+                        rhs=z_codes[:, b, cols].bitcast(FP8X4),
+                        rhs_scale=z_scale[:, b, cols],
+                        start=(b == 0),
+                        stop=(b == H_PASSES - 1),
+                    )
+                nc.scalar.copy(y[:, cols], acc[:])
+            logits = ring2.tile([P, PICKS], F32, name="logits", tag="sq")
+            x = ring2.tile([P, PICKS], F32, name="x", tag="u")
+            step = BANK if n == 0 else PICKS
+            for lo in range(0, PICKS, step):
+                cols = slice(lo, lo + step)
+                nc.vector.tensor_copy(logits[:, cols], y[:].indirect(part(promoted, lo, lo + step)))
+                nc.scalar.activation(x[:, cols], logits[:, cols], ACT.Sigmoid, bias=base_sb[:, n : n + 1])
+            return x
+
+        x_next = scores(0)
+        for n in range(N_TILES):
+            x = x_next
+            if n + 1 < N_TILES:
+                x_next = scores(n + 1)
+            banner = banners[n % 2]
+            nc.vector.tensor_tensor(banner[:].indirect(slots[:]), x[:], wgo_sb[:], MULT)
+            nc.sync.dma_start(out[P * n : P * (n + 1), :], banner[:])

@@ -34,7 +34,7 @@ def tile_list_audiobook_banner_scores_kernel(
         ring2 = ctx.enter_context(tc.tile_pool(name="ring2", bufs=2))
         ring3 = ctx.enter_context(tc.tile_pool(name="ring3", bufs=3))
         ring4 = ctx.enter_context(tc.tile_pool(name="ring4", bufs=4))
-        psum = ctx.enter_context(tc.psum_pool(name="psum", bufs=4))
+        psum = ctx.enter_context(tc.psum_pool(name="psum", bufs=8))
 
         lists = []
         for name, src in (("offs", offs), ("offs2", offs2), ("offs3", offs3), ("offs4", offs4)):
@@ -75,10 +75,10 @@ def tile_list_audiobook_banner_scores_kernel(
             tab_sb.append(words)
 
         wgs_rows = wgs.rearrange("(p t) j -> p t j", t=PACK)
-        wgs_first = keep.tile([P, 1, S], F32)
-        wgs_rest = keep.tile([P, PACK - 1, S], F32)
+        wgs_first = keep.tile([P, 2, S], F32)
+        wgs_rest = keep.tile([P, 2, S], F32)
         for q in range(4):
-            nc.sync.dma_start(wgs_first[32 * q : 32 * q + 32, :, :], wgs_rows[:, 0:1, :])
+            nc.sync.dma_start(wgs_first[32 * q : 32 * q + 32, :, :], wgs_rows[:, 0:2, :])
         shelf_rows = shelf.rearrange("(b p t) c -> b t p c", b=H_PASSES, t=PACK)
 
         def load_shelf(i):
@@ -88,10 +88,10 @@ def tile_list_audiobook_banner_scores_kernel(
 
         shelf_sb = {0: load_shelf(0)}
         for q in range(4):
-            nc.sync.dma_start(wgs_rest[32 * q : 32 * q + 32, :, :], wgs_rows[:, 1:PACK, :])
+            nc.sync.dma_start(wgs_rest[32 * q : 32 * q + 32, :, :], wgs_rows[:, 2:PACK, :])
 
         def wgs_of(t):
-            return wgs_first[:, 0, :] if t == 0 else wgs_rest[:, t - 1, :]
+            return wgs_first[:, t, :] if t < 2 else wgs_rest[:, t - 2, :]
 
         pages = []
         for i in range(2):
@@ -125,14 +125,13 @@ def tile_list_audiobook_banner_scores_kernel(
                 nc.vector.tensor_copy(codes[:, lo : lo + BANK], tab_sb[a][:].indirect(part(picked, lo, lo + BANK)))
             v_codes.append(codes)
 
-        def features(i):
+        def product(i):
             b, t = divmod(i, PACK)
-            h = ring2.tile([P, S], F32, name="h", tag="h")
-            sq = ring2.tile([P, S], F32, name="sq", tag="sq")
-            u = ring2.tile([P, S], F32, name="u", tag="u")
+            u = ring3.tile([P, S], F32, name="u", tag="u")
+            banks = []
             for lo in range(0, S, BANK):
                 cols = slice(lo, lo + BANK)
-                acc = psum.tile([P, BANK], F32, name="acc", tag="p")
+                acc = psum.tile([P, BANK], F32, name="acc", tag="bank")
                 for a in range(K_PASSES):
                     nc.tensor.matmul_mx(
                         out=acc[:],
@@ -143,9 +142,17 @@ def tile_list_audiobook_banner_scores_kernel(
                         start=(a == 0),
                         stop=(a == K_PASSES - 1),
                     )
-                nc.scalar.activation(sq[:, cols], acc[:], ACT.Square)
-                nc.scalar.activation(u[:, cols], sq[:, cols], ACT.Identity, bias=1.0, scale=cub_sb[:, b, t : t + 1])
-                nc.vector.tensor_tensor(h[:, cols], acc[:], u[:, cols], MULT)
+                nc.scalar.activation(u[:, cols], acc[:], ACT.Square)
+                nc.scalar.activation(u[:, cols], u[:, cols], ACT.Identity, bias=1.0, scale=cub_sb[:, b, t : t + 1])
+                banks.append(acc)
+            return banks, u
+
+        def features(i, banks, u):
+            h = ring3.tile([P, S], F32, name="h", tag="h")
+            for acc, lo in zip(banks, range(0, S, BANK)):
+                nc.vector.tensor_tensor(h[:, lo : lo + BANK], acc[:], u[:, lo : lo + BANK], MULT)
+            if i > 0:
+                nc.gpsimd.tensor_tensor(h[:], h[:], wgs_of(i % PACK), MULT)
             return h
 
         def interleave(dst, src):
@@ -173,12 +180,17 @@ def tile_list_audiobook_banner_scores_kernel(
         wgo_sb = keep.tile([P, PICKS], F32)
 
         tiles = H_PASSES * PACK
-        h_next = features(0)
+        products = {i: product(i) for i in range(2)}
+        h_next = features(0, *products[0])
         planes = pairs = None
         for i in range(tiles):
             b, t = divmod(i, PACK)
             h = h_next
             page = pages[i % 2]
+            if i + 2 < tiles:
+                products[i + 2] = product(i + 2)
+            if i + 1 < tiles:
+                h_next = features(i + 1, *products[i + 1])
             if i == 0:
                 for lo in range(0, S, BANK):
                     nc.vector.tensor_tensor(
@@ -188,22 +200,21 @@ def tile_list_audiobook_banner_scores_kernel(
                         MULT,
                     )
             else:
-                nc.vector.tensor_tensor(page[:].indirect(shelved[:]), h[:], wgs_of(t), MULT)
+                nc.vector.tensor_copy(page[:].indirect(shelved[:]), h[:])
             if i + 1 < tiles:
-                h_next = features(i + 1)
                 shelf_sb[i + 1] = load_shelf(i + 1)
             chunks = range(0, T2, BANK)
             if t == 0:
                 pairs = [ring4.tile([P, 2, BANK, 2], BF16, name="pairs", tag="pairs") for lo in chunks]
-            if t % 2 == 0:
+            if t % 2 == 0 and i < tiles - 2:
                 planes = ring2.tile([P, 2, T2], BF16, name="planes", tag="planes")
-            if i < tiles - 1:
-                nc.vector.tensor_tensor(planes[:, t % 2, :], page[:], shelf_sb[i][:], MULT)
+            if i < tiles - 2:
+                nc.gpsimd.tensor_tensor(planes[:, t % 2, :], page[:], shelf_sb[i][:], MULT)
             if i == tiles - 2:
                 for c, lo in enumerate(chunks):
-                    nc.scalar.copy(
-                        pairs[c][:, 1, :, :], planes[:, 0, lo : lo + BANK].unsqueeze(2).to_broadcast([P, BANK, 2])
-                    )
+                    single = ring2.tile([P, BANK], BF16, name="single", tag="planes")
+                    nc.gpsimd.tensor_tensor(single[:], page[:, lo : lo + BANK], shelf_sb[i][:, lo : lo + BANK], MULT)
+                    nc.scalar.copy(pairs[c][:, 1, :, :], single[:].unsqueeze(2).to_broadcast([P, BANK, 2]))
             elif i == tiles - 1:
                 for c, lo in enumerate(chunks):
                     nc.vector.tensor_tensor(
@@ -236,7 +247,7 @@ def tile_list_audiobook_banner_scores_kernel(
             y = ring3.tile([P, T2], F32, name="y", tag="wide")
             for lo in range(0, T2, BANK):
                 cols = slice(lo, lo + BANK)
-                acc = psum.tile([P, BANK], F32, name="acc", tag="y")
+                acc = psum.tile([P, BANK], F32, name="acc", tag="bank")
                 for b in range(H_PASSES):
                     nc.tensor.matmul_mx(
                         out=acc[:],
@@ -248,8 +259,8 @@ def tile_list_audiobook_banner_scores_kernel(
                         stop=(b == H_PASSES - 1),
                     )
                 nc.scalar.copy(y[:, cols], acc[:])
-            logits = ring2.tile([P, PICKS], F32, name="logits", tag="sq")
-            x = ring2.tile([P, PICKS], F32, name="x", tag="u")
+            logits = ring3.tile([P, PICKS], F32, name="logits", tag="h")
+            x = ring3.tile([P, PICKS], F32, name="x", tag="u")
             step = BANK if n == 0 else PICKS
             for lo in range(0, PICKS, step):
                 cols = slice(lo, lo + step)

@@ -31,103 +31,107 @@ def tile_list_audiobook_banner_scores_kernel(
     nc = tc.nc
     with ExitStack() as ctx:
         keep = ctx.enter_context(tc.tile_pool(name="keep", bufs=1))
-        ring2 = ctx.enter_context(tc.tile_pool(name="ring2", bufs=2))
-        ring3 = ctx.enter_context(tc.tile_pool(name="ring3", bufs=3))
         ring4 = ctx.enter_context(tc.tile_pool(name="ring4", bufs=4))
         psum = ctx.enter_context(tc.psum_pool(name="psum", bufs=8))
 
-        lists = []
-        for name, src in (("offs", offs), ("offs2", offs2), ("offs3", offs3), ("offs4", offs4)):
-            tile = keep.tile([P, S // PER_COLUMN], U16, name=name + "_sb")
-            nc.sync.dma_start(tile[:], src)
-            lists.append(tile)
-        picked, shelved, promoted, slots = lists
+        with tc.tile_pool(name="head", bufs=1) as head:
+            lists = []
+            for name, src in (("offs", offs), ("offs2", offs2), ("offs3", offs3), ("offs4", offs4)):
+                tile = keep.tile([P, S // PER_COLUMN], U16, name=name + "_sb")
+                nc.sync.dma_start(tile[:], src)
+                lists.append(tile)
+            picked, shelved, promoted, slots = lists
 
-        def part(tile, lo, hi):
-            return tile[:, lo // PER_COLUMN : hi // PER_COLUMN]
+            def part(tile, lo, hi):
+                return tile[:, lo // PER_COLUMN : hi // PER_COLUMN]
 
-        cub_sb = keep.tile([P, H_PASSES, PACK], F32)
-        nc.sync.dma_start(cub_sb[:], cub.rearrange("(b p t) -> p b t", b=H_PASSES, t=PACK))
-        base_sb = keep.tile([P, N_TILES], F32)
-        with nc.allow_non_contiguous_dma(reason="one bias value a partition"):
-            nc.sync.dma_start(base_sb[:], base.rearrange("(c p) -> p c", p=P))
+            cub_sb = keep.tile([P, H_PASSES, PACK], F32)
+            nc.sync.dma_start(cub_sb[:], cub.rearrange("(b p t) -> p b t", b=H_PASSES, t=PACK))
+            base_sb = keep.tile([P, N_TILES], F32)
+            with nc.allow_non_contiguous_dma(reason="one bias value a partition"):
+                nc.sync.dma_start(base_sb[:], base.rearrange("(c p) -> p c", p=P))
 
-        tab_scale_sb = keep.tile([P, K_PASSES, T], U8, align_bytes=64)
-        nc.gpsimd.memset(tab_scale_sb[:].bitcast(I32), 0)
-        w4_scale_raw = keep.tile([P, K_PASSES, H], U8, align_bytes=64)
-        nc.gpsimd.memset(w4_scale_raw[:].bitcast(I32), 0)
-        for q in range(4):
-            nc.scalar.dma_start(
-                w4_scale_raw[32 * q : 32 * q + 4, :, :].bitcast(I32),
-                w4_scales[:, 4 * q : 4 * q + 4, :].rearrange("a r n -> r a n").bitcast(I32),
+            tab_scale_sb = head.tile([P, K_PASSES, T], U8, align_bytes=64)
+            nc.gpsimd.memset(tab_scale_sb[:].bitcast(I32), 0)
+            w4_scale_raw = head.tile([P, K_PASSES, H], U8, align_bytes=64)
+            nc.gpsimd.memset(w4_scale_raw[:].bitcast(I32), 0)
+            for q in range(4):
+                nc.scalar.dma_start(
+                    w4_scale_raw[32 * q : 32 * q + 4, :, :].bitcast(I32),
+                    w4_scales[:, 4 * q : 4 * q + 4, :].rearrange("a r n -> r a n").bitcast(I32),
+                )
+            w4_raw = head.tile([P, K_PASSES, 2 * H], U8, align_bytes=64)
+            nc.sync.dma_start(w4_raw[:].bitcast(I32), w4_words.rearrange("a p n -> p a n").bitcast(I32))
+            for q in range(4):
+                nc.sync.dma_start(
+                    tab_scale_sb[32 * q : 32 * q + 4, :, :].bitcast(I32),
+                    tab_scales[:, 4 * q : 4 * q + 4, :].rearrange("a r n -> r a n").bitcast(I32),
+                )
+            tab_sb = []
+            for a in range(K_PASSES):
+                words = head.tile([P, T], U32, name="tab_sb%d" % a, align_bytes=64)
+                nc.sync.dma_start(words[:].bitcast(I32), tab_words[a].rearrange("p n t -> p (n t)").bitcast(I32))
+                tab_sb.append(words)
+
+            wgs_rows = wgs.rearrange("(p t) j -> p t j", t=PACK)
+            wgs_first = keep.tile([P, 2, S], F32)
+            wgs_rest = keep.tile([P, 2, S], F32, tag="shared", align_bytes=64)
+            for q in range(4):
+                nc.sync.dma_start(wgs_first[32 * q : 32 * q + 32, :, :], wgs_rows[:, 0:2, :])
+            shelf_rows = shelf.rearrange("(b p t) c -> b t p c", b=H_PASSES, t=PACK)
+
+            def load_shelf(i):
+                rows = ring4.tile([P, T2], F32, name="rows", tag="wide")
+                nc.sync.dma_start(rows[:], shelf_rows[i // PACK, i % PACK])
+                return rows
+
+            for q in range(4):
+                nc.sync.dma_start(wgs_rest[32 * q : 32 * q + 32, :, :], wgs_rows[:, 2:PACK, :])
+
+            wgo_sb = keep.tile([P, PICKS], F32)
+            nc.sync.dma_start(wgo_sb[:], wgo)
+            shelf_sb = {0: load_shelf(0)}
+
+            def wgs_of(t):
+                return wgs_first[:, t, :] if t < 2 else wgs_rest[:, t - 2, :]
+
+            pages = []
+            for i in range(2):
+                page = keep.tile([P, T2], F32, name="page%d" % i)
+                nc.gpsimd.memset(page[:], 0.0)
+                pages.append(page)
+            banners = []
+            for i in range(2):
+                banner = keep.tile([P, T2], F32, name="banner%d" % i)
+                nc.gpsimd.memset(banner[:], 0.0)
+                banners.append(banner)
+
+            w4_sb = keep.tile([P, K_PASSES, 2 * H], U8, align_bytes=64)
+            nc.vector.tensor_copy(
+                w4_sb[:].bitcast(U16).rearrange("p a (b t m) -> p (a b) t m", b=H_PASSES, t=PACK),
+                w4_raw[:].bitcast(U16).rearrange("p a (b m t) -> p (a b) t m", b=H_PASSES, t=PACK),
             )
-        w4_raw = keep.tile([P, K_PASSES, 2 * H], U8, align_bytes=64)
-        nc.sync.dma_start(w4_raw[:].bitcast(I32), w4_words.rearrange("a p n -> p a n").bitcast(I32))
-        for q in range(4):
-            nc.sync.dma_start(
-                tab_scale_sb[32 * q : 32 * q + 4, :, :].bitcast(I32),
-                tab_scales[:, 4 * q : 4 * q + 4, :].rearrange("a r n -> r a n").bitcast(I32),
+            w4_scale_sb = keep.tile([P, K_PASSES, H], U8, align_bytes=64)
+            nc.vector.tensor_copy(
+                w4_scale_sb[:].rearrange("p a (b t m) -> p (a b) t m", b=H_PASSES, t=PACK),
+                w4_scale_raw[:].rearrange("p a (b m t) -> p (a b) t m", b=H_PASSES, t=PACK),
             )
-        tab_sb = []
-        for a in range(K_PASSES):
-            words = keep.tile([P, T], U32, name="tab_sb%d" % a, align_bytes=64)
-            nc.sync.dma_start(words[:].bitcast(I32), tab_words[a].rearrange("p n t -> p (n t)").bitcast(I32))
-            tab_sb.append(words)
 
-        wgs_rows = wgs.rearrange("(p t) j -> p t j", t=PACK)
-        wgs_first = keep.tile([P, 2, S], F32)
-        wgs_rest = keep.tile([P, 2, S], F32)
-        for q in range(4):
-            nc.sync.dma_start(wgs_first[32 * q : 32 * q + 32, :, :], wgs_rows[:, 0:2, :])
-        shelf_rows = shelf.rearrange("(b p t) c -> b t p c", b=H_PASSES, t=PACK)
+            v_scale = keep.tile([P, K_PASSES, S], U8, align_bytes=64)
+            for a in range(K_PASSES):
+                nc.vector.tensor_copy(v_scale[:, a, :], tab_scale_sb[:, a, :].indirect(picked[:]))
+            v_codes = []
+            for a in range(K_PASSES):
+                codes = keep.tile([P, S], U32, name="v_codes%d" % a, align_bytes=64)
+                for lo in range(0, S, BANK):
+                    nc.vector.tensor_copy(codes[:, lo : lo + BANK], tab_sb[a][:].indirect(part(picked, lo, lo + BANK)))
+                v_codes.append(codes)
 
-        def load_shelf(i):
-            rows = ring3.tile([P, T2], F32, name="rows", tag="wide")
-            nc.sync.dma_start(rows[:], shelf_rows[i // PACK, i % PACK])
-            return rows
-
-        shelf_sb = {0: load_shelf(0)}
-        for q in range(4):
-            nc.sync.dma_start(wgs_rest[32 * q : 32 * q + 32, :, :], wgs_rows[:, 2:PACK, :])
-
-        def wgs_of(t):
-            return wgs_first[:, t, :] if t < 2 else wgs_rest[:, t - 2, :]
-
-        pages = []
-        for i in range(2):
-            page = keep.tile([P, T2], F32, name="page%d" % i)
-            nc.gpsimd.memset(page[:], 0.0)
-            pages.append(page)
-        banners = []
-        for i in range(2):
-            banner = keep.tile([P, T2], F32, name="banner%d" % i)
-            nc.gpsimd.memset(banner[:], 0.0)
-            banners.append(banner)
-
-        w4_sb = keep.tile([P, K_PASSES, 2 * H], U8, align_bytes=64)
-        nc.vector.tensor_copy(
-            w4_sb[:].bitcast(U16).rearrange("p a (b t m) -> p (a b) t m", b=H_PASSES, t=PACK),
-            w4_raw[:].bitcast(U16).rearrange("p a (b m t) -> p (a b) t m", b=H_PASSES, t=PACK),
-        )
-        w4_scale_sb = keep.tile([P, K_PASSES, H], U8, align_bytes=64)
-        nc.vector.tensor_copy(
-            w4_scale_sb[:].rearrange("p a (b t m) -> p (a b) t m", b=H_PASSES, t=PACK),
-            w4_scale_raw[:].rearrange("p a (b m t) -> p (a b) t m", b=H_PASSES, t=PACK),
-        )
-
-        v_scale = keep.tile([P, K_PASSES, S], U8, align_bytes=64)
-        for a in range(K_PASSES):
-            nc.vector.tensor_copy(v_scale[:, a, :], tab_scale_sb[:, a, :].indirect(picked[:]))
-        v_codes = []
-        for a in range(K_PASSES):
-            codes = keep.tile([P, S], U32, name="v_codes%d" % a, align_bytes=64)
-            for lo in range(0, S, BANK):
-                nc.vector.tensor_copy(codes[:, lo : lo + BANK], tab_sb[a][:].indirect(part(picked, lo, lo + BANK)))
-            v_codes.append(codes)
+        late = ctx.enter_context(tc.tile_pool(name="late", bufs=1))
 
         def product(i):
             b, t = divmod(i, PACK)
-            u = ring3.tile([P, S], F32, name="u", tag="u")
+            u = ring4.tile([P, S], F32, name="u", tag="u")
             banks = []
             for lo in range(0, S, BANK):
                 cols = slice(lo, lo + BANK)
@@ -147,13 +151,22 @@ def tile_list_audiobook_banner_scores_kernel(
                 banks.append(acc)
             return banks, u
 
+        planes_first = late.tile([P, PACK * T2], BF16)
+        planes_second = late.tile([P, 2 * T2], BF16)
+        plane_third = late.tile([P, T2], BF16)
+        plane_of = [planes_first[:, T2 * t : T2 * (t + 1)] for t in range(PACK)]
+        plane_of.extend(planes_second[:, T2 * t : T2 * (t + 1)] for t in range(2))
+        plane_of.append(plane_third[:])
+        h_first = late.tile([P, S], F32)
+
         def features(i, banks, u):
-            h = ring3.tile([P, S], F32, name="h", tag="h")
+            h = h_first[:] if i == 0 else plane_of[i - 1].bitcast(F32)
+            hw = late.tile([P, S], F32, name="hw", tag="h", bufs=2)
             for acc, lo in zip(banks, range(0, S, BANK)):
-                nc.vector.tensor_tensor(h[:, lo : lo + BANK], acc[:], u[:, lo : lo + BANK], MULT)
-            if i > 0:
-                nc.gpsimd.tensor_tensor(h[:], h[:], wgs_of(i % PACK), MULT)
-            return h
+                cols = slice(lo, lo + BANK)
+                nc.vector.tensor_tensor(h[:, cols], acc[:], u[:, cols], MULT)
+                nc.gpsimd.tensor_tensor(hw[:, cols], h[:, cols], wgs_of(i % PACK)[:, cols], MULT)
+            return hw
 
         def interleave(dst, src):
             nc.scalar.copy(
@@ -161,106 +174,104 @@ def tile_list_audiobook_banner_scores_kernel(
                 src.rearrange("p t (c i) -> p c t i", i=4),
             )
 
-        w2_codes = keep.tile([P, H_PASSES, N], U32, align_bytes=64)
-        w2_scale = keep.tile([P, H_PASSES, N], U8, align_bytes=64)
-
-        def quantize_w2(b):
-            raw = ring3.tile([P, PACK, N], F32, name="raw", tag="wide")
+        def group_w2(b):
+            raw = ring4.tile([P, PACK, N], F32, name="raw", tag="wide")
             nc.sync.dma_start(raw[:], w2[P * PACK * b : P * PACK * (b + 1), :].rearrange("(p t) n -> p t n", t=PACK))
-            grouped = ring3.tile([P, N, PACK], BF16, name="grouped", tag="grouped", align_bytes=64)
-            interleave(grouped[:], raw[:])
-            nc.vector.quantize_mx(
-                out=w2_codes[:, b, :].bitcast(FP8X4),
-                scales=w2_scale[:, b, :],
-                in_=grouped[:].rearrange("p n t -> p (n t)"),
-            )
+            grouped = late.tile([P, N * PACK], BF16, name="grouped", tag="grouped", bufs=8, align_bytes=64)
+            interleave(grouped[:].rearrange("p (n t) -> p n t", t=PACK), raw[:])
+            return grouped
 
-        z_codes = keep.tile([P, H_PASSES, T2], U32, align_bytes=64)
-        z_scale = keep.tile([P, H_PASSES, T2], U8, align_bytes=64)
-        wgo_sb = keep.tile([P, PICKS], F32)
+        def group_z(pair):
+            grouped = late.tile([P, BANK * PACK], BF16, name="grouped", tag="grouped", bufs=8, align_bytes=64)
+            nc.scalar.copy(
+                grouped[:].bitcast(F32).rearrange("p (c h) -> p c h", h=2),
+                pair[:].rearrange("p h c e -> p h (c e)").bitcast(F32).rearrange("p h c -> p c h"),
+            )
+            return grouped
 
         tiles = H_PASSES * PACK
-        products = {i: product(i) for i in range(2)}
+        chunks = range(0, T2, BANK)
+        products = [product(i) for i in range(tiles)]
         h_next = features(0, *products[0])
         planes = pairs = None
+        w2_grouped = []
+        z_grouped = []
         for i in range(tiles):
             b, t = divmod(i, PACK)
-            h = h_next
             page = pages[i % 2]
-            if i + 2 < tiles:
-                products[i + 2] = product(i + 2)
+            h = h_next
             if i + 1 < tiles:
                 h_next = features(i + 1, *products[i + 1])
-            if i == 0:
-                for lo in range(0, S, BANK):
-                    nc.vector.tensor_tensor(
-                        page[:].indirect(part(shelved, lo, lo + BANK)),
-                        h[:, lo : lo + BANK],
-                        wgs_of(t)[:, lo : lo + BANK],
-                        MULT,
-                    )
-            else:
-                nc.vector.tensor_copy(page[:].indirect(shelved[:]), h[:])
+            for lo in range(0, S, BANK):
+                nc.vector.tensor_copy(page[:].indirect(part(shelved, lo, lo + BANK)), h[:, lo : lo + BANK])
             if i + 1 < tiles:
                 shelf_sb[i + 1] = load_shelf(i + 1)
-            chunks = range(0, T2, BANK)
-            if t == 0:
-                pairs = [ring4.tile([P, 2, BANK, 2], BF16, name="pairs", tag="pairs") for lo in chunks]
-            if t % 2 == 0 and i < tiles - 2:
-                planes = ring2.tile([P, 2, T2], BF16, name="planes", tag="planes")
+            if i in (3, 4):
+                w2_grouped.append(group_w2(i - 3))
+            if i == 0:
+                planes = planes_first[:].rearrange("p (t c) -> p t c", t=PACK)
+            if i == PACK:
+                planes = planes_second[:].rearrange("p (t c) -> p t c", t=2)
+                pairs = [late.tile([P, 2, BANK, 2], BF16, name="pairs", tag="pairs", bufs=4) for lo in chunks]
             if i < tiles - 2:
-                nc.gpsimd.tensor_tensor(planes[:, t % 2, :], page[:], shelf_sb[i][:], MULT)
-            if i == tiles - 2:
+                nc.gpsimd.tensor_tensor(plane_of[i], page[:], shelf_sb[i][:], MULT)
+            if i == PACK - 1:
+                for lo in chunks:
+                    grouped = late.tile([P, BANK * PACK], BF16, name="grouped", tag="grouped", bufs=8, align_bytes=64)
+                    interleave(grouped[:].rearrange("p (n t) -> p n t", t=PACK), planes[:, :, lo : lo + BANK])
+                    z_grouped.append(grouped)
+            elif i == tiles - 3:
                 for c, lo in enumerate(chunks):
-                    single = ring2.tile([P, BANK], BF16, name="single", tag="planes")
-                    nc.gpsimd.tensor_tensor(single[:], page[:, lo : lo + BANK], shelf_sb[i][:, lo : lo + BANK], MULT)
-                    nc.scalar.copy(pairs[c][:, 1, :, :], single[:].unsqueeze(2).to_broadcast([P, BANK, 2]))
+                    nc.scalar.copy(
+                        pairs[c][:, 0, :, :].rearrange("p (c i) e -> p c e i", i=4),
+                        planes[:, :, lo : lo + BANK].rearrange("p e (c i) -> p c e i", i=4),
+                    )
+            elif i == tiles - 2:
+                for c, lo in enumerate(chunks):
+                    single = plane_of[i][:, T2 - BANK - lo : T2 - lo]
+                    nc.gpsimd.tensor_tensor(single, page[:, lo : lo + BANK], shelf_sb[i][:, lo : lo + BANK], MULT)
+                    nc.scalar.copy(pairs[c][:, 1, :, :], single.unsqueeze(2).to_broadcast([P, BANK, 2]))
             elif i == tiles - 1:
                 for c, lo in enumerate(chunks):
                     nc.vector.tensor_tensor(
                         pairs[c][:, 1, :, 1], page[:, lo : lo + BANK], shelf_sb[i][:, lo : lo + BANK], MULT
                     )
-            elif t % 2 == 1:
-                for c, lo in enumerate(chunks):
-                    nc.scalar.copy(
-                        pairs[c][:, t // 2, :, :].rearrange("p (c i) e -> p c e i", i=4),
-                        planes[:, :, lo : lo + BANK].rearrange("p e (c i) -> p c e i", i=4),
-                    )
-            if i in (1, 2):
-                quantize_w2(i - 1)
-            if i == 3:
-                nc.sync.dma_start(wgo_sb[:], wgo)
-            if t == PACK - 1:
-                for c, lo in enumerate(chunks):
-                    grouped = ring3.tile([P, BANK * PACK], BF16, name="grouped", tag="grouped", align_bytes=64)
-                    nc.scalar.copy(
-                        grouped[:].bitcast(F32).rearrange("p (c h) -> p c h", h=2),
-                        pairs[c][:].rearrange("p h c e -> p h (c e)").bitcast(F32).rearrange("p h c -> p c h"),
-                    )
-                    nc.vector.quantize_mx(
-                        out=z_codes[:, b, lo : lo + BANK].bitcast(FP8X4),
-                        scales=z_scale[:, b, lo : lo + BANK],
-                        in_=grouped[:],
-                    )
+
+        early = keep.tile([P, T2 + H_PASSES * N], U32, tag="shared", align_bytes=64)
+        z_last = late.tile([P, T2], U32, align_bytes=64)
+        z_codes = [early[:, :T2], z_last[:]]
+        w2_codes = [early[:, T2 + N * b : T2 + N * (b + 1)] for b in range(H_PASSES)]
+        z_scale = keep.tile([P, H_PASSES, T2], U8, align_bytes=64)
+        w2_scale = keep.tile([P, H_PASSES, N], U8, align_bytes=64)
+        for b in range(H_PASSES):
+            nc.vector.quantize_mx(out=w2_codes[b].bitcast(FP8X4), scales=w2_scale[:, b, :], in_=w2_grouped[b][:])
+        for b in range(H_PASSES):
+            for c, lo in enumerate(chunks):
+                grouped = z_grouped[c] if b == 0 else group_z(pairs[c])
+                nc.vector.quantize_mx(
+                    out=z_codes[b][:, lo : lo + BANK].bitcast(FP8X4),
+                    scales=z_scale[:, b, lo : lo + BANK],
+                    in_=grouped[:],
+                )
 
         def scores(n):
-            y = ring3.tile([P, T2], F32, name="y", tag="wide")
+            y = ring4.tile([P, T2], F32, name="y", tag="wide")
             for lo in range(0, T2, BANK):
                 cols = slice(lo, lo + BANK)
                 acc = psum.tile([P, BANK], F32, name="acc", tag="bank")
                 for b in range(H_PASSES):
                     nc.tensor.matmul_mx(
                         out=acc[:],
-                        lhsT=w2_codes[:, b, P * n : P * (n + 1)].bitcast(FP8X4),
+                        lhsT=w2_codes[b][:, P * n : P * (n + 1)].bitcast(FP8X4),
                         lhsT_scale=w2_scale[:, b, P * n : P * (n + 1)],
-                        rhs=z_codes[:, b, cols].bitcast(FP8X4),
+                        rhs=z_codes[b][:, cols].bitcast(FP8X4),
                         rhs_scale=z_scale[:, b, cols],
                         start=(b == 0),
                         stop=(b == H_PASSES - 1),
                     )
                 nc.scalar.copy(y[:, cols], acc[:])
-            logits = ring3.tile([P, PICKS], F32, name="logits", tag="h")
-            x = ring3.tile([P, PICKS], F32, name="x", tag="u")
+            logits = late.tile([P, PICKS], F32, name="logits", tag="h", bufs=2)
+            x = ring4.tile([P, PICKS], F32, name="x", tag="u")
             step = BANK if n == 0 else PICKS
             for lo in range(0, PICKS, step):
                 cols = slice(lo, lo + step)

@@ -17,12 +17,20 @@ ACT = mybir.ActivationFunctionType
 MULT = mybir.AluOpType.mult
 
 P = 128
+QUADRANT = 32
+QUADRANTS = P // QUADRANT
+SCALE_ROWS = 4
 PACK = 4
 BANK = 512
+BANKS = 8
+PER_COLUMN = 16
 K_PASSES = K // (P * PACK)
 H_PASSES = H // (P * PACK)
+ROW_TILES = H_PASSES * PACK
+LAST = ROW_TILES - 1
 N_TILES = N // P
-PER_COLUMN = 16
+PAGES = 3
+RUN = 4
 
 
 def tile_list_audiobook_banner_scores_kernel(
@@ -31,72 +39,71 @@ def tile_list_audiobook_banner_scores_kernel(
     nc = tc.nc
     with ExitStack() as ctx:
         keep = ctx.enter_context(tc.tile_pool(name="keep", bufs=1))
-        ring4 = ctx.enter_context(tc.tile_pool(name="ring4", bufs=4))
-        psum = ctx.enter_context(tc.psum_pool(name="psum", bufs=8))
+        ring2 = ctx.enter_context(tc.tile_pool(name="ring2", bufs=2))
+        psum = ctx.enter_context(tc.psum_pool(name="psum", bufs=BANKS))
+
+        def part(list_tile, lo, hi):
+            return list_tile[:, lo // PER_COLUMN : hi // PER_COLUMN]
+
+        def load_scale_rows(queue, tile, scales):
+            for quadrant in range(QUADRANTS):
+                first, row = QUADRANT * quadrant, SCALE_ROWS * quadrant
+                queue.dma_start(
+                    tile[first : first + SCALE_ROWS, :, :].bitcast(I32),
+                    scales[:, row : row + SCALE_ROWS, :].rearrange("a r n -> r a n").bitcast(I32),
+                )
+
+        def load_wgs(tile, slots):
+            rows = wgs.rearrange("(q t) j -> q t j", t=PACK)
+            for quadrant in range(QUADRANTS):
+                nc.sync.dma_start(tile[QUADRANT * quadrant : QUADRANT * (quadrant + 1), :, :], rows[:, slots, :])
+
+        def load_shelf(i, cols):
+            rows = ring2.tile([P, cols.stop - cols.start], F32, name="rows", tag="shelf")
+            by_tile = shelf.rearrange("(b q t) c -> b t q c", b=H_PASSES, t=PACK)
+            nc.sync.dma_start(rows[:], by_tile[i // PACK, i % PACK][:, cols])
+            return rows
 
         with tc.tile_pool(name="head", bufs=1) as head:
             lists = []
             for name, src in (("offs", offs), ("offs2", offs2), ("offs3", offs3), ("offs4", offs4)):
-                tile = keep.tile([P, S // PER_COLUMN], U16, name=name + "_sb")
-                nc.sync.dma_start(tile[:], src)
-                lists.append(tile)
-            picked, shelved, promoted, slots = lists
+                list_tile = keep.tile([P, S // PER_COLUMN], U16, name=name + "_sb")
+                nc.sync.dma_start(list_tile[:], src)
+                lists.append(list_tile)
+            listed, shelved, promoted, banner_slots = lists
 
-            def part(tile, lo, hi):
-                return tile[:, lo // PER_COLUMN : hi // PER_COLUMN]
-
-            cub_sb = keep.tile([P, H_PASSES, PACK], F32)
-            nc.sync.dma_start(cub_sb[:], cub.rearrange("(b p t) -> p b t", b=H_PASSES, t=PACK))
+            cub_sb = keep.tile([P, H_PASSES, PACK], F32, tag="cub", align_bytes=64)
+            nc.sync.dma_start(cub_sb[:], cub.rearrange("(b q t) -> q b t", b=H_PASSES, t=PACK))
             base_sb = keep.tile([P, N_TILES], F32)
             with nc.allow_non_contiguous_dma(reason="one bias value a partition"):
-                nc.sync.dma_start(base_sb[:], base.rearrange("(c p) -> p c", p=P))
+                nc.sync.dma_start(base_sb[:], base.rearrange("(c q) -> q c", q=P))
 
             tab_scale_sb = head.tile([P, K_PASSES, T], U8, align_bytes=64)
             nc.gpsimd.memset(tab_scale_sb[:].bitcast(I32), 0)
             w4_scale_raw = head.tile([P, K_PASSES, H], U8, align_bytes=64)
             nc.gpsimd.memset(w4_scale_raw[:].bitcast(I32), 0)
-            for q in range(4):
-                nc.scalar.dma_start(
-                    w4_scale_raw[32 * q : 32 * q + 4, :, :].bitcast(I32),
-                    w4_scales[:, 4 * q : 4 * q + 4, :].rearrange("a r n -> r a n").bitcast(I32),
-                )
+            load_scale_rows(nc.scalar, w4_scale_raw, w4_scales)
             w4_raw = head.tile([P, K_PASSES, 2 * H], U8, align_bytes=64)
-            nc.sync.dma_start(w4_raw[:].bitcast(I32), w4_words.rearrange("a p n -> p a n").bitcast(I32))
-            for q in range(4):
-                nc.sync.dma_start(
-                    tab_scale_sb[32 * q : 32 * q + 4, :, :].bitcast(I32),
-                    tab_scales[:, 4 * q : 4 * q + 4, :].rearrange("a r n -> r a n").bitcast(I32),
-                )
+            nc.sync.dma_start(w4_raw[:].bitcast(I32), w4_words.rearrange("a q n -> q a n").bitcast(I32))
+            load_scale_rows(nc.sync, tab_scale_sb, tab_scales)
             tab_sb = []
             for a in range(K_PASSES):
                 words = head.tile([P, T], U32, name="tab_sb%d" % a, align_bytes=64)
-                nc.sync.dma_start(words[:].bitcast(I32), tab_words[a].rearrange("p n t -> p (n t)").bitcast(I32))
+                nc.sync.dma_start(words[:].bitcast(I32), tab_words[a].rearrange("q n t -> q (n t)").bitcast(I32))
                 tab_sb.append(words)
 
-            wgs_rows = wgs.rearrange("(p t) j -> p t j", t=PACK)
-            wgs_first = keep.tile([P, 2, S], F32)
-            wgs_rest = keep.tile([P, 2, S], F32, tag="shared", align_bytes=64)
-            for q in range(4):
-                nc.sync.dma_start(wgs_first[32 * q : 32 * q + 32, :, :], wgs_rows[:, 0:2, :])
-            shelf_rows = shelf.rearrange("(b p t) c -> b t p c", b=H_PASSES, t=PACK)
-
-            def load_shelf(i):
-                rows = ring4.tile([P, T2], F32, name="rows", tag="wide")
-                nc.sync.dma_start(rows[:], shelf_rows[i // PACK, i % PACK])
-                return rows
-
-            for q in range(4):
-                nc.sync.dma_start(wgs_rest[32 * q : 32 * q + 32, :, :], wgs_rows[:, 2:PACK, :])
-
+            wgs_low = keep.tile([P, 2, S], F32)
+            wgs_high = keep.tile([P, 2, S], F32)
+            load_wgs(wgs_low, slice(0, 2))
+            load_wgs(wgs_high, slice(2, PACK))
             wgo_sb = keep.tile([P, PICKS], F32)
             nc.sync.dma_start(wgo_sb[:], wgo)
-            shelf_sb = {0: load_shelf(0)}
-
-            def wgs_of(t):
-                return wgs_first[:, t, :] if t < 2 else wgs_rest[:, t - 2, :]
+            halves = (slice(0, T2 // 2), slice(T2 // 2, T2))
+            shelf_first = [load_shelf(0, half) for half in halves]
+            shelf_sb = {}
 
             pages = []
-            for i in range(2):
+            for i in range(PAGES):
                 page = keep.tile([P, T2], F32, name="page%d" % i)
                 nc.gpsimd.memset(page[:], 0.0)
                 pages.append(page)
@@ -108,182 +115,196 @@ def tile_list_audiobook_banner_scores_kernel(
 
             w4_sb = keep.tile([P, K_PASSES, 2 * H], U8, align_bytes=64)
             nc.vector.tensor_copy(
-                w4_sb[:].bitcast(U16).rearrange("p a (b t m) -> p (a b) t m", b=H_PASSES, t=PACK),
-                w4_raw[:].bitcast(U16).rearrange("p a (b m t) -> p (a b) t m", b=H_PASSES, t=PACK),
+                w4_sb[:].bitcast(U16).rearrange("q a (b t m) -> q (a b) t m", b=H_PASSES, t=PACK),
+                w4_raw[:].bitcast(U16).rearrange("q a (b m t) -> q (a b) t m", b=H_PASSES, t=PACK),
             )
             w4_scale_sb = keep.tile([P, K_PASSES, H], U8, align_bytes=64)
             nc.vector.tensor_copy(
-                w4_scale_sb[:].rearrange("p a (b t m) -> p (a b) t m", b=H_PASSES, t=PACK),
-                w4_scale_raw[:].rearrange("p a (b m t) -> p (a b) t m", b=H_PASSES, t=PACK),
+                w4_scale_sb[:].rearrange("q a (b t m) -> q (a b) t m", b=H_PASSES, t=PACK),
+                w4_scale_raw[:].rearrange("q a (b m t) -> q (a b) t m", b=H_PASSES, t=PACK),
             )
 
             v_scale = keep.tile([P, K_PASSES, S], U8, align_bytes=64)
             for a in range(K_PASSES):
-                nc.vector.tensor_copy(v_scale[:, a, :], tab_scale_sb[:, a, :].indirect(picked[:]))
+                nc.vector.tensor_copy(v_scale[:, a, :], tab_scale_sb[:, a, :].indirect(listed[:]))
             v_codes = []
             for a in range(K_PASSES):
                 codes = keep.tile([P, S], U32, name="v_codes%d" % a, align_bytes=64)
                 for lo in range(0, S, BANK):
-                    nc.vector.tensor_copy(codes[:, lo : lo + BANK], tab_sb[a][:].indirect(part(picked, lo, lo + BANK)))
+                    nc.vector.tensor_copy(codes[:, lo : lo + BANK], tab_sb[a][:].indirect(part(listed, lo, lo + BANK)))
                 v_codes.append(codes)
 
         late = ctx.enter_context(tc.tile_pool(name="late", bufs=1))
 
-        def product(i):
-            b, t = divmod(i, PACK)
-            u = ring4.tile([P, S], F32, name="u", tag="u")
+        z_pass0 = late.tile([P, PACK * T2], BF16)
+        z_slot2 = late.tile([P, T2], BF16)
+        z_slots01 = late.tile([P, 2 * T2], BF16)
+        z_rows = [z_pass0[:, T2 * t : T2 * (t + 1)] for t in range(PACK)]
+        z_rows.extend(z_slots01[:, T2 * t : T2 * (t + 1)] for t in range(2))
+        z_rows.append(z_slot2[:])
+
+        def products(k):
+            gain = keep.tile([P, 2 * S], F32, name="gain", tag="gain%d" % (k % 2))
+            factor = z_pass0[:, : 2 * T2].bitcast(F32) if k == 1 else gain[:]
+            wgs_sb = (wgs_low if k % 2 == 0 else wgs_high)[:].rearrange("q e j -> q (e j)")
             banks = []
+            for i in (2 * k, 2 * k + 1):
+                b, t = divmod(i, PACK)
+                factor_i = factor[:, S * (i % 2) : S * (i % 2 + 1)]
+                square = keep.tile([P, S], F32, name="square", tag="square")
+                width = BANK if i == 0 else S
+                for lo in range(0, S, BANK):
+                    cols = slice(lo, lo + BANK)
+                    acc = psum.tile([P, BANK], F32, name="acc", tag="bank")
+                    for a in range(K_PASSES):
+                        nc.tensor.matmul_mx(
+                            out=acc[:],
+                            lhsT=w4_sb[:, a, 2 * P * i : 2 * P * (i + 1)].bitcast(FP4X4),
+                            lhsT_scale=w4_scale_sb[:, a, P * i : P * (i + 1)],
+                            rhs=v_codes[a][:, cols].bitcast(FP8X4),
+                            rhs_scale=v_scale[:, a, cols],
+                            start=(a == 0),
+                            stop=(a == K_PASSES - 1),
+                        )
+                    nc.scalar.activation(square[:, cols], acc[:], ACT.Square)
+                    if cols.stop % width == 0:
+                        done = slice(cols.stop - width, cols.stop)
+                        nc.scalar.activation(
+                            factor_i[:, done], square[:, done], ACT.Identity, bias=1.0, scale=cub_sb[:, b, t : t + 1]
+                        )
+                    banks.append(acc)
+            cuts = {0: (0, BANK, S, 2 * S), 1: (0, S, 2 * S)}.get(k, (0, 2 * S))
+            for lo, hi in zip(cuts, cuts[1:]):
+                nc.gpsimd.tensor_tensor(gain[:, lo:hi], factor[:, lo:hi], wgs_sb[:, lo:hi], MULT)
+            return banks, gain
+
+        def features(i, banks, gain):
+            placed = late.tile([P, S], F32, name="placed", tag="placed%d" % (i % 2), align_bytes=64)
             for lo in range(0, S, BANK):
-                cols = slice(lo, lo + BANK)
-                acc = psum.tile([P, BANK], F32, name="acc", tag="bank")
-                for a in range(K_PASSES):
-                    nc.tensor.matmul_mx(
-                        out=acc[:],
-                        lhsT=w4_sb[:, a, 2 * P * i : 2 * P * (i + 1)].bitcast(FP4X4),
-                        lhsT_scale=w4_scale_sb[:, a, P * i : P * (i + 1)],
-                        rhs=v_codes[a][:, cols].bitcast(FP8X4),
-                        rhs_scale=v_scale[:, a, cols],
-                        start=(a == 0),
-                        stop=(a == K_PASSES - 1),
-                    )
-                nc.scalar.activation(u[:, cols], acc[:], ACT.Square)
-                nc.scalar.activation(u[:, cols], u[:, cols], ACT.Identity, bias=1.0, scale=cub_sb[:, b, t : t + 1])
-                banks.append(acc)
-            return banks, u
-
-        planes_first = late.tile([P, PACK * T2], BF16)
-        planes_second = late.tile([P, 2 * T2], BF16)
-        plane_third = late.tile([P, T2], BF16)
-        plane_of = [planes_first[:, T2 * t : T2 * (t + 1)] for t in range(PACK)]
-        plane_of.extend(planes_second[:, T2 * t : T2 * (t + 1)] for t in range(2))
-        plane_of.append(plane_third[:])
-        h_first = late.tile([P, S], F32)
-
-        def features(i, banks, u):
-            h = h_first[:] if i == 0 else plane_of[i - 1].bitcast(F32)
-            hw = late.tile([P, S], F32, name="hw", tag="h", bufs=2)
-            for acc, lo in zip(banks, range(0, S, BANK)):
-                cols = slice(lo, lo + BANK)
-                nc.vector.tensor_tensor(h[:, cols], acc[:], u[:, cols], MULT)
-                nc.gpsimd.tensor_tensor(hw[:, cols], h[:, cols], wgs_of(i % PACK)[:, cols], MULT)
-            return hw
+                at = (i % 2) * S + lo
+                nc.vector.tensor_tensor(placed[:, lo : lo + BANK], banks[at // BANK][:], gain[:, at : at + BANK], MULT)
+            return placed
 
         def interleave(dst, src):
             nc.scalar.copy(
-                dst.rearrange("p (c i) t -> p c t i", i=4),
-                src.rearrange("p t (c i) -> p c t i", i=4),
+                dst.rearrange("q (c i) t -> q c t i", i=RUN),
+                src.rearrange("q t (c i) -> q c t i", i=RUN),
             )
 
-        def group_w2(b):
-            raw = ring4.tile([P, PACK, N], F32, name="raw", tag="wide")
-            nc.sync.dma_start(raw[:], w2[P * PACK * b : P * PACK * (b + 1), :].rearrange("(p t) n -> p t n", t=PACK))
-            grouped = late.tile([P, N * PACK], BF16, name="grouped", tag="grouped", bufs=8, align_bytes=64)
-            interleave(grouped[:].rearrange("p (n t) -> p n t", t=PACK), raw[:])
-            return grouped
+        def four_to_a_column(flat):
+            return flat.rearrange("q (c t) -> q c t", t=PACK)
 
-        def group_z(pair):
-            grouped = late.tile([P, BANK * PACK], BF16, name="grouped", tag="grouped", bufs=8, align_bytes=64)
-            nc.scalar.copy(
-                grouped[:].bitcast(F32).rearrange("p (c h) -> p c h", h=2),
-                pair[:].rearrange("p h c e -> p h (c e)").bitcast(F32).rearrange("p h c -> p c h"),
-            )
-            return grouped
-
-        tiles = H_PASSES * PACK
         chunks = range(0, T2, BANK)
-        products = [product(i) for i in range(tiles)]
-        h_next = features(0, *products[0])
-        planes = pairs = None
-        w2_grouped = []
-        z_grouped = []
-        for i in range(tiles):
-            b, t = divmod(i, PACK)
-            page = pages[i % 2]
-            h = h_next
-            if i + 1 < tiles:
-                h_next = features(i + 1, *products[i + 1])
-            for lo in range(0, S, BANK):
-                nc.vector.tensor_copy(page[:].indirect(part(shelved, lo, lo + BANK)), h[:, lo : lo + BANK])
-            if i + 1 < tiles:
-                shelf_sb[i + 1] = load_shelf(i + 1)
-            if i in (3, 4):
-                w2_grouped.append(group_w2(i - 3))
+        made = {k: products(k) for k in range(2)}
+        placed_next = features(0, *made[0])
+        w2_grouped = z_grouped = pairs = None
+        for i in range(ROW_TILES):
+            page = pages[i % PAGES]
+            placed = placed_next
+            if i < LAST:
+                placed_next = features(i + 1, *made[(i + 1) // 2])
+            if i % 2 == 0 and i + 4 < ROW_TILES:
+                made[i // 2 + 2] = products(i // 2 + 2)
+            width = BANK if i == 0 else S
+            for lo in range(0, S, width):
+                nc.vector.tensor_copy(page[:].indirect(part(shelved, lo, lo + width)), placed[:, lo : lo + width])
+            if i == PACK - 1:
+                held = keep.tile([P, (H_PASSES * N + T2) * PACK], BF16, name="held", tag="cub", align_bytes=64)
+                w2_grouped = [held[:, N * PACK * b : N * PACK * (b + 1)] for b in range(H_PASSES)]
+                z_grouped = held[:, H_PASSES * N * PACK :]
+                for b in range(H_PASSES):
+                    w2_raw = ring2.tile([P, PACK, N], F32, name="w2_raw", tag="wide")
+                    w2_rows = w2[P * PACK * b : P * PACK * (b + 1), :]
+                    nc.sync.dma_start(w2_raw[:], w2_rows.rearrange("(q t) n -> q t n", t=PACK))
+                    interleave(four_to_a_column(w2_grouped[b]), w2_raw[:])
             if i == 0:
-                planes = planes_first[:].rearrange("p (t c) -> p t c", t=PACK)
+                for half, rows in zip(halves, shelf_first):
+                    nc.gpsimd.tensor_tensor(z_rows[0][:, half], page[:, half], rows[:], MULT)
+            if i < LAST:
+                shelf_sb[i + 1] = load_shelf(i + 1, slice(0, T2))
             if i == PACK:
-                planes = planes_second[:].rearrange("p (t c) -> p t c", t=2)
-                pairs = [late.tile([P, 2, BANK, 2], BF16, name="pairs", tag="pairs", bufs=4) for lo in chunks]
-            if i < tiles - 2:
-                nc.gpsimd.tensor_tensor(plane_of[i], page[:], shelf_sb[i][:], MULT)
+                pairs = [late.tile([P, 2, BANK, 2], BF16, name="pairs", tag="pairs", bufs=len(chunks)) for lo in chunks]
+            if 0 < i < LAST - 1:
+                nc.gpsimd.tensor_tensor(z_rows[i], page[:], shelf_sb[i][:], MULT)
             if i == PACK - 1:
                 for lo in chunks:
-                    grouped = late.tile([P, BANK * PACK], BF16, name="grouped", tag="grouped", bufs=8, align_bytes=64)
-                    interleave(grouped[:].rearrange("p (n t) -> p n t", t=PACK), planes[:, :, lo : lo + BANK])
-                    z_grouped.append(grouped)
-            elif i == tiles - 3:
-                for c, lo in enumerate(chunks):
-                    nc.scalar.copy(
-                        pairs[c][:, 0, :, :].rearrange("p (c i) e -> p c e i", i=4),
-                        planes[:, :, lo : lo + BANK].rearrange("p e (c i) -> p c e i", i=4),
+                    interleave(
+                        four_to_a_column(z_grouped[:, PACK * lo : PACK * (lo + BANK)]),
+                        z_pass0[:].rearrange("q (t c) -> q t c", t=PACK)[:, :, lo : lo + BANK],
                     )
-            elif i == tiles - 2:
+            elif i == LAST - 2:
                 for c, lo in enumerate(chunks):
-                    single = plane_of[i][:, T2 - BANK - lo : T2 - lo]
-                    nc.gpsimd.tensor_tensor(single, page[:, lo : lo + BANK], shelf_sb[i][:, lo : lo + BANK], MULT)
-                    nc.scalar.copy(pairs[c][:, 1, :, :], single.unsqueeze(2).to_broadcast([P, BANK, 2]))
-            elif i == tiles - 1:
+                    interleave(
+                        pairs[c][:, 0, :, :], z_slots01[:].rearrange("q (t c) -> q t c", t=2)[:, :, lo : lo + BANK]
+                    )
+            elif i == LAST - 1:
+                for c, lo in enumerate(chunks):
+                    if c % 2 == 0:
+                        half = slice(lo, lo + 2 * BANK)
+                        nc.gpsimd.tensor_tensor(z_rows[i][:, half], page[:, half], shelf_sb[i][:, half], MULT)
+                    nc.scalar.copy(
+                        pairs[c][:, 1, :, :], z_rows[i][:, lo : lo + BANK].unsqueeze(2).to_broadcast([P, BANK, 2])
+                    )
+            elif i == LAST:
                 for c, lo in enumerate(chunks):
                     nc.vector.tensor_tensor(
                         pairs[c][:, 1, :, 1], page[:, lo : lo + BANK], shelf_sb[i][:, lo : lo + BANK], MULT
                     )
 
-        early = keep.tile([P, T2 + H_PASSES * N], U32, tag="shared", align_bytes=64)
-        z_last = late.tile([P, T2], U32, align_bytes=64)
-        z_codes = [early[:, :T2], z_last[:]]
-        w2_codes = [early[:, T2 + N * b : T2 + N * (b + 1)] for b in range(H_PASSES)]
-        z_scale = keep.tile([P, H_PASSES, T2], U8, align_bytes=64)
-        w2_scale = keep.tile([P, H_PASSES, N], U8, align_bytes=64)
+        z_codes = late.tile([P, H_PASSES, T2], U32, align_bytes=64)
+        w2_codes = late.tile([P, H_PASSES, N], U32, align_bytes=64)
+        scale_bytes = late.tile([P, H_PASSES, T2 + N], U8, tag="placed%d" % (LAST % 2), align_bytes=64)
+        z_scale = scale_bytes[:, :, :T2]
+        w2_scale = scale_bytes[:, :, T2:]
         for b in range(H_PASSES):
-            nc.vector.quantize_mx(out=w2_codes[b].bitcast(FP8X4), scales=w2_scale[:, b, :], in_=w2_grouped[b][:])
-        for b in range(H_PASSES):
-            for c, lo in enumerate(chunks):
-                grouped = z_grouped[c] if b == 0 else group_z(pairs[c])
-                nc.vector.quantize_mx(
-                    out=z_codes[b][:, lo : lo + BANK].bitcast(FP8X4),
-                    scales=z_scale[:, b, lo : lo + BANK],
-                    in_=grouped[:],
-                )
+            nc.vector.quantize_mx(out=w2_codes[:, b, :].bitcast(FP8X4), scales=w2_scale[:, b, :], in_=w2_grouped[b])
+        for lo in range(0, T2, 2 * BANK):
+            nc.vector.quantize_mx(
+                out=z_codes[:, 0, lo : lo + 2 * BANK].bitcast(FP8X4),
+                scales=z_scale[:, 0, lo : lo + 2 * BANK],
+                in_=z_grouped[:, PACK * lo : PACK * (lo + 2 * BANK)],
+            )
+        for c, lo in enumerate(chunks):
+            grouped = late.tile([P, BANK * PACK], BF16, name="grouped", tag="grouped", bufs=3, align_bytes=64)
+            nc.scalar.copy(
+                grouped[:].bitcast(F32).rearrange("q (c h) -> q c h", h=2),
+                pairs[c][:].rearrange("q h c e -> q h (c e)").bitcast(F32).rearrange("q h c -> q c h"),
+            )
+            nc.vector.quantize_mx(
+                out=z_codes[:, 1, lo : lo + BANK].bitcast(FP8X4), scales=z_scale[:, 1, lo : lo + BANK], in_=grouped[:]
+            )
 
         def scores(n):
-            y = ring4.tile([P, T2], F32, name="y", tag="wide")
-            for lo in range(0, T2, BANK):
+            y = ring2.tile([P, T2], F32, name="y", tag="wide" if n < H_PASSES else "shelf")
+            for lo in chunks:
                 cols = slice(lo, lo + BANK)
                 acc = psum.tile([P, BANK], F32, name="acc", tag="bank")
                 for b in range(H_PASSES):
                     nc.tensor.matmul_mx(
                         out=acc[:],
-                        lhsT=w2_codes[b][:, P * n : P * (n + 1)].bitcast(FP8X4),
+                        lhsT=w2_codes[:, b, P * n : P * (n + 1)].bitcast(FP8X4),
                         lhsT_scale=w2_scale[:, b, P * n : P * (n + 1)],
-                        rhs=z_codes[b][:, cols].bitcast(FP8X4),
+                        rhs=z_codes[:, b, cols].bitcast(FP8X4),
                         rhs_scale=z_scale[:, b, cols],
                         start=(b == 0),
                         stop=(b == H_PASSES - 1),
                     )
                 nc.scalar.copy(y[:, cols], acc[:])
-            logits = late.tile([P, PICKS], F32, name="logits", tag="h", bufs=2)
-            x = ring4.tile([P, PICKS], F32, name="x", tag="u")
-            step = BANK if n == 0 else PICKS
-            for lo in range(0, PICKS, step):
-                cols = slice(lo, lo + step)
-                nc.vector.tensor_copy(logits[:, cols], y[:].indirect(part(promoted, lo, lo + step)))
-                nc.scalar.activation(x[:, cols], logits[:, cols], ACT.Sigmoid, bias=base_sb[:, n : n + 1])
-            return x
+            both = keep.tile([P, 2 * PICKS], F32, name="both", tag="gain%d" % (n % 2))
+            logits = both[:, :PICKS]
+            score = both[:, PICKS:]
+            width = PICKS // 2 if n == 0 else PICKS
+            for lo in range(0, PICKS, width):
+                cols = slice(lo, lo + width)
+                nc.vector.tensor_copy(logits[:, cols], y[:].indirect(part(promoted, lo, lo + width)))
+                nc.scalar.activation(score[:, cols], logits[:, cols], ACT.Sigmoid, bias=base_sb[:, n : n + 1])
+            return score
 
-        x_next = scores(0)
+        score_next = scores(0)
         for n in range(N_TILES):
-            x = x_next
+            score = score_next
             if n + 1 < N_TILES:
-                x_next = scores(n + 1)
+                score_next = scores(n + 1)
             banner = banners[n % 2]
-            nc.vector.tensor_tensor(banner[:].indirect(slots[:]), x[:], wgo_sb[:], MULT)
+            nc.vector.tensor_tensor(banner[:].indirect(banner_slots[:]), score, wgo_sb[:], MULT)
             nc.sync.dma_start(out[P * n : P * (n + 1), :], banner[:])

@@ -20,6 +20,7 @@ P = 128
 QUADRANT = 32
 QUADRANTS = P // QUADRANT
 SCALE_ROWS = 4
+SPREAD = QUADRANT // SCALE_ROWS
 PACK = 4
 BANK = 512
 BANKS = 8
@@ -28,9 +29,30 @@ K_PASSES = K // (P * PACK)
 H_PASSES = H // (P * PACK)
 ROW_TILES = H_PASSES * PACK
 LAST = ROW_TILES - 1
+HALVES = ROW_TILES * 2
 N_TILES = N // P
 PAGES = 3
 RUN = 4
+
+AT_TABLE = (0, 16)
+AT_PAGE = (68, 0, 16)
+AT_SHELF = (8, 24)
+AT_TAB_SCALES, AT_W4_RAW, AT_W4_SCALES, AT_PICKED_SCALES = 32, 40, 44, 46
+AT_WGS = 32
+AT_PAIRS = 32
+AT_W4 = 48
+AT_CODES = (56, 60)
+AT_BANNER = (48, 56)
+AT_SCALES = 64
+AT_Z_PASS0, AT_Z45, AT_Z6 = 76, 92, 100
+AT_Z_GROUPED = 104
+AT_W2_GROUPED = 120
+AT_W2_RAW = 128
+AT_Y = (128, 136, 104, 112)
+AT_PLACED = (144, 148)
+AT_GAIN = (154, 158)
+AT_SCORE = (154, 162)
+AT_Z_CODES, AT_W2_CODES, AT_BASE = 170, 186, 190
 
 
 def tile_list_audiobook_banner_scores_kernel(
@@ -38,152 +60,164 @@ def tile_list_audiobook_banner_scores_kernel(
 ):
     nc = tc.nc
     with ExitStack() as ctx:
-        keep = ctx.enter_context(tc.tile_pool(name="keep", bufs=1))
-        ring2 = ctx.enter_context(tc.tile_pool(name="ring2", bufs=2))
+        list_pool = ctx.enter_context(tc.tile_pool(name="lists", bufs=1))
+        pool = ctx.enter_context(tc.tile_pool(name="sbuf", bufs=1))
         psum = ctx.enter_context(tc.psum_pool(name="psum", bufs=BANKS))
+
+        def place(name, shape, dtype, kib):
+            return pool.tile(shape, dtype, name=name, offset=1024 * kib, align_bytes=64)
 
         def part(list_tile, lo, hi):
             return list_tile[:, lo // PER_COLUMN : hi // PER_COLUMN]
 
-        def load_scale_rows(queue, tile, scales):
-            for quadrant in range(QUADRANTS):
-                first, row = QUADRANT * quadrant, SCALE_ROWS * quadrant
-                queue.dma_start(
-                    tile[first : first + SCALE_ROWS, :, :].bitcast(I32),
-                    scales[:, row : row + SCALE_ROWS, :].rearrange("a r n -> r a n").bitcast(I32),
-                )
+        lists = []
+        for name, src in (("offs", offs), ("offs2", offs2), ("offs3", offs3), ("offs4", offs4)):
+            list_tile = list_pool.tile([P, S // PER_COLUMN], U16, name=name + "_sb")
+            nc.sync.dma_start(list_tile[:], src)
+            lists.append(list_tile)
+        listed, shelved, promoted, banner_slots = lists
 
-        def load_wgs(tile, slots):
-            rows = wgs.rearrange("(q t) j -> q t j", t=PACK)
-            for quadrant in range(QUADRANTS):
-                nc.sync.dma_start(tile[QUADRANT * quadrant : QUADRANT * (quadrant + 1), :, :], rows[:, slots, :])
+        tab_sb = []
+        for a in range(K_PASSES):
+            words = place("tab_sb%d" % a, [P, T], U32, AT_TABLE[a])
+            nc.sync.dma_start(words[:].bitcast(I32), tab_words[a].rearrange("q n t -> q (n t)").bitcast(I32))
+            tab_sb.append(words)
 
-        def load_shelf(i, cols):
-            rows = ring2.tile([P, cols.stop - cols.start], F32, name="rows", tag="shelf")
+        w4_raw = place("w4_raw", [P, K_PASSES, 2 * H], U8, AT_W4_RAW)
+        nc.scalar.dma_start(w4_raw[:].bitcast(I32), w4_words.rearrange("a q n -> q a n").bitcast(I32))
+        tab_scale_sb = place("tab_scale_sb", [P, K_PASSES, T], U8, AT_TAB_SCALES)
+        w4_scale_raw = place("w4_scale_raw", [P, K_PASSES, H], U8, AT_W4_SCALES)
+        for tile, scales in ((tab_scale_sb, tab_scales), (w4_scale_raw, w4_scales)):
+            nc.vector.memset(tile[:].bitcast(I32), 0)
+            nc.scalar.dma_start(tile[0:P:SPREAD, :, :].bitcast(I32), scales.rearrange("a r n -> r a n").bitcast(I32))
+
+        cub_sb = place("cub_sb", [P, H_PASSES, PACK], F32, AT_W2_GROUPED)
+        nc.gpsimd.dma_start(cub_sb[:], cub.rearrange("(b q t) -> q b t", b=H_PASSES, t=PACK))
+        base_sb = place("base_sb", [P, N_TILES], F32, AT_BASE)
+        with nc.allow_non_contiguous_dma(reason="one bias value a partition"):
+            nc.gpsimd.dma_start(base_sb[:], base.rearrange("(c q) -> q c", q=P))
+
+        pages = [place("page%d" % i, [P, T2], F32, AT_PAGE[i]) for i in range(PAGES)]
+        nc.vector.memset(pages[0][:], 0.0)
+
+        scales1 = place("scales1", [P, 2 * K_PASSES * S], U8, AT_SCALES)
+        v_scale = [scales1[:, S * a : S * (a + 1)] for a in range(K_PASSES)]
+        w4_scale = [scales1[:, S * (K_PASSES + a) : S * (K_PASSES + a + 1)] for a in range(K_PASSES)]
+        nc.vector.tensor_copy(
+            scales1[:, K_PASSES * S :].rearrange("q (g t m) -> q g t m", t=PACK, m=P),
+            w4_scale_raw[:].rearrange("q a (b m t) -> q (a b) t m", b=H_PASSES, t=PACK),
+        )
+        picked_scales = place("picked_scales", [P, K_PASSES * S], U8, AT_PICKED_SCALES)
+        for a in range(K_PASSES):
+            nc.vector.tensor_copy(picked_scales[:, S * a : S * (a + 1)], tab_scale_sb[:, a, :].indirect(listed[:]))
+        nc.vector.tensor_copy(scales1[:, : K_PASSES * S].bitcast(I32), picked_scales[:].bitcast(I32))
+        for row in range(1, SCALE_ROWS):
+            nc.scalar.dma_start(
+                scales1[row:P:QUADRANT, :].bitcast(I32), scales1[SPREAD * row : P : QUADRANT, :].bitcast(I32)
+            )
+
+        w4_sb = place("w4_sb", [P, K_PASSES, 2 * H], U8, AT_W4)
+        nc.vector.tensor_copy(
+            w4_sb[:].bitcast(U16).rearrange("q a (b t m) -> q (a b) t m", b=H_PASSES, t=PACK),
+            w4_raw[:].bitcast(U16).rearrange("q a (b m t) -> q (a b) t m", b=H_PASSES, t=PACK),
+        )
+
+        wgs_sb = place("wgs_sb", [P, PACK * S], F32, AT_WGS)
+        wgs_rows = wgs.rearrange("(q t) j -> q (t j)", t=PACK)
+        for cols in (slice(0, S), slice(S, PACK * S)):
+            for quadrant in (0, 2, 1, 3):
+                nc.sync.dma_start(wgs_sb[QUADRANT * quadrant : QUADRANT * (quadrant + 1), cols], wgs_rows[:, cols])
+
+        v_codes = []
+        for a in range(K_PASSES):
+            codes = place("v_codes%d" % a, [P, S], U32, AT_CODES[a])
+            width = S if a < K_PASSES - 1 else BANK
+            for lo in range(0, S, width):
+                nc.vector.tensor_copy(codes[:, lo : lo + width], tab_sb[a][:].indirect(part(listed, lo, lo + width)))
+            v_codes.append(codes)
+
+        def load_shelf(i):
+            rows = place("shelf%d" % (i % 2), [P, T2], F32, AT_SHELF[i % 2])
             by_tile = shelf.rearrange("(b q t) c -> b t q c", b=H_PASSES, t=PACK)
-            nc.sync.dma_start(rows[:], by_tile[i // PACK, i % PACK][:, cols])
+            nc.sync.dma_start(rows[:], by_tile[i // PACK, i % PACK])
             return rows
 
-        with tc.tile_pool(name="head", bufs=1) as head:
-            lists = []
-            for name, src in (("offs", offs), ("offs2", offs2), ("offs3", offs3), ("offs4", offs4)):
-                list_tile = keep.tile([P, S // PER_COLUMN], U16, name=name + "_sb")
-                nc.sync.dma_start(list_tile[:], src)
-                lists.append(list_tile)
-            listed, shelved, promoted, banner_slots = lists
+        shelf_sb = {i: load_shelf(i) for i in range(2)}
+        for page in pages[1:]:
+            nc.gpsimd.memset(page[:], 0.0)
 
-            cub_sb = keep.tile([P, H_PASSES, PACK], F32, tag="cub", align_bytes=64)
-            nc.sync.dma_start(cub_sb[:], cub.rearrange("(b q t) -> q b t", b=H_PASSES, t=PACK))
-            base_sb = keep.tile([P, N_TILES], F32)
-            with nc.allow_non_contiguous_dma(reason="one bias value a partition"):
-                nc.sync.dma_start(base_sb[:], base.rearrange("(c q) -> q c", q=P))
-
-            tab_scale_sb = head.tile([P, K_PASSES, T], U8, align_bytes=64)
-            nc.gpsimd.memset(tab_scale_sb[:].bitcast(I32), 0)
-            w4_scale_raw = head.tile([P, K_PASSES, H], U8, align_bytes=64)
-            nc.gpsimd.memset(w4_scale_raw[:].bitcast(I32), 0)
-            load_scale_rows(nc.scalar, w4_scale_raw, w4_scales)
-            w4_raw = head.tile([P, K_PASSES, 2 * H], U8, align_bytes=64)
-            nc.sync.dma_start(w4_raw[:].bitcast(I32), w4_words.rearrange("a q n -> q a n").bitcast(I32))
-            load_scale_rows(nc.sync, tab_scale_sb, tab_scales)
-            tab_sb = []
-            for a in range(K_PASSES):
-                words = head.tile([P, T], U32, name="tab_sb%d" % a, align_bytes=64)
-                nc.sync.dma_start(words[:].bitcast(I32), tab_words[a].rearrange("q n t -> q (n t)").bitcast(I32))
-                tab_sb.append(words)
-
-            wgs_low = keep.tile([P, 2, S], F32)
-            wgs_high = keep.tile([P, 2, S], F32)
-            load_wgs(wgs_low, slice(0, 2))
-            load_wgs(wgs_high, slice(2, PACK))
-            wgo_sb = keep.tile([P, PICKS], F32)
-            nc.sync.dma_start(wgo_sb[:], wgo)
-            halves = (slice(0, T2 // 2), slice(T2 // 2, T2))
-            shelf_first = [load_shelf(0, half) for half in halves]
-            shelf_sb = {}
-
-            pages = []
-            for i in range(PAGES):
-                page = keep.tile([P, T2], F32, name="page%d" % i)
-                nc.gpsimd.memset(page[:], 0.0)
-                pages.append(page)
-            banners = []
-            for i in range(2):
-                banner = keep.tile([P, T2], F32, name="banner%d" % i)
-                nc.gpsimd.memset(banner[:], 0.0)
-                banners.append(banner)
-
-            w4_sb = keep.tile([P, K_PASSES, 2 * H], U8, align_bytes=64)
-            nc.vector.tensor_copy(
-                w4_sb[:].bitcast(U16).rearrange("q a (b t m) -> q (a b) t m", b=H_PASSES, t=PACK),
-                w4_raw[:].bitcast(U16).rearrange("q a (b m t) -> q (a b) t m", b=H_PASSES, t=PACK),
-            )
-            w4_scale_sb = keep.tile([P, K_PASSES, H], U8, align_bytes=64)
-            nc.vector.tensor_copy(
-                w4_scale_sb[:].rearrange("q a (b t m) -> q (a b) t m", b=H_PASSES, t=PACK),
-                w4_scale_raw[:].rearrange("q a (b m t) -> q (a b) t m", b=H_PASSES, t=PACK),
-            )
-
-            v_scale = keep.tile([P, K_PASSES, S], U8, align_bytes=64)
-            for a in range(K_PASSES):
-                nc.vector.tensor_copy(v_scale[:, a, :], tab_scale_sb[:, a, :].indirect(listed[:]))
-            v_codes = []
-            for a in range(K_PASSES):
-                codes = keep.tile([P, S], U32, name="v_codes%d" % a, align_bytes=64)
-                for lo in range(0, S, BANK):
-                    nc.vector.tensor_copy(codes[:, lo : lo + BANK], tab_sb[a][:].indirect(part(listed, lo, lo + BANK)))
-                v_codes.append(codes)
-
-        late = ctx.enter_context(tc.tile_pool(name="late", bufs=1))
-
-        z_pass0 = late.tile([P, PACK * T2], BF16)
-        z_slot2 = late.tile([P, T2], BF16)
-        z_slots01 = late.tile([P, 2 * T2], BF16)
+        z_pass0 = place("z_pass0", [P, PACK * T2], BF16, AT_Z_PASS0)
+        z45 = place("z45", [P, 2 * T2], BF16, AT_Z45)
+        z6 = place("z6", [P, T2], BF16, AT_Z6)
         z_rows = [z_pass0[:, T2 * t : T2 * (t + 1)] for t in range(PACK)]
-        z_rows.extend(z_slots01[:, T2 * t : T2 * (t + 1)] for t in range(2))
-        z_rows.append(z_slot2[:])
+        z_rows.extend(z45[:, T2 * t : T2 * (t + 1)] for t in range(2))
+        z_rows.append(z6[:])
 
-        def products(k):
-            gain = keep.tile([P, 2 * S], F32, name="gain", tag="gain%d" % (k % 2))
-            factor = z_pass0[:, : 2 * T2].bitcast(F32) if k == 1 else gain[:]
-            wgs_sb = (wgs_low if k % 2 == 0 else wgs_high)[:].rearrange("q e j -> q (e j)")
-            banks = []
-            for i in (2 * k, 2 * k + 1):
-                b, t = divmod(i, PACK)
-                factor_i = factor[:, S * (i % 2) : S * (i % 2 + 1)]
-                square = keep.tile([P, S], F32, name="square", tag="square")
-                width = BANK if i == 0 else S
-                for lo in range(0, S, BANK):
-                    cols = slice(lo, lo + BANK)
-                    acc = psum.tile([P, BANK], F32, name="acc", tag="bank")
-                    for a in range(K_PASSES):
-                        nc.tensor.matmul_mx(
-                            out=acc[:],
-                            lhsT=w4_sb[:, a, 2 * P * i : 2 * P * (i + 1)].bitcast(FP4X4),
-                            lhsT_scale=w4_scale_sb[:, a, P * i : P * (i + 1)],
-                            rhs=v_codes[a][:, cols].bitcast(FP8X4),
-                            rhs_scale=v_scale[:, a, cols],
-                            start=(a == 0),
-                            stop=(a == K_PASSES - 1),
-                        )
-                    nc.scalar.activation(square[:, cols], acc[:], ACT.Square)
-                    if cols.stop % width == 0:
-                        done = slice(cols.stop - width, cols.stop)
-                        nc.scalar.activation(
-                            factor_i[:, done], square[:, done], ACT.Identity, bias=1.0, scale=cub_sb[:, b, t : t + 1]
-                        )
-                    banks.append(acc)
-            cuts = {0: (0, BANK, S, 2 * S), 1: (0, S, 2 * S)}.get(k, (0, 2 * S))
-            for lo, hi in zip(cuts, cuts[1:]):
-                nc.gpsimd.tensor_tensor(gain[:, lo:hi], factor[:, lo:hi], wgs_sb[:, lo:hi], MULT)
-            return banks, gain
+        factor0 = place("factor0", [P, BANK], F32, AT_W2_RAW)
+        hosts = {0: z_rows[6], 1: z_rows[5], LAST: z_rows[5]}
+        for j in range(2, LAST):
+            hosts[j] = z_rows[j - 2]
 
-        def features(i, banks, gain):
-            placed = late.tile([P, S], F32, name="placed", tag="placed%d" % (i % 2), align_bytes=64)
-            for lo in range(0, S, BANK):
-                at = (i % 2) * S + lo
-                nc.vector.tensor_tensor(placed[:, lo : lo + BANK], banks[at // BANK][:], gain[:, at : at + BANK], MULT)
-            return placed
+        def factor_of(u):
+            if u == 0:
+                return factor0[:]
+            j, e = divmod(u - 1, 2)
+            return hosts[j].bitcast(F32)[:, BANK * e : BANK * (e + 1)]
+
+        banks = {}
+
+        def product(u):
+            i, h = divmod(u, 2)
+            b, t = divmod(i, PACK)
+            cols = slice(BANK * h, BANK * (h + 1))
+            acc = psum.tile([P, BANK], F32, name="acc", tag="bank")
+            for a in range(K_PASSES):
+                nc.tensor.matmul_mx(
+                    out=acc[:],
+                    lhsT=w4_sb[:, a, 2 * P * i : 2 * P * (i + 1)].bitcast(FP4X4),
+                    lhsT_scale=w4_scale[a][:, P * i : P * (i + 1)],
+                    rhs=v_codes[a][:, cols].bitcast(FP8X4),
+                    rhs_scale=v_scale[a][:, cols],
+                    start=(a == 0),
+                    stop=(a == K_PASSES - 1),
+                )
+            factor = factor_of(u)
+            nc.scalar.activation(factor, acc[:], ACT.Square)
+            nc.scalar.activation(factor, factor, ACT.Identity, bias=1.0, scale=cub_sb[:, b, t : t + 1])
+            banks[u] = acc
+
+        gains = {}
+
+        def couple(j):
+            halves = [u for u in (2 * j + 1, 2 * j + 2) if u < HALVES]
+            gain = place("gain%d" % (j % 2), [P, S], F32, AT_GAIN[j % 2])
+            first = BANK * halves[0] % (PACK * S)
+            whole = j > 0 and len(halves) == 2 and first + S <= PACK * S
+            for u in halves:
+                product(u)
+                e = u - halves[0]
+                gains[u] = gain[:, BANK * e : BANK * (e + 1)]
+                if not whole:
+                    at = BANK * u % (PACK * S)
+                    nc.gpsimd.tensor_tensor(gains[u], factor_of(u), wgs_sb[:, at : at + BANK], MULT)
+            if whole:
+                nc.gpsimd.tensor_tensor(gain[:], hosts[j].bitcast(F32), wgs_sb[:, first : first + S], MULT)
+
+        placed = {}
+
+        def features(u):
+            i, h = divmod(u, 2)
+            if h == 0:
+                placed[i] = place("placed%d" % (i % 2), [P, S], F32, AT_PLACED[i % 2])
+            dst = placed[i][:, BANK * h : BANK * (h + 1)]
+            if u == 0:
+                nc.vector.tensor_tensor(dst, banks[u][:], wgs_sb[:, :BANK], MULT)
+                nc.vector.tensor_tensor(dst, dst, factor0[:], MULT)
+            else:
+                nc.vector.tensor_tensor(dst, banks[u][:], gains[u], MULT)
+
+        def shelve(i, lo, hi):
+            nc.vector.tensor_copy(pages[i % PAGES][:].indirect(part(shelved, lo, hi)), placed[i][:, lo:hi])
 
         def interleave(dst, src):
             nc.scalar.copy(
@@ -195,48 +229,48 @@ def tile_list_audiobook_banner_scores_kernel(
             return flat.rearrange("q (c t) -> q c t", t=PACK)
 
         chunks = range(0, T2, BANK)
-        made = {k: products(k) for k in range(2)}
-        placed_next = features(0, *made[0])
-        w2_grouped = z_grouped = pairs = None
+        product(0)
+        couple(0)
+        couple(1)
+        features(0)
+        shelve(0, 0, BANK)
+        w2_raw = place("w2_raw", [P, H_PASSES, PACK * N], F32, AT_W2_RAW)
+        nc.sync.dma_start(w2_raw[:], w2.rearrange("(b q t) n -> q b (t n)", b=H_PASSES, t=PACK))
+        banners = []
+        w2_grouped = z_grouped = pairs = wgo_sb = None
         for i in range(ROW_TILES):
             page = pages[i % PAGES]
-            placed = placed_next
-            if i < LAST:
-                placed_next = features(i + 1, *made[(i + 1) // 2])
-            if i % 2 == 0 and i + 4 < ROW_TILES:
-                made[i // 2 + 2] = products(i // 2 + 2)
-            width = BANK if i == 0 else S
-            for lo in range(0, S, width):
-                nc.vector.tensor_copy(page[:].indirect(part(shelved, lo, lo + width)), placed[:, lo : lo + width])
-            if i == PACK - 1:
-                held = keep.tile([P, (H_PASSES * N + T2) * PACK], BF16, name="held", tag="cub", align_bytes=64)
-                w2_grouped = [held[:, N * PACK * b : N * PACK * (b + 1)] for b in range(H_PASSES)]
-                z_grouped = held[:, H_PASSES * N * PACK :]
+            for u in (2 * i + 1, 2 * i + 2):
+                if u < HALVES:
+                    features(u)
+            shelve(i, BANK if i == 0 else 0, S)
+            if i + 2 <= LAST:
+                couple(i + 2)
+            if i + 2 == LAST:
+                wgo_sb = place("wgo_sb", [P, PICKS], F32, AT_SCALES)
+                nc.sync.dma_start(wgo_sb[:], wgo)
+                w2_grouped = place("w2_grouped", [P, H_PASSES, N * PACK], BF16, AT_W2_GROUPED)
                 for b in range(H_PASSES):
-                    w2_raw = ring2.tile([P, PACK, N], F32, name="w2_raw", tag="wide")
-                    w2_rows = w2[P * PACK * b : P * PACK * (b + 1), :]
-                    nc.sync.dma_start(w2_raw[:], w2_rows.rearrange("(q t) n -> q t n", t=PACK))
-                    interleave(four_to_a_column(w2_grouped[b]), w2_raw[:])
-            if i == 0:
-                for half, rows in zip(halves, shelf_first):
-                    nc.gpsimd.tensor_tensor(z_rows[0][:, half], page[:, half], rows[:], MULT)
-            if i < LAST:
-                shelf_sb[i + 1] = load_shelf(i + 1, slice(0, T2))
-            if i == PACK:
-                pairs = [late.tile([P, 2, BANK, 2], BF16, name="pairs", tag="pairs", bufs=len(chunks)) for lo in chunks]
-            if 0 < i < LAST - 1:
+                    interleave(
+                        four_to_a_column(w2_grouped[:, b, :]), w2_raw[:, b, :].rearrange("q (t n) -> q t n", t=PACK)
+                    )
+            if i < LAST - 1:
                 nc.gpsimd.tensor_tensor(z_rows[i], page[:], shelf_sb[i][:], MULT)
             if i == PACK - 1:
+                z_grouped = place("z_grouped", [P, PACK * T2], BF16, AT_Z_GROUPED)
                 for lo in chunks:
                     interleave(
                         four_to_a_column(z_grouped[:, PACK * lo : PACK * (lo + BANK)]),
                         z_pass0[:].rearrange("q (t c) -> q t c", t=PACK)[:, :, lo : lo + BANK],
                     )
             elif i == LAST - 2:
+                for n in range(2):
+                    banner = place("banner%d" % n, [P, T2], F32, AT_BANNER[n])
+                    nc.gpsimd.memset(banner[:], 0.0)
+                    banners.append(banner)
+                pairs = [place("pairs%d" % c, [P, 2, BANK, 2], BF16, AT_PAIRS + 4 * c) for c in range(len(chunks))]
                 for c, lo in enumerate(chunks):
-                    interleave(
-                        pairs[c][:, 0, :, :], z_slots01[:].rearrange("q (t c) -> q t c", t=2)[:, :, lo : lo + BANK]
-                    )
+                    interleave(pairs[c][:, 0, :, :], z45[:].rearrange("q (t c) -> q t c", t=2)[:, :, lo : lo + BANK])
             elif i == LAST - 1:
                 for c, lo in enumerate(chunks):
                     if c % 2 == 0:
@@ -250,14 +284,24 @@ def tile_list_audiobook_banner_scores_kernel(
                     nc.vector.tensor_tensor(
                         pairs[c][:, 1, :, 1], page[:, lo : lo + BANK], shelf_sb[i][:, lo : lo + BANK], MULT
                     )
+            if i + 2 <= LAST:
+                shelf_sb[i + 2] = load_shelf(i + 2)
 
-        z_codes = late.tile([P, H_PASSES, T2], U32, align_bytes=64)
-        w2_codes = late.tile([P, H_PASSES, N], U32, align_bytes=64)
-        scale_bytes = late.tile([P, H_PASSES, T2 + N], U8, tag="placed%d" % (LAST % 2), align_bytes=64)
+        z_codes = place("z_codes", [P, H_PASSES, T2], U32, AT_Z_CODES)
+        w2_codes = place("w2_codes", [P, H_PASSES, N], U32, AT_W2_CODES)
+        scale_bytes = place("scale_bytes", [P, H_PASSES, T2 + N], U8, AT_PLACED[LAST % 2])
         z_scale = scale_bytes[:, :, :T2]
         w2_scale = scale_bytes[:, :, T2:]
-        for b in range(H_PASSES):
-            nc.vector.quantize_mx(out=w2_codes[:, b, :].bitcast(FP8X4), scales=w2_scale[:, b, :], in_=w2_grouped[b])
+
+        def quantise_w2(lo, hi):
+            for b in range(H_PASSES):
+                nc.vector.quantize_mx(
+                    out=w2_codes[:, b, lo:hi].bitcast(FP8X4),
+                    scales=w2_scale[:, b, lo:hi],
+                    in_=w2_grouped[:, b, PACK * lo : PACK * hi],
+                )
+
+        quantise_w2(0, N // 2)
         for lo in range(0, T2, 2 * BANK):
             nc.vector.quantize_mx(
                 out=z_codes[:, 0, lo : lo + 2 * BANK].bitcast(FP8X4),
@@ -265,7 +309,7 @@ def tile_list_audiobook_banner_scores_kernel(
                 in_=z_grouped[:, PACK * lo : PACK * (lo + 2 * BANK)],
             )
         for c, lo in enumerate(chunks):
-            grouped = late.tile([P, BANK * PACK], BF16, name="grouped", tag="grouped", bufs=3, align_bytes=64)
+            grouped = place("grouped%d" % c, [P, BANK * PACK], BF16, AT_Z_PASS0 + 4 * c)
             nc.scalar.copy(
                 grouped[:].bitcast(F32).rearrange("q (c h) -> q c h", h=2),
                 pairs[c][:].rearrange("q h c e -> q h (c e)").bitcast(F32).rearrange("q h c -> q c h"),
@@ -273,38 +317,37 @@ def tile_list_audiobook_banner_scores_kernel(
             nc.vector.quantize_mx(
                 out=z_codes[:, 1, lo : lo + BANK].bitcast(FP8X4), scales=z_scale[:, 1, lo : lo + BANK], in_=grouped[:]
             )
+        quantise_w2(N // 2, N)
 
-        def scores(n):
-            y = ring2.tile([P, T2], F32, name="y", tag="wide" if n < H_PASSES else "shelf")
-            for lo in chunks:
-                cols = slice(lo, lo + BANK)
-                acc = psum.tile([P, BANK], F32, name="acc", tag="bank")
-                for b in range(H_PASSES):
-                    nc.tensor.matmul_mx(
-                        out=acc[:],
-                        lhsT=w2_codes[:, b, P * n : P * (n + 1)].bitcast(FP8X4),
-                        lhsT_scale=w2_scale[:, b, P * n : P * (n + 1)],
-                        rhs=z_codes[:, b, cols].bitcast(FP8X4),
-                        rhs_scale=z_scale[:, b, cols],
-                        start=(b == 0),
-                        stop=(b == H_PASSES - 1),
-                    )
-                nc.scalar.copy(y[:, cols], acc[:])
-            both = keep.tile([P, 2 * PICKS], F32, name="both", tag="gain%d" % (n % 2))
-            logits = both[:, :PICKS]
-            score = both[:, PICKS:]
-            width = PICKS // 2 if n == 0 else PICKS
-            for lo in range(0, PICKS, width):
-                cols = slice(lo, lo + width)
-                nc.vector.tensor_copy(logits[:, cols], y[:].indirect(part(promoted, lo, lo + width)))
-                nc.scalar.activation(score[:, cols], logits[:, cols], ACT.Sigmoid, bias=base_sb[:, n : n + 1])
-            return score
+        def second_pass(acc, n, b, lo):
+            nc.tensor.matmul_mx(
+                out=acc[:],
+                lhsT=w2_codes[:, b, P * n : P * (n + 1)].bitcast(FP8X4),
+                lhsT_scale=w2_scale[:, b, P * n : P * (n + 1)],
+                rhs=z_codes[:, b, lo : lo + BANK].bitcast(FP8X4),
+                rhs_scale=z_scale[:, b, lo : lo + BANK],
+                start=(b == 0),
+                stop=(b == H_PASSES - 1),
+            )
 
-        score_next = scores(0)
+        def second_product(n):
+            y = place("y%d" % n, [P, T2], F32, AT_Y[n])
+            accs = [psum.tile([P, BANK], F32, name="acc", tag="bank") for lo in chunks]
+            for b in range(H_PASSES):
+                for acc, lo in zip(accs, chunks):
+                    second_pass(acc, n, b, lo)
+            for acc, lo in zip(accs, chunks):
+                nc.scalar.copy(y[:, lo : lo + BANK], acc[:])
+            both = place("both%d" % (n % 2), [P, 2 * PICKS], F32, AT_SCORE[n % 2])
+            nc.vector.tensor_copy(both[:, :PICKS], y[:].indirect(promoted[:]))
+            return both
+
+        picked_next = second_product(0)
         for n in range(N_TILES):
-            score = score_next
+            both = picked_next
             if n + 1 < N_TILES:
-                score_next = scores(n + 1)
+                picked_next = second_product(n + 1)
+            nc.scalar.activation(both[:, PICKS:], both[:, :PICKS], ACT.Sigmoid, bias=base_sb[:, n : n + 1])
             banner = banners[n % 2]
-            nc.vector.tensor_tensor(banner[:].indirect(banner_slots[:]), score, wgo_sb[:], MULT)
+            nc.vector.tensor_tensor(banner[:].indirect(banner_slots[:]), both[:, PICKS:], wgo_sb[:], MULT)
             nc.sync.dma_start(out[P * n : P * (n + 1), :], banner[:])

@@ -32,27 +32,28 @@ LAST = ROW_TILES - 1
 HALVES = ROW_TILES * 2
 N_TILES = N // P
 PAGES = 3
+SHELVES = 4
 RUN = 4
 
 AT_TABLE = (0, 16)
-AT_PAGE = (68, 0, 16)
-AT_SHELF = (8, 24)
-AT_TAB_SCALES, AT_W4_RAW, AT_W4_SCALES, AT_PICKED_SCALES = 32, 40, 44, 46
-AT_WGS = 32
-AT_PAIRS = 32
-AT_W4 = 48
-AT_CODES = (56, 60)
-AT_BANNER = (48, 56)
-AT_SCALES = 64
-AT_Z_PASS0, AT_Z45, AT_Z6 = 76, 92, 100
-AT_Z_GROUPED = 104
-AT_W2_GROUPED = 120
-AT_W2_RAW = 128
-AT_Y = (128, 136, 104, 112)
-AT_PLACED = (144, 148)
-AT_GAIN = (154, 158)
-AT_SCORE = (154, 162)
-AT_Z_CODES, AT_W2_CODES, AT_BASE = 170, 186, 190
+AT_SHELF = (16, 24, 32, 40)
+AT_WGS = 0
+AT_PAIRS = 0
+AT_TAB_SCALES, AT_W4_SCALES, AT_W4_RAW = 32, 36, 46
+AT_PAGE = (80, 48, 56)
+AT_PICKED_SCALES = 63.5
+AT_CODES = (64, 68)
+AT_W4, AT_SCALES = 72, 76
+AT_BANNER = (32, 80)
+AT_Z_PASS0, AT_Z45, AT_Z6 = 88, 104, 112
+AT_Z_GROUPED = 116
+AT_W2_GROUPED = 132
+AT_W2_RAW, AT_WGO = 140, 156
+AT_Y = (140, 148, 116, 124)
+AT_PLACED = (160, 164)
+AT_GAIN = (32, 40, 140, 16, 24, 32, 40, 16)
+AT_SCORE = (170, 178)
+AT_Z_CODES, AT_W2_CODES, AT_BASE = 186, 202, 206
 
 
 def tile_list_audiobook_banner_scores_kernel(
@@ -65,31 +66,38 @@ def tile_list_audiobook_banner_scores_kernel(
         psum = ctx.enter_context(tc.psum_pool(name="psum", bufs=BANKS))
 
         def place(name, shape, dtype, kib):
-            return pool.tile(shape, dtype, name=name, offset=1024 * kib, align_bytes=64)
+            return pool.tile(shape, dtype, name=name, offset=int(1024 * kib), align_bytes=64)
 
         def part(list_tile, lo, hi):
             return list_tile[:, lo // PER_COLUMN : hi // PER_COLUMN]
 
-        lists = []
-        for name, src in (("offs", offs), ("offs2", offs2), ("offs3", offs3), ("offs4", offs4)):
-            list_tile = list_pool.tile([P, S // PER_COLUMN], U16, name=name + "_sb")
+        def load_list(name, src):
+            list_tile = list_pool.tile([P, S // PER_COLUMN], U16, name=name)
             nc.sync.dma_start(list_tile[:], src)
-            lists.append(list_tile)
-        listed, shelved, promoted, banner_slots = lists
+            return list_tile
 
-        tab_sb = []
-        for a in range(K_PASSES):
+        def load_table(a):
             words = place("tab_sb%d" % a, [P, T], U32, AT_TABLE[a])
             nc.sync.dma_start(words[:].bitcast(I32), tab_words[a].rearrange("q n t -> q (n t)").bitcast(I32))
-            tab_sb.append(words)
+            return words
 
+        listed = load_list("listed", offs)
+        shelved = load_list("shelved", offs2)
         w4_raw = place("w4_raw", [P, K_PASSES, 2 * H], U8, AT_W4_RAW)
-        nc.scalar.dma_start(w4_raw[:].bitcast(I32), w4_words.rearrange("a q n -> q a n").bitcast(I32))
-        tab_scale_sb = place("tab_scale_sb", [P, K_PASSES, T], U8, AT_TAB_SCALES)
+        nc.sync.dma_start(w4_raw[:].bitcast(I32), w4_words.rearrange("a q n -> q a n").bitcast(I32))
+        promoted = load_list("promoted", offs3)
+        tab_scale_sb = place("tab_scale_sb", [P, T], U8, AT_TAB_SCALES)
+        nc.vector.memset(tab_scale_sb[:].bitcast(I32), 0)
+        for a in range(K_PASSES):
+            nc.sync.dma_start(tab_scale_sb[SCALE_ROWS * a : P : SPREAD, :].bitcast(I32), tab_scales[a].bitcast(I32))
         w4_scale_raw = place("w4_scale_raw", [P, K_PASSES, H], U8, AT_W4_SCALES)
-        for tile, scales in ((tab_scale_sb, tab_scales), (w4_scale_raw, w4_scales)):
-            nc.vector.memset(tile[:].bitcast(I32), 0)
-            nc.scalar.dma_start(tile[0:P:SPREAD, :, :].bitcast(I32), scales.rearrange("a r n -> r a n").bitcast(I32))
+        nc.vector.memset(w4_scale_raw[:].bitcast(I32), 0)
+        nc.sync.dma_start(
+            w4_scale_raw[0:P:SPREAD, :, :].bitcast(I32), w4_scales.rearrange("a r n -> r a n").bitcast(I32)
+        )
+        tab_sb = [load_table(0)]
+        banner_slots = load_list("banner_slots", offs4)
+        tab_sb.append(load_table(1))
 
         cub_sb = place("cub_sb", [P, H_PASSES, PACK], F32, AT_W2_GROUPED)
         nc.gpsimd.dma_start(cub_sb[:], cub.rearrange("(b q t) -> q b t", b=H_PASSES, t=PACK))
@@ -101,19 +109,24 @@ def tile_list_audiobook_banner_scores_kernel(
         nc.vector.memset(pages[0][:], 0.0)
 
         scales1 = place("scales1", [P, 2 * K_PASSES * S], U8, AT_SCALES)
-        v_scale = [scales1[:, S * a : S * (a + 1)] for a in range(K_PASSES)]
-        w4_scale = [scales1[:, S * (K_PASSES + a) : S * (K_PASSES + a + 1)] for a in range(K_PASSES)]
+        w4_scale = [scales1[:, S * a : S * (a + 1)] for a in range(K_PASSES)]
+        v_scale = [scales1[:, S * (K_PASSES + a) : S * (K_PASSES + a + 1)] for a in range(K_PASSES)]
+        picked_scales = place("picked_scales", [P, S], U8, AT_PICKED_SCALES)
+        nc.vector.tensor_copy(picked_scales[:], tab_scale_sb[:].indirect(listed[:]))
         nc.vector.tensor_copy(
-            scales1[:, K_PASSES * S :].rearrange("q (g t m) -> q g t m", t=PACK, m=P),
+            scales1[:, : K_PASSES * S].rearrange("q (g t m) -> q g t m", t=PACK, m=P),
             w4_scale_raw[:].rearrange("q a (b m t) -> q (a b) t m", b=H_PASSES, t=PACK),
         )
-        picked_scales = place("picked_scales", [P, K_PASSES * S], U8, AT_PICKED_SCALES)
         for a in range(K_PASSES):
-            nc.vector.tensor_copy(picked_scales[:, S * a : S * (a + 1)], tab_scale_sb[:, a, :].indirect(listed[:]))
-        nc.vector.tensor_copy(scales1[:, : K_PASSES * S].bitcast(I32), picked_scales[:].bitcast(I32))
+            nc.vector.tensor_copy(v_scale[a].bitcast(I32), picked_scales[:].bitcast(I32))
         for row in range(1, SCALE_ROWS):
             nc.scalar.dma_start(
-                scales1[row:P:QUADRANT, :].bitcast(I32), scales1[SPREAD * row : P : QUADRANT, :].bitcast(I32)
+                scales1[row:P:QUADRANT, : 3 * S].bitcast(I32), scales1[SPREAD * row : P : QUADRANT, : 3 * S].bitcast(I32)
+            )
+        for row in range(SCALE_ROWS):
+            nc.scalar.dma_start(
+                scales1[row:P:QUADRANT, 3 * S :].bitcast(I32),
+                scales1[SPREAD * row + SCALE_ROWS : P : QUADRANT, 3 * S :].bitcast(I32),
             )
 
         w4_sb = place("w4_sb", [P, K_PASSES, 2 * H], U8, AT_W4)
@@ -137,7 +150,7 @@ def tile_list_audiobook_banner_scores_kernel(
             v_codes.append(codes)
 
         def load_shelf(i):
-            rows = place("shelf%d" % (i % 2), [P, T2], F32, AT_SHELF[i % 2])
+            rows = place("shelf%d" % i, [P, T2], F32, AT_SHELF[i % SHELVES])
             by_tile = shelf.rearrange("(b q t) c -> b t q c", b=H_PASSES, t=PACK)
             nc.sync.dma_start(rows[:], by_tile[i // PACK, i % PACK])
             return rows
@@ -153,7 +166,7 @@ def tile_list_audiobook_banner_scores_kernel(
         z_rows.extend(z45[:, T2 * t : T2 * (t + 1)] for t in range(2))
         z_rows.append(z6[:])
 
-        factor0 = place("factor0", [P, BANK], F32, AT_W2_RAW)
+        factor0 = place("factor0", [P, BANK], F32, AT_WGO)
         hosts = {0: z_rows[6], 1: z_rows[5], LAST: z_rows[5]}
         for j in range(2, LAST):
             hosts[j] = z_rows[j - 2]
@@ -171,26 +184,27 @@ def tile_list_audiobook_banner_scores_kernel(
             b, t = divmod(i, PACK)
             cols = slice(BANK * h, BANK * (h + 1))
             acc = psum.tile([P, BANK], F32, name="acc", tag="bank")
-            for a in range(K_PASSES):
+            for a in reversed(range(K_PASSES)):
                 nc.tensor.matmul_mx(
                     out=acc[:],
                     lhsT=w4_sb[:, a, 2 * P * i : 2 * P * (i + 1)].bitcast(FP4X4),
                     lhsT_scale=w4_scale[a][:, P * i : P * (i + 1)],
                     rhs=v_codes[a][:, cols].bitcast(FP8X4),
                     rhs_scale=v_scale[a][:, cols],
-                    start=(a == 0),
-                    stop=(a == K_PASSES - 1),
+                    start=(a == K_PASSES - 1),
+                    stop=(a == 0),
                 )
             factor = factor_of(u)
-            nc.scalar.activation(factor, acc[:], ACT.Square)
-            nc.scalar.activation(factor, factor, ACT.Identity, bias=1.0, scale=cub_sb[:, b, t : t + 1])
+            square = place("square0", [P, BANK], F32, AT_Z6 - 1)[:] if u == 0 else factor
+            nc.scalar.activation(square, acc[:], ACT.Square)
+            nc.scalar.activation(factor, square, ACT.Identity, bias=1.0, scale=cub_sb[:, b, t : t + 1])
             banks[u] = acc
 
         gains = {}
 
         def couple(j):
             halves = [u for u in (2 * j + 1, 2 * j + 2) if u < HALVES]
-            gain = place("gain%d" % (j % 2), [P, S], F32, AT_GAIN[j % 2])
+            gain = place("gain%d" % j, [P, S], F32, AT_GAIN[j])
             first = BANK * halves[0] % (PACK * S)
             whole = j > 0 and len(halves) == 2 and first + S <= PACK * S
             for u in halves:
@@ -234,21 +248,26 @@ def tile_list_audiobook_banner_scores_kernel(
         couple(1)
         features(0)
         shelve(0, 0, BANK)
-        w2_raw = place("w2_raw", [P, H_PASSES, PACK * N], F32, AT_W2_RAW)
-        nc.sync.dma_start(w2_raw[:], w2.rearrange("(b q t) n -> q b (t n)", b=H_PASSES, t=PACK))
+        wgo_sb = place("wgo_sb", [P, PICKS], F32, AT_WGO)
+        nc.sync.dma_start(wgo_sb[:], wgo)
         banners = []
-        w2_grouped = z_grouped = pairs = wgo_sb = None
+        w2_grouped = z_grouped = pairs = w2_raw = None
         for i in range(ROW_TILES):
             page = pages[i % PAGES]
             for u in (2 * i + 1, 2 * i + 2):
                 if u < HALVES:
                     features(u)
+            if i < 2:
+                shelf_sb[i + 2] = load_shelf(i + 2)
+            elif i == 2:
+                w2_raw = place("w2_raw", [P, H_PASSES, PACK * N], F32, AT_W2_RAW)
+                nc.sync.dma_start(w2_raw[:], w2.rearrange("(b q t) n -> q b (t n)", b=H_PASSES, t=PACK))
+            elif i < LAST:
+                shelf_sb[i + 1] = load_shelf(i + 1)
             shelve(i, BANK if i == 0 else 0, S)
             if i + 2 <= LAST:
                 couple(i + 2)
             if i + 2 == LAST:
-                wgo_sb = place("wgo_sb", [P, PICKS], F32, AT_SCALES)
-                nc.sync.dma_start(wgo_sb[:], wgo)
                 w2_grouped = place("w2_grouped", [P, H_PASSES, N * PACK], BF16, AT_W2_GROUPED)
                 for b in range(H_PASSES):
                     interleave(
@@ -264,10 +283,6 @@ def tile_list_audiobook_banner_scores_kernel(
                         z_pass0[:].rearrange("q (t c) -> q t c", t=PACK)[:, :, lo : lo + BANK],
                     )
             elif i == LAST - 2:
-                for n in range(2):
-                    banner = place("banner%d" % n, [P, T2], F32, AT_BANNER[n])
-                    nc.gpsimd.memset(banner[:], 0.0)
-                    banners.append(banner)
                 pairs = [place("pairs%d" % c, [P, 2, BANK, 2], BF16, AT_PAIRS + 4 * c) for c in range(len(chunks))]
                 for c, lo in enumerate(chunks):
                     interleave(pairs[c][:, 0, :, :], z45[:].rearrange("q (t c) -> q t c", t=2)[:, :, lo : lo + BANK])
@@ -279,13 +294,15 @@ def tile_list_audiobook_banner_scores_kernel(
                     nc.scalar.copy(
                         pairs[c][:, 1, :, :], z_rows[i][:, lo : lo + BANK].unsqueeze(2).to_broadcast([P, BANK, 2])
                     )
+                for n in range(2):
+                    banner = place("banner%d" % n, [P, T2], F32, AT_BANNER[n])
+                    nc.gpsimd.memset(banner[:], 0.0)
+                    banners.append(banner)
             elif i == LAST:
                 for c, lo in enumerate(chunks):
                     nc.vector.tensor_tensor(
                         pairs[c][:, 1, :, 1], page[:, lo : lo + BANK], shelf_sb[i][:, lo : lo + BANK], MULT
                     )
-            if i + 2 <= LAST:
-                shelf_sb[i + 2] = load_shelf(i + 2)
 
         z_codes = place("z_codes", [P, H_PASSES, T2], U32, AT_Z_CODES)
         w2_codes = place("w2_codes", [P, H_PASSES, N], U32, AT_W2_CODES)

@@ -38,19 +38,19 @@ RUN = 4
 AT_TABLE = (0, 16)
 AT_SHELF = (16, 24, 32, 40)
 AT_WGS = 0
-AT_PAIRS = 0
 AT_TAB_SCALES, AT_W4_SCALES, AT_W4_RAW = 32, 36, 46
 AT_PAGE = (80, 48, 56)
 AT_PICKED_SCALES = 63.5
 AT_CODES = (64, 68)
 AT_W4, AT_SCALES = 72, 76
-AT_BANNER = (32, 80)
-AT_Z_PASS0, AT_Z45, AT_Z6 = 88, 104, 112
-AT_Z_GROUPED = 116
+AT_BANNER = (32, 132)
+AT_Z_PASS0, AT_Z45, AT_Z67 = 88, 104, 112
+AT_Z_GROUPED = 208
 AT_W2_GROUPED = 132
 AT_W2_RAW, AT_WGO = 140, 156
-AT_Y = (140, 148, 116, 124)
+AT_Y = (140, 96, 208, 216)
 AT_PLACED = (160, 164)
+AT_PLACED_LAST = 122
 AT_GAIN = (32, 40, 140, 16, 24, 32, 40, 16)
 AT_SCORE = (170, 178)
 AT_Z_CODES, AT_W2_CODES, AT_BASE = 186, 202, 206
@@ -161,15 +161,19 @@ def tile_list_audiobook_banner_scores_kernel(
 
         z_pass0 = place("z_pass0", [P, PACK * T2], BF16, AT_Z_PASS0)
         z45 = place("z45", [P, 2 * T2], BF16, AT_Z45)
-        z6 = place("z6", [P, T2], BF16, AT_Z6)
         z_rows = [z_pass0[:, T2 * t : T2 * (t + 1)] for t in range(PACK)]
         z_rows.extend(z45[:, T2 * t : T2 * (t + 1)] for t in range(2))
-        z_rows.append(z6[:])
 
         factor0 = place("factor0", [P, BANK], F32, AT_WGO)
-        hosts = {0: z_rows[6], 1: z_rows[5], LAST: z_rows[5]}
-        for j in range(2, LAST):
+        hosts = {0: place("factor1", [P, T2], BF16, AT_Z67)[:], 1: z_rows[5], LAST: z_rows[5]}
+        for j in range(2, LAST - 1):
             hosts[j] = z_rows[j - 2]
+        copies = {
+            HALVES - 3: z_rows[4].bitcast(F32)[:, :BANK],
+            HALVES - 2: z_rows[4].bitcast(F32)[:, BANK:],
+            HALVES - 1: z_rows[5].bitcast(F32)[:, BANK:],
+        }
+        placed_last = place("placed_last", [P, 2 * S], F32, AT_PLACED_LAST)
 
         def factor_of(u):
             if u == 0:
@@ -195,15 +199,19 @@ def tile_list_audiobook_banner_scores_kernel(
                     stop=(a == 0),
                 )
             factor = factor_of(u)
-            square = place("square0", [P, BANK], F32, AT_Z6 - 1)[:] if u == 0 else factor
+            square = place("square0", [P, BANK], F32, AT_Z67 - 1)[:] if u == 0 else factor
             nc.scalar.activation(square, acc[:], ACT.Square)
             nc.scalar.activation(factor, square, ACT.Identity, bias=1.0, scale=cub_sb[:, b, t : t + 1])
+            if u in copies:
+                nc.scalar.copy(copies[u], acc[:])
             banks[u] = acc
 
         gains = {}
 
         def couple(j):
             halves = [u for u in (2 * j + 1, 2 * j + 2) if u < HALVES]
+            if j == LAST - 1:
+                hosts[j] = place("factor6", [P, T2], BF16, AT_Z67)[:]
             gain = place("gain%d" % j, [P, S], F32, AT_GAIN[j])
             first = BANK * halves[0] % (PACK * S)
             whole = j > 0 and len(halves) == 2 and first + S <= PACK * S
@@ -216,13 +224,19 @@ def tile_list_audiobook_banner_scores_kernel(
                     nc.gpsimd.tensor_tensor(gains[u], factor_of(u), wgs_sb[:, at : at + BANK], MULT)
             if whole:
                 nc.gpsimd.tensor_tensor(gain[:], hosts[j].bitcast(F32), wgs_sb[:, first : first + S], MULT)
+            if j == LAST - 1:
+                nc.gpsimd.tensor_tensor(placed_last[:, BANK : BANK + S], z_rows[4].bitcast(F32), gain[:], MULT)
+            if j == LAST:
+                nc.gpsimd.tensor_tensor(placed_last[:, BANK + S :], copies[HALVES - 1], gain[:, :BANK], MULT)
 
-        placed = {}
+        placed = {LAST - 1: placed_last[:, :S], LAST: placed_last[:, S:]}
 
         def features(u):
             i, h = divmod(u, 2)
-            if h == 0:
-                placed[i] = place("placed%d" % (i % 2), [P, S], F32, AT_PLACED[i % 2])
+            if u in copies:
+                return
+            if i not in placed:
+                placed[i] = place("placed%d" % (i % 2), [P, S], F32, AT_PLACED[i % 2])[:]
             dst = placed[i][:, BANK * h : BANK * (h + 1)]
             if u == 0:
                 nc.vector.tensor_tensor(dst, banks[u][:], wgs_sb[:, :BANK], MULT)
@@ -242,6 +256,11 @@ def tile_list_audiobook_banner_scores_kernel(
         def four_to_a_column(flat):
             return flat.rearrange("q (c t) -> q c t", t=PACK)
 
+        def zeroed_banner(n):
+            banner = place("banner%d" % n, [P, T2], F32, AT_BANNER[n])
+            nc.gpsimd.memset(banner[:], 0.0)
+            return banner
+
         chunks = range(0, T2, BANK)
         product(0)
         couple(0)
@@ -251,7 +270,7 @@ def tile_list_audiobook_banner_scores_kernel(
         wgo_sb = place("wgo_sb", [P, PICKS], F32, AT_WGO)
         nc.sync.dma_start(wgo_sb[:], wgo)
         banners = []
-        w2_grouped = z_grouped = pairs = w2_raw = None
+        w2_grouped = z_grouped = grouped = z67 = w2_raw = None
         for i in range(ROW_TILES):
             page = pages[i % PAGES]
             for u in (2 * i + 1, 2 * i + 2):
@@ -283,42 +302,41 @@ def tile_list_audiobook_banner_scores_kernel(
                         z_pass0[:].rearrange("q (t c) -> q t c", t=PACK)[:, :, lo : lo + BANK],
                     )
             elif i == LAST - 2:
-                pairs = [place("pairs%d" % c, [P, 2, BANK, 2], BF16, AT_PAIRS + 4 * c) for c in range(len(chunks))]
+                grouped = [place("grouped%d" % c, [P, BANK, PACK], BF16, AT_Z_PASS0 + 4 * c) for c in range(len(chunks))]
                 for c, lo in enumerate(chunks):
-                    interleave(pairs[c][:, 0, :, :], z45[:].rearrange("q (t c) -> q t c", t=2)[:, :, lo : lo + BANK])
+                    interleave(grouped[c][:, :, 0:2], z45[:].rearrange("q (t c) -> q t c", t=2)[:, :, lo : lo + BANK])
             elif i == LAST - 1:
+                z67 = [place("z67_%d" % c, [P, 2, BANK], BF16, AT_Z67 + 2 * c) for c in range(len(chunks))]
                 for c, lo in enumerate(chunks):
-                    if c % 2 == 0:
-                        half = slice(lo, lo + 2 * BANK)
-                        nc.gpsimd.tensor_tensor(z_rows[i][:, half], page[:, half], shelf_sb[i][:, half], MULT)
-                    nc.scalar.copy(
-                        pairs[c][:, 1, :, :], z_rows[i][:, lo : lo + BANK].unsqueeze(2).to_broadcast([P, BANK, 2])
-                    )
-                for n in range(2):
-                    banner = place("banner%d" % n, [P, T2], F32, AT_BANNER[n])
-                    nc.gpsimd.memset(banner[:], 0.0)
-                    banners.append(banner)
+                    cols = slice(lo, lo + BANK)
+                    nc.gpsimd.tensor_tensor(z67[c][:, 0, :], page[:, cols], shelf_sb[i][:, cols], MULT)
+                banners.append(zeroed_banner(0))
             elif i == LAST:
                 for c, lo in enumerate(chunks):
-                    nc.vector.tensor_tensor(
-                        pairs[c][:, 1, :, 1], page[:, lo : lo + BANK], shelf_sb[i][:, lo : lo + BANK], MULT
-                    )
+                    cols = slice(lo, lo + BANK)
+                    nc.vector.tensor_tensor(z67[c][:, 1, :], page[:, cols], shelf_sb[i][:, cols], MULT)
+                    interleave(grouped[c][:, :, 2:PACK], z67[c][:])
 
         z_codes = place("z_codes", [P, H_PASSES, T2], U32, AT_Z_CODES)
-        w2_codes = place("w2_codes", [P, H_PASSES, N], U32, AT_W2_CODES)
-        scale_bytes = place("scale_bytes", [P, H_PASSES, T2 + N], U8, AT_PLACED[LAST % 2])
+        w2_first = place("w2_first", [P, H_PASSES, P], U32, AT_W2_CODES)
+        w2_rest = place("w2_rest", [P, H_PASSES, N - P], U32, AT_Z67 + 6)
+
+        def w2_codes(b, lo, hi):
+            return (w2_first[:, b, lo:hi] if hi <= P else w2_rest[:, b, lo - P : hi - P]).bitcast(FP8X4)
+
+        scale_bytes = place("scale_bytes", [P, H_PASSES, T2 + N], U8, AT_PAGE[LAST % PAGES])
         z_scale = scale_bytes[:, :, :T2]
         w2_scale = scale_bytes[:, :, T2:]
 
         def quantise_w2(lo, hi):
             for b in range(H_PASSES):
                 nc.vector.quantize_mx(
-                    out=w2_codes[:, b, lo:hi].bitcast(FP8X4),
+                    out=w2_codes(b, lo, hi),
                     scales=w2_scale[:, b, lo:hi],
                     in_=w2_grouped[:, b, PACK * lo : PACK * hi],
                 )
 
-        quantise_w2(0, N // 2)
+        quantise_w2(0, P)
         for lo in range(0, T2, 2 * BANK):
             nc.vector.quantize_mx(
                 out=z_codes[:, 0, lo : lo + 2 * BANK].bitcast(FP8X4),
@@ -326,20 +344,17 @@ def tile_list_audiobook_banner_scores_kernel(
                 in_=z_grouped[:, PACK * lo : PACK * (lo + 2 * BANK)],
             )
         for c, lo in enumerate(chunks):
-            grouped = place("grouped%d" % c, [P, BANK * PACK], BF16, AT_Z_PASS0 + 4 * c)
-            nc.scalar.copy(
-                grouped[:].bitcast(F32).rearrange("q (c h) -> q c h", h=2),
-                pairs[c][:].rearrange("q h c e -> q h (c e)").bitcast(F32).rearrange("q h c -> q c h"),
-            )
             nc.vector.quantize_mx(
-                out=z_codes[:, 1, lo : lo + BANK].bitcast(FP8X4), scales=z_scale[:, 1, lo : lo + BANK], in_=grouped[:]
+                out=z_codes[:, 1, lo : lo + BANK].bitcast(FP8X4), scales=z_scale[:, 1, lo : lo + BANK], in_=grouped[c][:].rearrange("q c t -> q (c t)")
             )
-        quantise_w2(N // 2, N)
+        quantise_w2(P, 2 * P)
+        quantise_w2(2 * P, N)
+        banners.append(zeroed_banner(1))
 
         def second_pass(acc, n, b, lo):
             nc.tensor.matmul_mx(
                 out=acc[:],
-                lhsT=w2_codes[:, b, P * n : P * (n + 1)].bitcast(FP8X4),
+                lhsT=w2_codes(b, P * n, P * (n + 1)),
                 lhsT_scale=w2_scale[:, b, P * n : P * (n + 1)],
                 rhs=z_codes[:, b, lo : lo + BANK].bitcast(FP8X4),
                 rhs_scale=z_scale[:, b, lo : lo + BANK],

@@ -83,9 +83,10 @@ def tile_list_audiobook_banner_scores_kernel(
 
         listed = load_list("listed", offs)
         shelved = load_list("shelved", offs2)
+        promoted = load_list("promoted", offs3)
+        banner_slots = load_list("banner_slots", offs4)
         w4_raw = place("w4_raw", [P, K_PASSES, 2 * H], U8, AT_W4_RAW)
         nc.sync.dma_start(w4_raw[:].bitcast(I32), w4_words.rearrange("a q n -> q a n").bitcast(I32))
-        promoted = load_list("promoted", offs3)
         tab_scale_sb = place("tab_scale_sb", [P, T], U8, AT_TAB_SCALES)
         nc.vector.memset(tab_scale_sb[:].bitcast(I32), 0)
         for a in range(K_PASSES):
@@ -95,9 +96,7 @@ def tile_list_audiobook_banner_scores_kernel(
         nc.sync.dma_start(
             w4_scale_raw[0:P:SPREAD, :, :].bitcast(I32), w4_scales.rearrange("a r n -> r a n").bitcast(I32)
         )
-        tab_sb = [load_table(0)]
-        banner_slots = load_list("banner_slots", offs4)
-        tab_sb.append(load_table(1))
+        tab_sb = [load_table(a) for a in range(K_PASSES)]
 
         cub_sb = place("cub_sb", [P, H_PASSES, PACK], F32, AT_W2_GROUPED)
         nc.gpsimd.dma_start(cub_sb[:], cub.rearrange("(b q t) -> q b t", b=H_PASSES, t=PACK))
@@ -188,15 +187,16 @@ def tile_list_audiobook_banner_scores_kernel(
             b, t = divmod(i, PACK)
             cols = slice(BANK * h, BANK * (h + 1))
             acc = psum.tile([P, BANK], F32, name="acc", tag="bank")
-            for a in reversed(range(K_PASSES)):
+            order = (0, 1) if u == 0 else (1, 0)
+            for a in order:
                 nc.tensor.matmul_mx(
                     out=acc[:],
                     lhsT=w4_sb[:, a, 2 * P * i : 2 * P * (i + 1)].bitcast(FP4X4),
                     lhsT_scale=w4_scale[a][:, P * i : P * (i + 1)],
                     rhs=v_codes[a][:, cols].bitcast(FP8X4),
                     rhs_scale=v_scale[a][:, cols],
-                    start=(a == K_PASSES - 1),
-                    stop=(a == 0),
+                    start=(a == order[0]),
+                    stop=(a == order[1]),
                 )
             factor = factor_of(u)
             square = place("square0", [P, BANK], F32, AT_Z67 - 1)[:] if u == 0 else factor

@@ -35,25 +35,25 @@ PAGES = 3
 SHELVES = 4
 RUN = 4
 
-AT_TABLE = (0, 16)
+AT_TABLE = (132, 16)
 AT_SHELF = (16, 24, 32, 40)
-AT_WGS = 0
+AT_CUB, AT_WGS = 150, 132
 AT_TAB_SCALES, AT_W4_SCALES, AT_W4_RAW = 32, 36, 46
 AT_PAGE = (80, 48, 56)
 AT_PICKED_SCALES = 63.5
 AT_CODES = (64, 68)
 AT_W4, AT_SCALES = 72, 76
-AT_BANNER = (32, 132)
+AT_BANNER = (32, 72)
 AT_Z_PASS0, AT_Z45, AT_Z67 = 88, 104, 112
 AT_Z_GROUPED = 208
-AT_W2_GROUPED = 132
-AT_W2_RAW, AT_WGO = 140, 156
-AT_Y = (140, 96, 208, 216)
+AT_W2_GROUPED = 72
+AT_W2_RAW, AT_WGO = 0, 156
+AT_Y = (0, 96, 208, 216)
 AT_PLACED = (160, 164)
 AT_PLACED_LAST = 122
-AT_GAIN = (32, 40, 140, 16, 24, 32, 40, 16)
-AT_SCORE = (170, 178)
-AT_Z_CODES, AT_W2_CODES, AT_BASE = 186, 202, 206
+AT_GAIN = (32, 40, 0, 16, 24, 32, 40, 16)
+AT_SCORE = (170, 178, 160, 122)
+AT_Z_CODES, AT_W2_CODES, AT_BASE = 186, 202, 155.5
 
 
 def tile_list_audiobook_banner_scores_kernel(
@@ -85,6 +85,8 @@ def tile_list_audiobook_banner_scores_kernel(
         shelved = load_list("shelved", offs2)
         promoted = load_list("promoted", offs3)
         banner_slots = load_list("banner_slots", offs4)
+        cub_sb = place("cub_sb", [P, H_PASSES, PACK], F32, AT_CUB)
+        nc.sync.dma_start(cub_sb[:], cub.rearrange("(b q t) -> q b t", b=H_PASSES, t=PACK))
         w4_raw = place("w4_raw", [P, K_PASSES, 2 * H], U8, AT_W4_RAW)
         nc.sync.dma_start(w4_raw[:].bitcast(I32), w4_words.rearrange("a q n -> q a n").bitcast(I32))
         tab_scale_sb = place("tab_scale_sb", [P, T], U8, AT_TAB_SCALES)
@@ -97,12 +99,6 @@ def tile_list_audiobook_banner_scores_kernel(
             w4_scale_raw[0:P:SPREAD, :, :].bitcast(I32), w4_scales.rearrange("a r n -> r a n").bitcast(I32)
         )
         tab_sb = [load_table(a) for a in range(K_PASSES)]
-
-        cub_sb = place("cub_sb", [P, H_PASSES, PACK], F32, AT_W2_GROUPED)
-        nc.gpsimd.dma_start(cub_sb[:], cub.rearrange("(b q t) -> q b t", b=H_PASSES, t=PACK))
-        base_sb = place("base_sb", [P, N_TILES], F32, AT_BASE)
-        with nc.allow_non_contiguous_dma(reason="one bias value a partition"):
-            nc.gpsimd.dma_start(base_sb[:], base.rearrange("(c q) -> q c", q=P))
 
         pages = [place("page%d" % i, [P, T2], F32, AT_PAGE[i]) for i in range(PAGES)]
         nc.vector.memset(pages[0][:], 0.0)
@@ -163,7 +159,7 @@ def tile_list_audiobook_banner_scores_kernel(
         z_rows = [z_pass0[:, T2 * t : T2 * (t + 1)] for t in range(PACK)]
         z_rows.extend(z45[:, T2 * t : T2 * (t + 1)] for t in range(2))
 
-        factor0 = place("factor0", [P, BANK], F32, AT_WGO)
+        factor0 = place("factor0", [P, BANK], F32, AT_BASE)
         hosts = {0: place("factor1", [P, T2], BF16, AT_Z67)[:], 1: z_rows[5], LAST: z_rows[5]}
         for j in range(2, LAST - 1):
             hosts[j] = z_rows[j - 2]
@@ -267,6 +263,9 @@ def tile_list_audiobook_banner_scores_kernel(
         couple(1)
         features(0)
         shelve(0, 0, BANK)
+        base_sb = place("base_sb", [P, N_TILES], F32, AT_BASE)
+        with nc.allow_non_contiguous_dma(reason="one bias value a partition"):
+            nc.sync.dma_start(base_sb[:], base.rearrange("(c q) -> q c", q=P))
         wgo_sb = place("wgo_sb", [P, PICKS], F32, AT_WGO)
         nc.sync.dma_start(wgo_sb[:], wgo)
         banners = []
@@ -370,7 +369,7 @@ def tile_list_audiobook_banner_scores_kernel(
                     second_pass(acc, n, b, lo)
             for acc, lo in zip(accs, chunks):
                 nc.scalar.copy(y[:, lo : lo + BANK], acc[:])
-            both = place("both%d" % (n % 2), [P, 2 * PICKS], F32, AT_SCORE[n % 2])
+            both = place("both%d" % n, [P, 2 * PICKS], F32, AT_SCORE[n])
             nc.vector.tensor_copy(both[:, :PICKS], y[:].indirect(promoted[:]))
             return both
 

@@ -35,10 +35,11 @@ PAGES = 3
 SHELVES = 4
 RUN = 4
 
-AT_TABLE = (132, 16)
+AT_TABLE = (132, 15.9375)
+AT_W4_LOW = 14.5
 AT_SHELF = (16, 24, 32, 40)
-AT_CUB, AT_WGS = 150, 132
-AT_TAB_SCALES, AT_W4_SCALES, AT_W4_RAW = 32, 36, 46
+AT_CUB, AT_WGS, AT_WGS_FIRST = 150, 132, 151
+AT_TAB_SCALES, AT_W4_SCALES, AT_W4_RAW = 151, 47, 36
 AT_PAGE = (80, 48, 56)
 AT_PICKED_SCALES = 63.5
 AT_CODES = (64, 68)
@@ -98,6 +99,12 @@ def tile_list_audiobook_banner_scores_kernel(
         nc.sync.dma_start(
             w4_scale_raw[0:P:SPREAD, :, :].bitcast(I32), w4_scales.rearrange("a r n -> r a n").bitcast(I32)
         )
+        wgs_rows = wgs.rearrange("(q t) j -> q (t j)", t=PACK)
+
+        def load_wgs(queue, tile, cols):
+            for quadrant in (0, 2, 1, 3):
+                queue.dma_start(tile[QUADRANT * quadrant : QUADRANT * (quadrant + 1), cols], wgs_rows[:, cols])
+
         tab_sb = [load_table(a) for a in range(K_PASSES)]
 
         pages = [place("page%d" % i, [P, T2], F32, AT_PAGE[i]) for i in range(PAGES)]
@@ -108,6 +115,8 @@ def tile_list_audiobook_banner_scores_kernel(
         v_scale = [scales1[:, S * (K_PASSES + a) : S * (K_PASSES + a + 1)] for a in range(K_PASSES)]
         picked_scales = place("picked_scales", [P, S], U8, AT_PICKED_SCALES)
         nc.vector.tensor_copy(picked_scales[:], tab_scale_sb[:].indirect(listed[:]))
+        wgs_first = place("wgs_first", [P, BANK], F32, AT_WGS_FIRST)
+        load_wgs(nc.gpsimd, wgs_first, slice(0, BANK))
         nc.vector.tensor_copy(
             scales1[:, : K_PASSES * S].rearrange("q (g t m) -> q g t m", t=PACK, m=P),
             w4_scale_raw[:].rearrange("q a (b m t) -> q (a b) t m", b=H_PASSES, t=PACK),
@@ -124,17 +133,18 @@ def tile_list_audiobook_banner_scores_kernel(
                 scales1[SPREAD * row + SCALE_ROWS : P : QUADRANT, 3 * S :].bitcast(I32),
             )
 
-        w4_sb = place("w4_sb", [P, K_PASSES, 2 * H], U8, AT_W4)
-        nc.vector.tensor_copy(
-            w4_sb[:].bitcast(U16).rearrange("q a (b t m) -> q (a b) t m", b=H_PASSES, t=PACK),
-            w4_raw[:].bitcast(U16).rearrange("q a (b m t) -> q (a b) t m", b=H_PASSES, t=PACK),
-        )
+        def deal(dst, b, slots):
+            words = w4_raw[:].bitcast(U16).rearrange("q a (b m t) -> q a b t m", b=H_PASSES, t=PACK)
+            nc.vector.tensor_copy(dst.bitcast(U16).rearrange("q a (t m) -> q a t m", m=P), words[:, :, b, slots, :])
+
+        w4_first = place("w4_first", [P, K_PASSES, 2 * P], U8, AT_W4)
+        deal(w4_first[:], 0, slice(0, 1))
+        w4_high = place("w4_high", [P, K_PASSES, 2 * P * PACK], U8, AT_W4 + 1)
+        deal(w4_high[:], 1, slice(0, PACK))
 
         wgs_sb = place("wgs_sb", [P, PACK * S], F32, AT_WGS)
-        wgs_rows = wgs.rearrange("(q t) j -> q (t j)", t=PACK)
-        for cols in (slice(0, S), slice(S, PACK * S)):
-            for quadrant in (0, 2, 1, 3):
-                nc.sync.dma_start(wgs_sb[QUADRANT * quadrant : QUADRANT * (quadrant + 1), cols], wgs_rows[:, cols])
+        load_wgs(nc.sync, wgs_sb, slice(BANK, 2 * S))
+        load_wgs(nc.sync, wgs_sb, slice(2 * S, PACK * S))
 
         v_codes = []
         for a in range(K_PASSES):
@@ -144,13 +154,18 @@ def tile_list_audiobook_banner_scores_kernel(
                 nc.vector.tensor_copy(codes[:, lo : lo + width], tab_sb[a][:].indirect(part(listed, lo, lo + width)))
             v_codes.append(codes)
 
+        w4_low = place("w4_low", [P, K_PASSES, 2 * P * (PACK - 1)], U8, AT_W4_LOW)
+
+        def w4_columns(a, i):
+            tile, at = (w4_first, 0) if i == 0 else (w4_low, i - 1) if i < PACK else (w4_high, i - PACK)
+            return tile[:, a, 2 * P * at : 2 * P * (at + 1)].bitcast(FP4X4)
+
         def load_shelf(i):
             rows = place("shelf%d" % i, [P, T2], F32, AT_SHELF[i % SHELVES])
             by_tile = shelf.rearrange("(b q t) c -> b t q c", b=H_PASSES, t=PACK)
             nc.sync.dma_start(rows[:], by_tile[i // PACK, i % PACK])
             return rows
 
-        shelf_sb = {i: load_shelf(i) for i in range(2)}
         for page in pages[1:]:
             nc.gpsimd.memset(page[:], 0.0)
 
@@ -159,7 +174,7 @@ def tile_list_audiobook_banner_scores_kernel(
         z_rows = [z_pass0[:, T2 * t : T2 * (t + 1)] for t in range(PACK)]
         z_rows.extend(z45[:, T2 * t : T2 * (t + 1)] for t in range(2))
 
-        factor0 = place("factor0", [P, BANK], F32, AT_BASE)
+        factor0 = place("factor0", [P, BANK], F32, AT_SHELF[1] - 1)
         hosts = {0: place("factor1", [P, T2], BF16, AT_Z67)[:], 1: z_rows[5], LAST: z_rows[5]}
         for j in range(2, LAST - 1):
             hosts[j] = z_rows[j - 2]
@@ -187,7 +202,7 @@ def tile_list_audiobook_banner_scores_kernel(
             for a in order:
                 nc.tensor.matmul_mx(
                     out=acc[:],
-                    lhsT=w4_sb[:, a, 2 * P * i : 2 * P * (i + 1)].bitcast(FP4X4),
+                    lhsT=w4_columns(a, i),
                     lhsT_scale=w4_scale[a][:, P * i : P * (i + 1)],
                     rhs=v_codes[a][:, cols].bitcast(FP8X4),
                     rhs_scale=v_scale[a][:, cols],
@@ -195,7 +210,7 @@ def tile_list_audiobook_banner_scores_kernel(
                     stop=(a == order[1]),
                 )
             factor = factor_of(u)
-            square = place("square0", [P, BANK], F32, AT_Z67 - 1)[:] if u == 0 else factor
+            square = place("square0", [P, BANK], F32, AT_BASE)[:] if u == 0 else factor
             nc.scalar.activation(square, acc[:], ACT.Square)
             nc.scalar.activation(factor, square, ACT.Identity, bias=1.0, scale=cub_sb[:, b, t : t + 1])
             if u in copies:
@@ -217,7 +232,7 @@ def tile_list_audiobook_banner_scores_kernel(
                 gains[u] = gain[:, BANK * e : BANK * (e + 1)]
                 if not whole:
                     at = BANK * u % (PACK * S)
-                    nc.gpsimd.tensor_tensor(gains[u], factor_of(u), wgs_sb[:, at : at + BANK], MULT)
+                    nc.gpsimd.tensor_tensor(gains[u], factor_of(u), (wgs_sb if at else wgs_first)[:, at : at + BANK], MULT)
             if whole:
                 nc.gpsimd.tensor_tensor(gain[:], hosts[j].bitcast(F32), wgs_sb[:, first : first + S], MULT)
             if j == LAST - 1:
@@ -235,7 +250,7 @@ def tile_list_audiobook_banner_scores_kernel(
                 placed[i] = place("placed%d" % (i % 2), [P, S], F32, AT_PLACED[i % 2])[:]
             dst = placed[i][:, BANK * h : BANK * (h + 1)]
             if u == 0:
-                nc.vector.tensor_tensor(dst, banks[u][:], wgs_sb[:, :BANK], MULT)
+                nc.vector.tensor_tensor(dst, banks[u][:], wgs_first[:], MULT)
                 nc.vector.tensor_tensor(dst, dst, factor0[:], MULT)
             else:
                 nc.vector.tensor_tensor(dst, banks[u][:], gains[u], MULT)
@@ -259,9 +274,11 @@ def tile_list_audiobook_banner_scores_kernel(
 
         chunks = range(0, T2, BANK)
         product(0)
+        deal(w4_low[:], 0, slice(1, PACK))
         couple(0)
         couple(1)
         features(0)
+        shelf_sb = {i: load_shelf(i) for i in range(2)}
         shelve(0, 0, BANK)
         base_sb = place("base_sb", [P, N_TILES], F32, AT_BASE)
         with nc.allow_non_contiguous_dma(reason="one bias value a partition"):

@@ -52,7 +52,8 @@ AT_W2_RAW, AT_WGO = 0, 156
 AT_Y = (0, 96, 208, 216)
 AT_PLACED = (160, 164)
 AT_PLACED_LAST = 122
-AT_GAIN = (32, 40, 0, 16, 24, 32, 40, 16)
+AT_SQUARE = 130
+AT_GAIN = (154, 40, 0, 16, 24, 32, 40, 16)
 AT_SCORE = (170, 178, 160, 122)
 AT_Z_CODES, AT_W2_CODES, AT_BASE = 186, 202, 155.5
 
@@ -143,8 +144,8 @@ def tile_list_audiobook_banner_scores_kernel(
         deal(w4_high[:], 1, slice(0, PACK))
 
         wgs_sb = place("wgs_sb", [P, PACK * S], F32, AT_WGS)
-        load_wgs(nc.sync, wgs_sb, slice(BANK, 2 * S))
-        load_wgs(nc.sync, wgs_sb, slice(2 * S, PACK * S))
+        for lo in range(BANK, BANK + 3 * S, S):
+            load_wgs(nc.sync, wgs_sb, slice(lo, lo + S if lo < BANK + 2 * S else PACK * S))
 
         v_codes = []
         for a in range(K_PASSES):
@@ -175,7 +176,7 @@ def tile_list_audiobook_banner_scores_kernel(
         z_rows.extend(z45[:, T2 * t : T2 * (t + 1)] for t in range(2))
 
         factor0 = place("factor0", [P, BANK], F32, AT_SHELF[1] - 1)
-        hosts = {0: place("factor1", [P, T2], BF16, AT_Z67)[:], 1: z_rows[5], LAST: z_rows[5]}
+        hosts = {0: place("factor1", [P, T2], BF16, AT_SHELF[2])[:], 1: z_rows[5], LAST: z_rows[5]}
         for j in range(2, LAST - 1):
             hosts[j] = z_rows[j - 2]
         copies = {
@@ -210,7 +211,7 @@ def tile_list_audiobook_banner_scores_kernel(
                     stop=(a == order[1]),
                 )
             factor = factor_of(u)
-            square = place("square0", [P, BANK], F32, AT_BASE)[:] if u == 0 else factor
+            square = place("square0", [P, BANK], F32, AT_SQUARE)[:] if u == 0 else factor
             nc.scalar.activation(square, acc[:], ACT.Square)
             nc.scalar.activation(factor, square, ACT.Identity, bias=1.0, scale=cub_sb[:, b, t : t + 1])
             if u in copies:
@@ -273,6 +274,8 @@ def tile_list_audiobook_banner_scores_kernel(
             return banner
 
         chunks = range(0, T2, BANK)
+        cuts = (0, BANK, 2 * BANK, 3 * BANK, T2 - BANK // 2, T2)
+        pieces = list(zip(cuts, cuts[1:]))
         product(0)
         deal(w4_low[:], 0, slice(1, PACK))
         couple(0)
@@ -280,13 +283,8 @@ def tile_list_audiobook_banner_scores_kernel(
         features(0)
         shelf_sb = {i: load_shelf(i) for i in range(2)}
         shelve(0, 0, BANK)
-        base_sb = place("base_sb", [P, N_TILES], F32, AT_BASE)
-        with nc.allow_non_contiguous_dma(reason="one bias value a partition"):
-            nc.sync.dma_start(base_sb[:], base.rearrange("(c q) -> q c", q=P))
-        wgo_sb = place("wgo_sb", [P, PICKS], F32, AT_WGO)
-        nc.sync.dma_start(wgo_sb[:], wgo)
         banners = []
-        w2_grouped = z_grouped = grouped = z67 = w2_raw = None
+        w2_grouped = z_grouped = grouped = z67 = w2_raw = base_sb = wgo_sb = None
         for i in range(ROW_TILES):
             page = pages[i % PAGES]
             for u in (2 * i + 1, 2 * i + 2):
@@ -294,6 +292,12 @@ def tile_list_audiobook_banner_scores_kernel(
                     features(u)
             if i < 2:
                 shelf_sb[i + 2] = load_shelf(i + 2)
+                if i == 0:
+                    base_sb = place("base_sb", [P, N_TILES], F32, AT_BASE)
+                    with nc.allow_non_contiguous_dma(reason="one bias value a partition"):
+                        nc.sync.dma_start(base_sb[:], base.rearrange("(c q) -> q c", q=P))
+                    wgo_sb = place("wgo_sb", [P, PICKS], F32, AT_WGO)
+                    nc.sync.dma_start(wgo_sb[:], wgo)
             elif i == 2:
                 w2_raw = place("w2_raw", [P, H_PASSES, PACK * N], F32, AT_W2_RAW)
                 nc.sync.dma_start(w2_raw[:], w2.rearrange("(b q t) n -> q b (t n)", b=H_PASSES, t=PACK))
@@ -318,9 +322,11 @@ def tile_list_audiobook_banner_scores_kernel(
                         z_pass0[:].rearrange("q (t c) -> q t c", t=PACK)[:, :, lo : lo + BANK],
                     )
             elif i == LAST - 2:
-                grouped = [place("grouped%d" % c, [P, BANK, PACK], BF16, AT_Z_PASS0 + 4 * c) for c in range(len(chunks))]
-                for c, lo in enumerate(chunks):
-                    interleave(grouped[c][:, :, 0:2], z45[:].rearrange("q (t c) -> q t c", t=2)[:, :, lo : lo + BANK])
+                grouped = {
+                    lo: place("grouped%d" % lo, [P, hi - lo, PACK], BF16, AT_Z_PASS0 + lo // P) for lo, hi in pieces
+                }
+                for lo, hi in pieces:
+                    interleave(grouped[lo][:, :, 0:2], z45[:].rearrange("q (t c) -> q t c", t=2)[:, :, lo:hi])
             elif i == LAST - 1:
                 z67 = [place("z67_%d" % c, [P, 2, BANK], BF16, AT_Z67 + 2 * c) for c in range(len(chunks))]
                 for c, lo in enumerate(chunks):
@@ -331,7 +337,9 @@ def tile_list_audiobook_banner_scores_kernel(
                 for c, lo in enumerate(chunks):
                     cols = slice(lo, lo + BANK)
                     nc.vector.tensor_tensor(z67[c][:, 1, :], page[:, cols], shelf_sb[i][:, cols], MULT)
-                    interleave(grouped[c][:, :, 2:PACK], z67[c][:])
+                    for at, hi in pieces:
+                        if lo <= at < lo + BANK:
+                            interleave(grouped[at][:, :, 2:PACK], z67[c][:, :, at - lo : hi - lo])
 
         z_codes = place("z_codes", [P, H_PASSES, T2], U32, AT_Z_CODES)
         w2_first = place("w2_first", [P, H_PASSES, P], U32, AT_W2_CODES)
@@ -359,43 +367,68 @@ def tile_list_audiobook_banner_scores_kernel(
                 scales=z_scale[:, 0, lo : lo + 2 * BANK],
                 in_=z_grouped[:, PACK * lo : PACK * (lo + 2 * BANK)],
             )
-        for c, lo in enumerate(chunks):
-            nc.vector.quantize_mx(
-                out=z_codes[:, 1, lo : lo + BANK].bitcast(FP8X4), scales=z_scale[:, 1, lo : lo + BANK], in_=grouped[c][:].rearrange("q c t -> q (c t)")
+
+        def second_pass(acc, n, b, lo, hi):
+            nc.tensor.matmul_mx(
+                out=acc[:, lo % BANK : lo % BANK + hi - lo],
+                lhsT=w2_codes(b, P * n, P * (n + 1)),
+                lhsT_scale=w2_scale[:, b, P * n : P * (n + 1)],
+                rhs=z_codes[:, b, lo:hi].bitcast(FP8X4),
+                rhs_scale=z_scale[:, b, lo:hi],
+                start=(b == 0),
+                stop=(b == H_PASSES - 1 and hi % BANK == 0),
             )
+
+        y_first = place("y0", [P, T2], F32, AT_Y[0])
+        accs_first = [psum.tile([P, BANK], F32, name="acc", tag="bank") for lo in chunks]
+        for acc, lo in zip(accs_first, chunks):
+            second_pass(acc, 0, 0, lo, lo + BANK)
+        for lo, hi in pieces:
+            nc.vector.quantize_mx(
+                out=z_codes[:, 1, lo:hi].bitcast(FP8X4),
+                scales=z_scale[:, 1, lo:hi],
+                in_=grouped[lo][:].rearrange("q c t -> q (c t)"),
+            )
+            second_pass(accs_first[lo // BANK], 0, 1, lo, hi)
         quantise_w2(P, 2 * P)
         quantise_w2(2 * P, N)
         banners.append(zeroed_banner(1))
 
-        def second_pass(acc, n, b, lo):
-            nc.tensor.matmul_mx(
-                out=acc[:],
-                lhsT=w2_codes(b, P * n, P * (n + 1)),
-                lhsT_scale=w2_scale[:, b, P * n : P * (n + 1)],
-                rhs=z_codes[:, b, lo : lo + BANK].bitcast(FP8X4),
-                rhs_scale=z_scale[:, b, lo : lo + BANK],
-                start=(b == 0),
-                stop=(b == H_PASSES - 1),
-            )
-
         def second_product(n):
-            y = place("y%d" % n, [P, T2], F32, AT_Y[n])
-            accs = [psum.tile([P, BANK], F32, name="acc", tag="bank") for lo in chunks]
-            for b in range(H_PASSES):
-                for acc, lo in zip(accs, chunks):
-                    second_pass(acc, n, b, lo)
+            if n == 0:
+                y, accs = y_first, accs_first
+            else:
+                y = place("y%d" % n, [P, T2], F32, AT_Y[n])
+                accs = [psum.tile([P, BANK], F32, name="acc", tag="bank") for lo in chunks]
+                for b in range(H_PASSES):
+                    for acc, lo in zip(accs, chunks):
+                        second_pass(acc, n, b, lo, lo + BANK)
             for acc, lo in zip(accs, chunks):
                 nc.scalar.copy(y[:, lo : lo + BANK], acc[:])
-            both = place("both%d" % n, [P, 2 * PICKS], F32, AT_SCORE[n])
-            nc.vector.tensor_copy(both[:, :PICKS], y[:].indirect(promoted[:]))
-            return both
+            return y
 
-        picked_next = second_product(0)
-        for n in range(N_TILES):
-            both = picked_next
+        def pick(n, y, lo, hi):
+            nc.vector.tensor_copy(both[n][:, lo:hi], y[:].indirect(part(promoted, lo, hi)))
+
+        def show(n, lo, hi):
+            score = both[n][:, PICKS + lo : PICKS + hi]
+            nc.scalar.activation(score, both[n][:, lo:hi], ACT.Sigmoid, bias=base_sb[:, n : n + 1])
+            nc.vector.tensor_tensor(banners[n % 2][:].indirect(part(banner_slots, lo, hi)), score, wgo_sb[:, lo:hi], MULT)
+            if hi == PICKS:
+                nc.sync.dma_start(out[P * n : P * (n + 1), :], banners[n % 2][:])
+
+        def picked(n, width):
+            y = second_product(n)
+            both[n] = place("both%d" % n, [P, 2 * PICKS], F32, AT_SCORE[n])
+            for lo in range(0, PICKS, width):
+                pick(n, y, lo, lo + width)
+
+        both = {}
+        picked(0, PICKS // 2)
+        show(0, 0, PICKS // 2)
+        picked(1, PICKS)
+        show(0, PICKS // 2, PICKS)
+        for n in range(1, N_TILES):
             if n + 1 < N_TILES:
-                picked_next = second_product(n + 1)
-            nc.scalar.activation(both[:, PICKS:], both[:, :PICKS], ACT.Sigmoid, bias=base_sb[:, n : n + 1])
-            banner = banners[n % 2]
-            nc.vector.tensor_tensor(banner[:].indirect(banner_slots[:]), both[:, PICKS:], wgo_sb[:], MULT)
-            nc.sync.dma_start(out[P * n : P * (n + 1), :], banner[:])
+                picked(n + 1, PICKS)
+            show(n, 0, PICKS)

@@ -52,6 +52,7 @@ AT_W2_RAW, AT_WGO = 0, 156
 AT_Y = (0, 96, 208, 216)
 AT_PLACED = (160, 164)
 AT_PLACED_LAST = 122
+AT_Z_SCALE, AT_W2_SCALE = (40, 224), 42
 AT_SQUARE = 130
 AT_GAIN = (154, 40, 0, 16, 24, 32, 40, 16)
 AT_SCORE = (170, 178, 160, 122)
@@ -161,10 +162,11 @@ def tile_list_audiobook_banner_scores_kernel(
             tile, at = (w4_first, 0) if i == 0 else (w4_low, i - 1) if i < PACK else (w4_high, i - PACK)
             return tile[:, a, 2 * P * at : 2 * P * (at + 1)].bitcast(FP4X4)
 
-        def load_shelf(i):
-            rows = place("shelf%d" % i, [P, T2], F32, AT_SHELF[i % SHELVES])
+        def load_shelf(i, h=None):
+            lo, hi = (0, T2) if h is None else (S * h, S * (h + 1))
+            rows = place("shelf%d_%d" % (i, lo), [P, hi - lo], F32, AT_SHELF[i % SHELVES] + lo // 256)
             by_tile = shelf.rearrange("(b q t) c -> b t q c", b=H_PASSES, t=PACK)
-            nc.sync.dma_start(rows[:], by_tile[i // PACK, i % PACK])
+            nc.sync.dma_start(rows[:], by_tile[i // PACK, i % PACK][:, lo:hi])
             return rows
 
         for page in pages[1:]:
@@ -185,6 +187,9 @@ def tile_list_audiobook_banner_scores_kernel(
             HALVES - 1: z_rows[5].bitcast(F32)[:, BANK:],
         }
         placed_last = place("placed_last", [P, 2 * S], F32, AT_PLACED_LAST)
+
+        placed = {LAST - 1: placed_last[:, :S], LAST: placed_last[:, S:]}
+        placed[0] = place("placed0", [P, S], F32, AT_PLACED[0])[:]
 
         def factor_of(u):
             if u == 0:
@@ -241,7 +246,6 @@ def tile_list_audiobook_banner_scores_kernel(
             if j == LAST:
                 nc.gpsimd.tensor_tensor(placed_last[:, BANK + S :], copies[HALVES - 1], gain[:, :BANK], MULT)
 
-        placed = {LAST - 1: placed_last[:, :S], LAST: placed_last[:, S:]}
 
         def features(u):
             i, h = divmod(u, 2)
@@ -284,7 +288,7 @@ def tile_list_audiobook_banner_scores_kernel(
         shelf_sb = {i: load_shelf(i) for i in range(2)}
         shelve(0, 0, BANK)
         banners = []
-        w2_grouped = z_grouped = grouped = z67 = w2_raw = base_sb = wgo_sb = None
+        w2_grouped = z_grouped = grouped = z67 = w2_raw = base_sb = wgo_sb = shelf_last = None
         for i in range(ROW_TILES):
             page = pages[i % PAGES]
             for u in (2 * i + 1, 2 * i + 2):
@@ -301,16 +305,19 @@ def tile_list_audiobook_banner_scores_kernel(
             elif i == 2:
                 w2_raw = place("w2_raw", [P, H_PASSES, PACK * N], F32, AT_W2_RAW)
                 nc.sync.dma_start(w2_raw[:], w2.rearrange("(b q t) n -> q b (t n)", b=H_PASSES, t=PACK))
-            elif i < LAST:
+            elif i < LAST - 1:
                 shelf_sb[i + 1] = load_shelf(i + 1)
+            elif i == LAST - 1:
+                shelf_last = [load_shelf(LAST, h) for h in range(2)]
             shelve(i, BANK if i == 0 else 0, S)
             if i + 2 <= LAST:
                 couple(i + 2)
             if i + 2 == LAST:
-                w2_grouped = place("w2_grouped", [P, H_PASSES, N * PACK], BF16, AT_W2_GROUPED)
+                w2_grouped = place("w2_grouped", [P, N_TILES * H_PASSES * P * PACK], BF16, AT_W2_GROUPED)
                 for b in range(H_PASSES):
-                    interleave(
-                        four_to_a_column(w2_grouped[:, b, :]), w2_raw[:, b, :].rearrange("q (t n) -> q t n", t=PACK)
+                    nc.scalar.copy(
+                        w2_grouped[:].rearrange("q (n b c i t) -> q b n c t i", b=H_PASSES, n=N_TILES, i=RUN, t=PACK)[:, b],
+                        w2_raw[:, b, :].rearrange("q (t n c i) -> q n c t i", t=PACK, n=N_TILES, i=RUN),
                     )
             if i < LAST - 1:
                 nc.gpsimd.tensor_tensor(z_rows[i], page[:], shelf_sb[i][:], MULT)
@@ -333,48 +340,52 @@ def tile_list_audiobook_banner_scores_kernel(
                     cols = slice(lo, lo + BANK)
                     nc.gpsimd.tensor_tensor(z67[c][:, 0, :], page[:, cols], shelf_sb[i][:, cols], MULT)
                 banners.append(zeroed_banner(0))
-            elif i == LAST:
-                for c, lo in enumerate(chunks):
-                    cols = slice(lo, lo + BANK)
-                    nc.vector.tensor_tensor(z67[c][:, 1, :], page[:, cols], shelf_sb[i][:, cols], MULT)
-                    for at, hi in pieces:
-                        if lo <= at < lo + BANK:
-                            interleave(grouped[at][:, :, 2:PACK], z67[c][:, :, at - lo : hi - lo])
 
+        def last_product(c):
+            lo = chunks[c]
+            rows = shelf_last[lo // S][:, lo % S : lo % S + BANK]
+            nc.vector.tensor_tensor(z67[c][:, 1, :], pages[LAST % PAGES][:, lo : lo + BANK], rows, MULT)
+            for at, hi in pieces:
+                if lo <= at < lo + BANK:
+                    interleave(grouped[at][:, :, 2:PACK], z67[c][:, :, at - lo : hi - lo])
+
+        for c in range(3):
+            last_product(c)
         z_codes = place("z_codes", [P, H_PASSES, T2], U32, AT_Z_CODES)
-        w2_first = place("w2_first", [P, H_PASSES, P], U32, AT_W2_CODES)
-        w2_rest = place("w2_rest", [P, H_PASSES, N - P], U32, AT_Z67 + 6)
+        w2_first = place("w2_first", [P, H_PASSES * P], U32, AT_W2_CODES)
+        w2_rest = place("w2_rest", [P, (N_TILES - 1) * H_PASSES * P], U32, AT_Z67 + 6)
 
-        def w2_codes(b, lo, hi):
-            return (w2_first[:, b, lo:hi] if hi <= P else w2_rest[:, b, lo - P : hi - P]).bitcast(FP8X4)
+        def w2_codes(lo, hi):
+            first = H_PASSES * P
+            return (w2_first[:, lo:hi] if hi <= first else w2_rest[:, lo - first : hi - first]).bitcast(FP8X4)
 
-        scale_bytes = place("scale_bytes", [P, H_PASSES, T2 + N], U8, AT_PAGE[LAST % PAGES])
-        z_scale = scale_bytes[:, :, :T2]
-        w2_scale = scale_bytes[:, :, T2:]
+        z_scale = [place("z_scale%d" % b, [P, T2], U8, AT_Z_SCALE[b]) for b in range(H_PASSES)]
+        w2_scale = place("w2_scale", [P, H_PASSES * N], U8, AT_W2_SCALE)
 
-        def quantise_w2(lo, hi):
-            for b in range(H_PASSES):
-                nc.vector.quantize_mx(
-                    out=w2_codes(b, lo, hi),
-                    scales=w2_scale[:, b, lo:hi],
-                    in_=w2_grouped[:, b, PACK * lo : PACK * hi],
-                )
+        def quantise_w2(first, last):
+            lo, hi = H_PASSES * P * first, H_PASSES * P * last
+            nc.vector.quantize_mx(
+                out=w2_codes(lo, hi), scales=w2_scale[:, lo:hi], in_=w2_grouped[:, PACK * lo : PACK * hi]
+            )
 
-        quantise_w2(0, P)
+        quantise_w2(0, 1)
         for lo in range(0, T2, 2 * BANK):
             nc.vector.quantize_mx(
                 out=z_codes[:, 0, lo : lo + 2 * BANK].bitcast(FP8X4),
-                scales=z_scale[:, 0, lo : lo + 2 * BANK],
+                scales=z_scale[0][:, lo : lo + 2 * BANK],
                 in_=z_grouped[:, PACK * lo : PACK * (lo + 2 * BANK)],
             )
+            if lo == 0:
+                last_product(3)
 
         def second_pass(acc, n, b, lo, hi):
+            at = P * (H_PASSES * n + b)
             nc.tensor.matmul_mx(
                 out=acc[:, lo % BANK : lo % BANK + hi - lo],
-                lhsT=w2_codes(b, P * n, P * (n + 1)),
-                lhsT_scale=w2_scale[:, b, P * n : P * (n + 1)],
+                lhsT=w2_codes(at, at + P),
+                lhsT_scale=w2_scale[:, at : at + P],
                 rhs=z_codes[:, b, lo:hi].bitcast(FP8X4),
-                rhs_scale=z_scale[:, b, lo:hi],
+                rhs_scale=z_scale[b][:, lo:hi],
                 start=(b == 0),
                 stop=(b == H_PASSES - 1 and hi % BANK == 0),
             )
@@ -386,12 +397,13 @@ def tile_list_audiobook_banner_scores_kernel(
         for lo, hi in pieces:
             nc.vector.quantize_mx(
                 out=z_codes[:, 1, lo:hi].bitcast(FP8X4),
-                scales=z_scale[:, 1, lo:hi],
+                scales=z_scale[1][:, lo:hi],
                 in_=grouped[lo][:].rearrange("q c t -> q (c t)"),
             )
             second_pass(accs_first[lo // BANK], 0, 1, lo, hi)
-        quantise_w2(P, 2 * P)
-        quantise_w2(2 * P, N)
+        quantise_w2(1, 2)
+        nc.vector.tensor_copy(y_first[:, :BANK], accs_first[0][:])
+        quantise_w2(2, N_TILES)
         banners.append(zeroed_banner(1))
 
         def second_product(n):
@@ -404,7 +416,8 @@ def tile_list_audiobook_banner_scores_kernel(
                     for acc, lo in zip(accs, chunks):
                         second_pass(acc, n, b, lo, lo + BANK)
             for acc, lo in zip(accs, chunks):
-                nc.scalar.copy(y[:, lo : lo + BANK], acc[:])
+                if n > 0 or lo > 0:
+                    nc.scalar.copy(y[:, lo : lo + BANK], acc[:])
             return y
 
         def pick(n, y, lo, hi):

@@ -39,9 +39,9 @@ AT_TABLE = (132, 15.9375)
 AT_W4_LOW = 14.5
 AT_SHELF = (16, 24, 32, 40)
 AT_CUB, AT_WGS, AT_WGS_FIRST = 150, 132, 151
-AT_TAB_SCALES, AT_W4_SCALES, AT_W4_RAW = 151, 47, 36
+AT_TAB_SCALES, AT_W4_SCALES, AT_W4_RAW = 44, 151, 36
 AT_PAGE = (80, 48, 56)
-AT_PICKED_SCALES = 63.5
+AT_PICKED_SCALES = 55.5
 AT_CODES = (64, 68)
 AT_W4, AT_SCALES = 72, 76
 AT_BANNER = (32, 72)
@@ -117,14 +117,16 @@ def tile_list_audiobook_banner_scores_kernel(
         v_scale = [scales1[:, S * (K_PASSES + a) : S * (K_PASSES + a + 1)] for a in range(K_PASSES)]
         picked_scales = place("picked_scales", [P, S], U8, AT_PICKED_SCALES)
         nc.vector.tensor_copy(picked_scales[:], tab_scale_sb[:].indirect(listed[:]))
-        wgs_first = place("wgs_first", [P, BANK], F32, AT_WGS_FIRST)
-        load_wgs(nc.gpsimd, wgs_first, slice(0, BANK))
         nc.vector.tensor_copy(
             scales1[:, : K_PASSES * S].rearrange("q (g t m) -> q g t m", t=PACK, m=P),
             w4_scale_raw[:].rearrange("q a (b m t) -> q (a b) t m", b=H_PASSES, t=PACK),
         )
-        for a in range(K_PASSES):
-            nc.vector.tensor_copy(v_scale[a].bitcast(I32), picked_scales[:].bitcast(I32))
+        wgs_first = place("wgs_first", [P, BANK], F32, AT_WGS_FIRST)
+        load_wgs(nc.gpsimd, wgs_first, slice(0, BANK))
+        nc.vector.tensor_copy(
+            scales1[:, K_PASSES * S :].bitcast(I32).rearrange("q (a w) -> q a w", a=K_PASSES),
+            picked_scales[:].bitcast(I32).unsqueeze(1).to_broadcast([P, K_PASSES, S // 4]),
+        )
         for row in range(1, SCALE_ROWS):
             nc.scalar.dma_start(
                 scales1[row:P:QUADRANT, : 3 * S].bitcast(I32), scales1[SPREAD * row : P : QUADRANT, : 3 * S].bitcast(I32)
@@ -428,7 +430,11 @@ def tile_list_audiobook_banner_scores_kernel(
             nc.scalar.activation(score, both[n][:, lo:hi], ACT.Sigmoid, bias=base_sb[:, n : n + 1])
             nc.vector.tensor_tensor(banners[n % 2][:].indirect(part(banner_slots, lo, hi)), score, wgo_sb[:, lo:hi], MULT)
             if hi == PICKS:
-                nc.sync.dma_start(out[P * n : P * (n + 1), :], banners[n % 2][:])
+                queues = (nc.sync, nc.scalar) if n == N_TILES - 1 else (nc.sync,)
+                width = T2 // len(queues)
+                for k, queue in enumerate(queues):
+                    cols = slice(width * k, width * (k + 1))
+                    queue.dma_start(out[P * n : P * (n + 1), cols], banners[n % 2][:, cols])
 
         def picked(n, width):
             y = second_product(n)

@@ -94,12 +94,13 @@ def tile_list_audiobook_banner_scores_kernel(
         nc.sync.dma_start(w4_raw[:].bitcast(I32), w4_words.rearrange("a q n -> q a n").bitcast(I32))
         tab_scale_sb = place("tab_scale_sb", [P, T], U8, AT_TAB_SCALES)
         nc.vector.memset(tab_scale_sb[:].bitcast(I32), 0)
-        for a in range(K_PASSES):
-            nc.sync.dma_start(tab_scale_sb[SCALE_ROWS * a : P : SPREAD, :].bitcast(I32), tab_scales[a].bitcast(I32))
-        w4_scale_raw = place("w4_scale_raw", [P, K_PASSES, H], U8, AT_W4_SCALES)
+        nc.sync.dma_start(
+            tab_scale_sb[0:P:SCALE_ROWS, :].bitcast(I32), tab_scales.rearrange("a r n -> r a n").bitcast(I32)
+        )
+        w4_scale_raw = place("w4_scale_raw", [P, H], U8, AT_W4_SCALES)
         nc.vector.memset(w4_scale_raw[:].bitcast(I32), 0)
         nc.sync.dma_start(
-            w4_scale_raw[0:P:SPREAD, :, :].bitcast(I32), w4_scales.rearrange("a r n -> r a n").bitcast(I32)
+            w4_scale_raw[0:P:SCALE_ROWS, :].bitcast(I32), w4_scales.rearrange("a r n -> r a n").bitcast(I32)
         )
         wgs_rows = wgs.rearrange("(q t) j -> q (t j)", t=PACK)
 
@@ -112,30 +113,25 @@ def tile_list_audiobook_banner_scores_kernel(
         pages = [place("page%d" % i, [P, T2], F32, AT_PAGE[i]) for i in range(PAGES)]
         nc.vector.memset(pages[0][:], 0.0)
 
-        scales1 = place("scales1", [P, 2 * K_PASSES * S], U8, AT_SCALES)
-        w4_scale = [scales1[:, S * a : S * (a + 1)] for a in range(K_PASSES)]
-        v_scale = [scales1[:, S * (K_PASSES + a) : S * (K_PASSES + a + 1)] for a in range(K_PASSES)]
-        picked_scales = place("picked_scales", [P, S], U8, AT_PICKED_SCALES)
-        nc.vector.tensor_copy(picked_scales[:], tab_scale_sb[:].indirect(listed[:]))
+        scales1 = place("scales1", [P, K_PASSES * 2 * S], U8, AT_SCALES)
+        nc.vector.memset(scales1[:, 2 * S :].bitcast(I32), 0)
+        w4_scale = [scales1[:, 2 * S * a : 2 * S * a + S] for a in range(K_PASSES)]
+        v_scale = [scales1[:, 2 * S * a + S : 2 * S * (a + 1)] for a in range(K_PASSES)]
         nc.vector.tensor_copy(
-            scales1[:, : K_PASSES * S].rearrange("q (g t m) -> q g t m", t=PACK, m=P),
-            w4_scale_raw[:].rearrange("q a (b m t) -> q (a b) t m", b=H_PASSES, t=PACK),
+            w4_scale[0].rearrange("q (b t m) -> q b t m", t=PACK, m=P),
+            w4_scale_raw[:].rearrange("q (b m t) -> q b t m", b=H_PASSES, t=PACK),
         )
         wgs_first = place("wgs_first", [P, BANK], F32, AT_WGS_FIRST)
         load_wgs(nc.gpsimd, wgs_first, slice(0, BANK))
-        nc.vector.tensor_copy(
-            scales1[:, K_PASSES * S :].bitcast(I32).rearrange("q (a w) -> q a w", a=K_PASSES),
-            picked_scales[:].bitcast(I32).unsqueeze(1).to_broadcast([P, K_PASSES, S // 4]),
-        )
-        for row in range(1, SCALE_ROWS):
-            nc.scalar.dma_start(
-                scales1[row:P:QUADRANT, : 3 * S].bitcast(I32), scales1[SPREAD * row : P : QUADRANT, : 3 * S].bitcast(I32)
-            )
-        for row in range(SCALE_ROWS):
-            nc.scalar.dma_start(
-                scales1[row:P:QUADRANT, 3 * S :].bitcast(I32),
-                scales1[SPREAD * row + SCALE_ROWS : P : QUADRANT, 3 * S :].bitcast(I32),
-            )
+        picked_scales = place("picked_scales", [P, S], U8, AT_PICKED_SCALES)
+        nc.vector.tensor_copy(picked_scales[:], tab_scale_sb[:].indirect(listed[:]))
+        nc.vector.tensor_copy(v_scale[0].bitcast(I32), picked_scales[:].bitcast(I32))
+        for a in range(K_PASSES):
+            for row in range(1 - a, SCALE_ROWS):
+                nc.scalar.dma_start(
+                    scales1[row:P:QUADRANT, 2 * S * a : 2 * S * (a + 1)].bitcast(I32),
+                    scales1[SPREAD * row + SCALE_ROWS * a : P : QUADRANT, : 2 * S].bitcast(I32),
+                )
 
         def deal(dst, b, slots):
             words = w4_raw[:].bitcast(U16).rearrange("q a (b m t) -> q a b t m", b=H_PASSES, t=PACK)

@@ -182,7 +182,7 @@ def tile_list_audiobook_banner_scores_kernel(
         copies = {
             HALVES - 3: z_rows[4].bitcast(F32)[:, :BANK],
             HALVES - 2: z_rows[4].bitcast(F32)[:, BANK:],
-            HALVES - 1: z_rows[5].bitcast(F32)[:, BANK:],
+            HALVES - 1: z_rows[5].bitcast(F32)[:, :BANK],
         }
         placed_last = place("placed_last", [P, 2 * S], F32, AT_PLACED_LAST)
 
@@ -193,9 +193,12 @@ def tile_list_audiobook_banner_scores_kernel(
             if u == 0:
                 return factor0[:]
             j, e = divmod(u - 1, 2)
+            if j == LAST:
+                e = 1
             return hosts[j].bitcast(F32)[:, BANK * e : BANK * (e + 1)]
 
         banks = {}
+        first_steps = [slice(0, BANK // 2), slice(BANK // 2, BANK)]
 
         def product(u):
             i, h = divmod(u, 2)
@@ -215,8 +218,11 @@ def tile_list_audiobook_banner_scores_kernel(
                 )
             factor = factor_of(u)
             square = place("square0", [P, BANK], F32, AT_SQUARE)[:] if u == 0 else factor
-            nc.scalar.activation(square, acc[:], ACT.Square)
-            nc.scalar.activation(factor, square, ACT.Identity, bias=1.0, scale=cub_sb[:, b, t : t + 1])
+            steps = first_steps if u == 0 else [slice(0, BANK)]
+            for step in steps:
+                nc.scalar.activation(square[:, step], acc[:, step], ACT.Square)
+            for step in steps:
+                nc.scalar.activation(factor[:, step], square[:, step], ACT.Identity, bias=1.0, scale=cub_sb[:, b, t : t + 1])
             if u in copies:
                 nc.scalar.copy(copies[u], acc[:])
             banks[u] = acc
@@ -254,7 +260,8 @@ def tile_list_audiobook_banner_scores_kernel(
             dst = placed[i][:, BANK * h : BANK * (h + 1)]
             if u == 0:
                 nc.vector.tensor_tensor(dst, banks[u][:], wgs_first[:], MULT)
-                nc.vector.tensor_tensor(dst, dst, factor0[:], MULT)
+                for step in first_steps:
+                    nc.vector.tensor_tensor(dst[:, step], dst[:, step], factor0[:, step], MULT)
             else:
                 nc.vector.tensor_tensor(dst, banks[u][:], gains[u], MULT)
 
@@ -318,7 +325,10 @@ def tile_list_audiobook_banner_scores_kernel(
                         w2_raw[:, b, :].rearrange("q (t n c i) -> q n c t i", t=PACK, n=N_TILES, i=RUN),
                     )
             if i < LAST - 1:
-                nc.gpsimd.tensor_tensor(z_rows[i], page[:], shelf_sb[i][:], MULT)
+                width = S if i == LAST - 2 else T2
+                for lo in range(0, T2, width):
+                    cols = slice(lo, lo + width)
+                    nc.gpsimd.tensor_tensor(z_rows[i][:, cols], page[:, cols], shelf_sb[i][:, cols], MULT)
             if i == PACK - 1:
                 z_grouped = place("z_grouped", [P, PACK * T2], BF16, AT_Z_GROUPED)
                 for lo in chunks:
@@ -341,14 +351,15 @@ def tile_list_audiobook_banner_scores_kernel(
 
         def last_product(c):
             lo = chunks[c]
-            rows = shelf_last[lo // S][:, lo % S : lo % S + BANK]
-            nc.vector.tensor_tensor(z67[c][:, 1, :], pages[LAST % PAGES][:, lo : lo + BANK], rows, MULT)
+            steps = [(lo, lo + BANK // 2), (lo + BANK // 2, lo + BANK)] if c == 0 else [(lo, lo + BANK)]
+            for at, hi in steps:
+                rows = shelf_last[at // S][:, at % S : at % S + hi - at]
+                nc.vector.tensor_tensor(z67[c][:, 1, at - lo : hi - lo], pages[LAST % PAGES][:, at:hi], rows, MULT)
             for at, hi in pieces:
                 if lo <= at < lo + BANK:
-                    interleave(grouped[at][:, :, 2:PACK], z67[c][:, :, at - lo : hi - lo])
+                    for left, right in steps if c == 0 else [(at, hi)]:
+                        interleave(grouped[at][:, left - at : right - at, 2:PACK], z67[c][:, :, left - lo : right - lo])
 
-        for c in range(3):
-            last_product(c)
         z_codes = place("z_codes", [P, H_PASSES, T2], U32, AT_Z_CODES)
         w2_first = place("w2_first", [P, H_PASSES * P], U32, AT_W2_CODES)
         w2_rest = place("w2_rest", [P, (N_TILES - 1) * H_PASSES * P], U32, AT_Z67 + 6)
@@ -366,6 +377,8 @@ def tile_list_audiobook_banner_scores_kernel(
                 out=w2_codes(lo, hi), scales=w2_scale[:, lo:hi], in_=w2_grouped[:, PACK * lo : PACK * hi]
             )
 
+        for c in range(3):
+            last_product(c)
         quantise_w2(0, 1)
         for lo in range(0, T2, 2 * BANK):
             nc.vector.quantize_mx(

@@ -32,12 +32,12 @@ LAST = ROW_TILES - 1
 HALVES = ROW_TILES * 2
 N_TILES = N // P
 PAGES = 3
-SHELVES = 4
+OWN = 12
 RUN = 4
 
 AT_TABLE = (132, 15.9375)
-AT_W4_LOW = 14.5
-AT_SHELF = (16, 24, 32, 40)
+AT_W4_LOW, AT_W4_LOW_FIRST = 15.25, 75
+AT_SHELF = (16, 24, 32, 40, 16, 24, 32, 226)
 AT_CUB, AT_WGS, AT_WGS_FIRST = 150, 132, 151
 AT_TAB_SCALES, AT_W4_SCALES, AT_W4_RAW = 44, 151, 36
 AT_PAGE = (80, 48, 56)
@@ -45,17 +45,17 @@ AT_PICKED_SCALES = 55.5
 AT_CODES = (64, 68)
 AT_W4, AT_SCALES = 72, 76
 AT_BANNER = (32, 72)
-AT_Z_PASS0, AT_Z45, AT_Z67 = 88, 104, 112
+AT_Z_PASS0, AT_Z45, AT_Z67 = 88, 108, 116
 AT_Z_GROUPED = 208
 AT_W2_GROUPED = 72
 AT_W2_RAW, AT_WGO = 0, 156
 AT_Y = (0, 96, 208, 216)
 AT_PLACED = (160, 164)
-AT_PLACED_LAST = 122
-AT_Z_SCALE, AT_W2_SCALE = (40, 224), 42
+AT_PLACED_LAST = 40
+AT_Z_SCALE, AT_W2_SCALE = (226, 224), 228
 AT_SQUARE = 130
-AT_GAIN = (154, 40, 0, 16, 24, 32, 40, 16)
-AT_SCORE = (170, 178, 160, 122)
+AT_GAIN = (154, 226, 40, 16, 24, 32)
+AT_SCORE = (170, 178, 160, 132)
 AT_Z_CODES, AT_W2_CODES, AT_BASE = 186, 202, 155.5
 
 
@@ -133,14 +133,17 @@ def tile_list_audiobook_banner_scores_kernel(
                     scales1[SPREAD * row + SCALE_ROWS * a : P : QUADRANT, : 2 * S].bitcast(I32),
                 )
 
-        def deal(dst, b, slots):
+        def deal(dst, b, slots, passes=slice(0, K_PASSES)):
             words = w4_raw[:].bitcast(U16).rearrange("q a (b m t) -> q a b t m", b=H_PASSES, t=PACK)
-            nc.vector.tensor_copy(dst.bitcast(U16).rearrange("q a (t m) -> q a t m", m=P), words[:, :, b, slots, :])
+            nc.vector.tensor_copy(dst.bitcast(U16).rearrange("q a (t m) -> q a t m", m=P), words[:, passes, b, slots, :])
 
         w4_first = place("w4_first", [P, K_PASSES, 2 * P], U8, AT_W4)
         deal(w4_first[:], 0, slice(0, 1))
         w4_high = place("w4_high", [P, K_PASSES, 2 * P * PACK], U8, AT_W4 + 1)
         deal(w4_high[:], 1, slice(0, PACK))
+
+        w4_low_first = place("w4_low_first", [P, 1, 2 * P * (PACK - 1)], U8, AT_W4_LOW_FIRST)
+        deal(w4_low_first[:], 0, slice(1, PACK), slice(0, 1))
 
         wgs_sb = place("wgs_sb", [P, PACK * S], F32, AT_WGS)
         for lo in range(BANK, BANK + 3 * S, S):
@@ -154,15 +157,17 @@ def tile_list_audiobook_banner_scores_kernel(
                 nc.vector.tensor_copy(codes[:, lo : lo + width], tab_sb[a][:].indirect(part(listed, lo, lo + width)))
             v_codes.append(codes)
 
-        w4_low = place("w4_low", [P, K_PASSES, 2 * P * (PACK - 1)], U8, AT_W4_LOW)
+        w4_low = place("w4_low", [P, 1, 2 * P * (PACK - 1)], U8, AT_W4_LOW)
 
         def w4_columns(a, i):
-            tile, at = (w4_first, 0) if i == 0 else (w4_low, i - 1) if i < PACK else (w4_high, i - PACK)
+            if 0 < i < PACK:
+                return (w4_low_first, w4_low)[a][:, 0, 2 * P * (i - 1) : 2 * P * i].bitcast(FP4X4)
+            tile, at = (w4_first, 0) if i == 0 else (w4_high, i - PACK)
             return tile[:, a, 2 * P * at : 2 * P * (at + 1)].bitcast(FP4X4)
 
         def load_shelf(i, h=None):
             lo, hi = (0, T2) if h is None else (S * h, S * (h + 1))
-            rows = place("shelf%d_%d" % (i, lo), [P, hi - lo], F32, AT_SHELF[i % SHELVES] + lo // 256)
+            rows = place("shelf%d_%d" % (i, lo), [P, hi - lo], F32, AT_SHELF[i] + lo // 256)
             by_tile = shelf.rearrange("(b q t) c -> b t q c", b=H_PASSES, t=PACK)
             nc.sync.dma_start(rows[:], by_tile[i // PACK, i % PACK][:, lo:hi])
             return rows
@@ -170,32 +175,25 @@ def tile_list_audiobook_banner_scores_kernel(
         for page in pages[1:]:
             nc.gpsimd.memset(page[:], 0.0)
 
-        z_pass0 = place("z_pass0", [P, PACK * T2], BF16, AT_Z_PASS0)
+        z_pass0 = place("z_pass0", [P, (PACK + 1) * T2], BF16, AT_Z_PASS0)
         z45 = place("z45", [P, 2 * T2], BF16, AT_Z45)
         z_rows = [z_pass0[:, T2 * t : T2 * (t + 1)] for t in range(PACK)]
         z_rows.extend(z45[:, T2 * t : T2 * (t + 1)] for t in range(2))
 
+        groups = [range(1, 3), range(3, 5), range(5, 7), range(7, 9), range(9, OWN), range(OWN, HALVES)]
+        group_of = {u: j for j, group in enumerate(groups) for u in group}
         factor0 = place("factor0", [P, BANK], F32, AT_SHELF[1] - 1)
-        hosts = {0: place("factor1", [P, T2], BF16, AT_SHELF[2])[:], 1: z_rows[5], LAST: z_rows[5]}
-        for j in range(2, LAST - 1):
-            hosts[j] = z_rows[j - 2]
-        copies = {
-            HALVES - 3: z_rows[4].bitcast(F32)[:, :BANK],
-            HALVES - 2: z_rows[4].bitcast(F32)[:, BANK:],
-            HALVES - 1: z_rows[5].bitcast(F32)[:, :BANK],
-        }
-        placed_last = place("placed_last", [P, 2 * S], F32, AT_PLACED_LAST)
-
-        placed = {LAST - 1: placed_last[:, :S], LAST: placed_last[:, S:]}
-        placed[0] = place("placed0", [P, S], F32, AT_PLACED[0])[:]
+        words0 = z_pass0[:].bitcast(F32)
+        hosts = [place("factor1", [P, S], F32, AT_SHELF[2])[:], z_rows[5].bitcast(F32)]
+        hosts.extend(words0[:, S * t : S * t + BANK * len(groups[t + 2])] for t in range(PACK))
+        held = z45[:].bitcast(F32)
+        placed = {0: place("placed0", [P, S], F32, AT_PLACED[0])[:]}
 
         def factor_of(u):
             if u == 0:
                 return factor0[:]
-            j, e = divmod(u - 1, 2)
-            if j == LAST:
-                e = 1
-            return hosts[j].bitcast(F32)[:, BANK * e : BANK * (e + 1)]
+            e = u - groups[group_of[u]][0]
+            return hosts[group_of[u]][:, BANK * e : BANK * (e + 1)]
 
         banks = {}
         first_steps = [slice(0, BANK // 2), slice(BANK // 2, BANK)]
@@ -223,43 +221,37 @@ def tile_list_audiobook_banner_scores_kernel(
                 nc.scalar.activation(square[:, step], acc[:, step], ACT.Square)
             for step in steps:
                 nc.scalar.activation(factor[:, step], square[:, step], ACT.Identity, bias=1.0, scale=cub_sb[:, b, t : t + 1])
-            if u in copies:
-                nc.scalar.copy(copies[u], acc[:])
+            if u >= OWN:
+                nc.scalar.copy(held[:, BANK * (u - OWN) : BANK * (u - OWN + 1)], acc[:])
             banks[u] = acc
 
         gains = {}
 
-        def couple(j):
-            halves = [u for u in (2 * j + 1, 2 * j + 2) if u < HALVES]
-            if j == LAST - 1:
-                hosts[j] = place("factor6", [P, T2], BF16, AT_Z67)[:]
-            gain = place("gain%d" % j, [P, S], F32, AT_GAIN[j])
+        gain_tiles = {}
+
+        def group_gains(j):
+            halves = groups[j]
+            width = BANK * len(halves)
+            gain = gain_tiles[j] = place("gain%d" % j, [P, width], F32, AT_GAIN[j])
             first = BANK * halves[0] % (PACK * S)
-            whole = j > 0 and len(halves) == 2 and first + S <= PACK * S
-            for u in halves:
+            whole = j > 0 and first + width <= PACK * S
+            for e, u in enumerate(halves):
                 product(u)
-                e = u - halves[0]
                 gains[u] = gain[:, BANK * e : BANK * (e + 1)]
                 if not whole:
                     at = BANK * u % (PACK * S)
                     nc.gpsimd.tensor_tensor(gains[u], factor_of(u), (wgs_sb if at else wgs_first)[:, at : at + BANK], MULT)
             if whole:
-                nc.gpsimd.tensor_tensor(gain[:], hosts[j].bitcast(F32), wgs_sb[:, first : first + S], MULT)
-            if j == LAST - 1:
-                nc.gpsimd.tensor_tensor(placed_last[:, BANK : BANK + S], z_rows[4].bitcast(F32), gain[:], MULT)
-            if j == LAST:
-                nc.gpsimd.tensor_tensor(placed_last[:, BANK + S :], copies[HALVES - 1], gain[:, :BANK], MULT)
-
+                nc.gpsimd.tensor_tensor(gain[:], hosts[j], wgs_sb[:, first : first + width], MULT)
 
         def features(u):
             i, h = divmod(u, 2)
-            if u in copies:
-                return
             if i not in placed:
                 placed[i] = place("placed%d" % (i % 2), [P, S], F32, AT_PLACED[i % 2])[:]
             dst = placed[i][:, BANK * h : BANK * (h + 1)]
             if u == 0:
-                nc.vector.tensor_tensor(dst, banks[u][:], wgs_first[:], MULT)
+                for step in first_steps:
+                    nc.vector.tensor_tensor(dst[:, step], banks[u][:, step], wgs_first[:, step], MULT)
                 for step in first_steps:
                     nc.vector.tensor_tensor(dst[:, step], dst[:, step], factor0[:, step], MULT)
             else:
@@ -286,9 +278,9 @@ def tile_list_audiobook_banner_scores_kernel(
         cuts = (0, BANK, 2 * BANK, 3 * BANK, T2 - BANK // 2, T2)
         pieces = list(zip(cuts, cuts[1:]))
         product(0)
-        deal(w4_low[:], 0, slice(1, PACK))
-        couple(0)
-        couple(1)
+        deal(w4_low[:], 0, slice(1, PACK), slice(1, 2))
+        group_gains(0)
+        group_gains(1)
         features(0)
         shelf_sb = {i: load_shelf(i) for i in range(2)}
         shelve(0, 0, BANK)
@@ -296,34 +288,38 @@ def tile_list_audiobook_banner_scores_kernel(
         w2_grouped = z_grouped = grouped = z67 = w2_raw = base_sb = wgo_sb = shelf_last = None
         for i in range(ROW_TILES):
             page = pages[i % PAGES]
-            for u in (2 * i + 1, 2 * i + 2):
-                if u < HALVES:
-                    features(u)
+            for u in groups[i] if i < len(groups) - 1 else ():
+                features(u)
             if i < 2:
-                shelf_sb[i + 2] = load_shelf(i + 2)
                 if i == 0:
+                    shelf_sb[2] = load_shelf(2)
                     base_sb = place("base_sb", [P, N_TILES], F32, AT_BASE)
                     with nc.allow_non_contiguous_dma(reason="one bias value a partition"):
                         nc.sync.dma_start(base_sb[:], base.rearrange("(c q) -> q c", q=P))
                     wgo_sb = place("wgo_sb", [P, PICKS], F32, AT_WGO)
                     nc.sync.dma_start(wgo_sb[:], wgo)
             elif i == 2:
+                shelf_sb[3] = load_shelf(3)
                 w2_raw = place("w2_raw", [P, H_PASSES, PACK * N], F32, AT_W2_RAW)
                 nc.sync.dma_start(w2_raw[:], w2.rearrange("(b q t) n -> q b (t n)", b=H_PASSES, t=PACK))
-            elif i < LAST - 1:
-                shelf_sb[i + 1] = load_shelf(i + 1)
-            elif i == LAST - 1:
                 shelf_last = [load_shelf(LAST, h) for h in range(2)]
+            elif i < LAST - 2:
+                shelf_sb[i + 1] = load_shelf(i + 1)
             shelve(i, BANK if i == 0 else 0, S)
-            if i + 2 <= LAST:
-                couple(i + 2)
-            if i + 2 == LAST:
+            if i + 2 < len(groups):
+                group_gains(i + 2)
+            if i + 3 == len(groups):
                 w2_grouped = place("w2_grouped", [P, N_TILES * H_PASSES * P * PACK], BF16, AT_W2_GROUPED)
                 for b in range(H_PASSES):
                     nc.scalar.copy(
                         w2_grouped[:].rearrange("q (n b c i t) -> q b n c t i", b=H_PASSES, n=N_TILES, i=RUN, t=PACK)[:, b],
                         w2_raw[:, b, :].rearrange("q (t n c i) -> q n c t i", t=PACK, n=N_TILES, i=RUN),
                     )
+            if i + 2 == len(groups):
+                placed_last = place("placed_last", [P, 2 * S], F32, AT_PLACED_LAST)
+                nc.gpsimd.tensor_tensor(placed_last[:], held, gain_tiles[i + 1][:], MULT)
+                placed.update({LAST - 1: placed_last[:, :S], LAST: placed_last[:, S:]})
+                shelf_sb[LAST - 1] = load_shelf(LAST - 1)
             if i < LAST - 1:
                 width = S if i == LAST - 2 else T2
                 for lo in range(0, T2, width):
@@ -334,7 +330,7 @@ def tile_list_audiobook_banner_scores_kernel(
                 for lo in chunks:
                     interleave(
                         four_to_a_column(z_grouped[:, PACK * lo : PACK * (lo + BANK)]),
-                        z_pass0[:].rearrange("q (t c) -> q t c", t=PACK)[:, :, lo : lo + BANK],
+                        z_pass0[:, : PACK * T2].rearrange("q (t c) -> q t c", t=PACK)[:, :, lo : lo + BANK],
                     )
             elif i == LAST - 2:
                 grouped = {
@@ -343,9 +339,9 @@ def tile_list_audiobook_banner_scores_kernel(
                 for lo, hi in pieces:
                     interleave(grouped[lo][:, :, 0:2], z45[:].rearrange("q (t c) -> q t c", t=2)[:, :, lo:hi])
             elif i == LAST - 1:
-                z67 = [place("z67_%d" % c, [P, 2, BANK], BF16, AT_Z67 + 2 * c) for c in range(len(chunks))]
-                for c, lo in enumerate(chunks):
-                    cols = slice(lo, lo + BANK)
+                z67 = [place("z67_%d" % c, [P, 2, S], BF16, AT_Z67 + 4 * c) for c in range(2)]
+                for c, lo in enumerate(range(0, T2, S)):
+                    cols = slice(lo, lo + S)
                     nc.gpsimd.tensor_tensor(z67[c][:, 0, :], page[:, cols], shelf_sb[i][:, cols], MULT)
                 banners.append(zeroed_banner(0))
 
@@ -354,11 +350,11 @@ def tile_list_audiobook_banner_scores_kernel(
             steps = [(lo, lo + BANK // 2), (lo + BANK // 2, lo + BANK)] if c == 0 else [(lo, lo + BANK)]
             for at, hi in steps:
                 rows = shelf_last[at // S][:, at % S : at % S + hi - at]
-                nc.vector.tensor_tensor(z67[c][:, 1, at - lo : hi - lo], pages[LAST % PAGES][:, at:hi], rows, MULT)
+                nc.vector.tensor_tensor(z67[at // S][:, 1, at % S : at % S + hi - at], pages[LAST % PAGES][:, at:hi], rows, MULT)
             for at, hi in pieces:
                 if lo <= at < lo + BANK:
                     for left, right in steps if c == 0 else [(at, hi)]:
-                        interleave(grouped[at][:, left - at : right - at, 2:PACK], z67[c][:, :, left - lo : right - lo])
+                        interleave(grouped[at][:, left - at : right - at, 2:PACK], z67[at // S][:, :, left % S : left % S + right - left])
 
         z_codes = place("z_codes", [P, H_PASSES, T2], U32, AT_Z_CODES)
         w2_first = place("w2_first", [P, H_PASSES * P], U32, AT_W2_CODES)

@@ -54,7 +54,7 @@ AT_PLACED = (160, 164)
 AT_PLACED_LAST = 40
 AT_Z_SCALE, AT_W2_SCALE = (226, 224), 228
 AT_SQUARE = 130
-AT_GAIN = (154, 226, 40, 16, 24, 32)
+AT_GAIN = (154, 228, 40, 16, 24, 32)
 AT_SCORE = (170, 178, 160, 132)
 AT_Z_CODES, AT_W2_CODES, AT_BASE = 186, 202, 155.5
 

@@ -39,12 +39,12 @@ AT_TABLE = (132, 15.9375)
 AT_W4_LOW, AT_W4_LOW_FIRST = 15.25, 75
 AT_SHELF = (16, 24, 32, 40, 16, 24, 32, 226)
 AT_CUB, AT_WGS, AT_WGS_FIRST = 150, 132, 151
-AT_TAB_SCALES, AT_W4_SCALES, AT_W4_RAW = 44, 151, 36
+AT_TAB_SCALES, AT_W4_SCALES, AT_W4_RAW = 178, 151, 36
 AT_PAGE = (80, 48, 56)
 AT_PICKED_SCALES = 55.5
 AT_CODES = (64, 68)
 AT_W4, AT_SCALES = 72, 76
-AT_BANNER = (32, 72)
+AT_BANNER = (178, 72)
 AT_Z_PASS0, AT_Z45, AT_Z67 = 88, 108, 116
 AT_Z_GROUPED = 208
 AT_W2_GROUPED = 72
@@ -55,8 +55,9 @@ AT_PLACED_LAST = 40
 AT_Z_SCALE, AT_W2_SCALE = (226, 224), 228
 AT_SQUARE = 130
 AT_GAIN = (154, 228, 40, 16, 24, 32)
-AT_SCORE = (170, 178, 160, 132)
-AT_Z_CODES, AT_W2_CODES, AT_BASE = 186, 202, 155.5
+AT_SCORE = (170, 32, 160, 132)
+AT_Z_CODES, AT_W2_CODES, AT_BASE = 186, 16, 155.5
+AT_W2_SCALE_FIRST = 17
 
 
 def tile_list_audiobook_banner_scores_kernel(
@@ -126,6 +127,8 @@ def tile_list_audiobook_banner_scores_kernel(
         picked_scales = place("picked_scales", [P, S], U8, AT_PICKED_SCALES)
         nc.vector.tensor_copy(picked_scales[:], tab_scale_sb[:].indirect(listed[:]))
         nc.vector.tensor_copy(v_scale[0].bitcast(I32), picked_scales[:].bitcast(I32))
+        banners = [place("banner0", [P, T2], F32, AT_BANNER[0])]
+        nc.vector.memset(banners[0][:], 0.0)
         for a in range(K_PASSES):
             for row in range(1 - a, SCALE_ROWS):
                 nc.scalar.dma_start(
@@ -284,7 +287,6 @@ def tile_list_audiobook_banner_scores_kernel(
         features(0)
         shelf_sb = {i: load_shelf(i) for i in range(2)}
         shelve(0, 0, BANK)
-        banners = []
         w2_grouped = z_grouped = grouped = z67 = w2_raw = base_sb = wgo_sb = shelf_last = None
         for i in range(ROW_TILES):
             page = pages[i % PAGES]
@@ -339,22 +341,19 @@ def tile_list_audiobook_banner_scores_kernel(
                 for lo, hi in pieces:
                     interleave(grouped[lo][:, :, 0:2], z45[:].rearrange("q (t c) -> q t c", t=2)[:, :, lo:hi])
             elif i == LAST - 1:
-                z67 = [place("z67_%d" % c, [P, 2, S], BF16, AT_Z67 + 4 * c) for c in range(2)]
-                for c, lo in enumerate(range(0, T2, S)):
-                    cols = slice(lo, lo + S)
-                    nc.gpsimd.tensor_tensor(z67[c][:, 0, :], page[:, cols], shelf_sb[i][:, cols], MULT)
-                banners.append(zeroed_banner(0))
+                z67 = place("z67", [P, 2, T2], BF16, AT_Z67)
+                nc.gpsimd.tensor_tensor(z67[:, 0, :], page[:], shelf_sb[i][:], MULT)
 
         def last_product(c):
             lo = chunks[c]
             steps = [(lo, lo + BANK // 2), (lo + BANK // 2, lo + BANK)] if c == 0 else [(lo, lo + BANK)]
             for at, hi in steps:
                 rows = shelf_last[at // S][:, at % S : at % S + hi - at]
-                nc.vector.tensor_tensor(z67[at // S][:, 1, at % S : at % S + hi - at], pages[LAST % PAGES][:, at:hi], rows, MULT)
+                nc.vector.tensor_tensor(z67[:, 1, at:hi], pages[LAST % PAGES][:, at:hi], rows, MULT)
             for at, hi in pieces:
                 if lo <= at < lo + BANK:
                     for left, right in steps if c == 0 else [(at, hi)]:
-                        interleave(grouped[at][:, left - at : right - at, 2:PACK], z67[at // S][:, :, left % S : left % S + right - left])
+                        interleave(grouped[at][:, left - at : right - at, 2:PACK], z67[:, :, left:right])
 
         z_codes = place("z_codes", [P, H_PASSES, T2], U32, AT_Z_CODES)
         w2_first = place("w2_first", [P, H_PASSES * P], U32, AT_W2_CODES)
@@ -365,17 +364,22 @@ def tile_list_audiobook_banner_scores_kernel(
             return (w2_first[:, lo:hi] if hi <= first else w2_rest[:, lo - first : hi - first]).bitcast(FP8X4)
 
         z_scale = [place("z_scale%d" % b, [P, T2], U8, AT_Z_SCALE[b]) for b in range(H_PASSES)]
-        w2_scale = place("w2_scale", [P, H_PASSES * N], U8, AT_W2_SCALE)
+        w2_scale_first = place("w2_scale_first", [P, H_PASSES * P], U8, AT_W2_SCALE_FIRST)
+        w2_scale_rest = place("w2_scale_rest", [P, (N_TILES - 1) * H_PASSES * P], U8, AT_W2_SCALE)
+
+        def w2_scale(lo, hi):
+            first = H_PASSES * P
+            return w2_scale_first[:, lo:hi] if hi <= first else w2_scale_rest[:, lo - first : hi - first]
 
         def quantise_w2(first, last):
             lo, hi = H_PASSES * P * first, H_PASSES * P * last
             nc.vector.quantize_mx(
-                out=w2_codes(lo, hi), scales=w2_scale[:, lo:hi], in_=w2_grouped[:, PACK * lo : PACK * hi]
+                out=w2_codes(lo, hi), scales=w2_scale(lo, hi), in_=w2_grouped[:, PACK * lo : PACK * hi]
             )
 
+        quantise_w2(0, 1)
         for c in range(3):
             last_product(c)
-        quantise_w2(0, 1)
         for lo in range(0, T2, 2 * BANK):
             nc.vector.quantize_mx(
                 out=z_codes[:, 0, lo : lo + 2 * BANK].bitcast(FP8X4),
@@ -390,7 +394,7 @@ def tile_list_audiobook_banner_scores_kernel(
             nc.tensor.matmul_mx(
                 out=acc[:, lo % BANK : lo % BANK + hi - lo],
                 lhsT=w2_codes(at, at + P),
-                lhsT_scale=w2_scale[:, at : at + P],
+                lhsT_scale=w2_scale(at, at + P),
                 rhs=z_codes[:, b, lo:hi].bitcast(FP8X4),
                 rhs_scale=z_scale[b][:, lo:hi],
                 start=(b == 0),

@@ -1,6 +1,7 @@
 from contextlib import ExitStack
 
 import concourse.mybir as mybir
+from concourse.masks import make_identity
 
 K, T, S, H, T2, PICKS, N = 1024, 4096, 1024, 1024, 2048, 1024, 512
 FLOPS = 2 * K * H * S + 2 * H * N * T2
@@ -20,44 +21,42 @@ P = 128
 QUADRANT = 32
 QUADRANTS = P // QUADRANT
 SCALE_ROWS = 4
-SPREAD = QUADRANT // SCALE_ROWS
 PACK = 4
 BANK = 512
-BANKS = 8
 PER_COLUMN = 16
 K_PASSES = K // (P * PACK)
 H_PASSES = H // (P * PACK)
 ROW_TILES = H_PASSES * PACK
 LAST = ROW_TILES - 1
-HALVES = ROW_TILES * 2
 N_TILES = N // P
 PAGES = 3
-OWN = 12
 RUN = 4
+SCALES_AT = P - K_PASSES * QUADRANTS * SCALE_ROWS
+OWN = 6
+SHARED = 3 * BANK
 
-AT_TABLE = (132, 15.9375)
-AT_W4_LOW, AT_W4_LOW_FIRST = 15.25, 75
-AT_SHELF = (16, 24, 32, 40, 16, 24, 32, 226)
-AT_CUB, AT_WGS, AT_WGS_FIRST = 150, 132, 151
-AT_TAB_SCALES, AT_W4_SCALES, AT_W4_RAW = 178, 151, 36
-AT_PAGE = (80, 48, 56)
-AT_PICKED_SCALES = 55.5
-AT_CODES = (64, 68)
-AT_W4, AT_SCALES = 72, 76
-AT_BANNER = (178, 72)
-AT_Z_PASS0, AT_Z45, AT_Z67 = 88, 108, 116
-AT_Z_GROUPED = 208
-AT_W2_GROUPED = 72
-AT_W2_RAW, AT_WGO = 0, 156
-AT_Y = (0, 96, 208, 216)
-AT_PLACED = (160, 164)
-AT_PLACED_LAST = 40
-AT_Z_SCALE, AT_W2_SCALE = (226, 224), 228
-AT_SQUARE = 130
-AT_GAIN = (154, 228, 40, 16, 24, 32)
-AT_SCORE = (170, 32, 160, 132)
-AT_Z_CODES, AT_W2_CODES, AT_BASE = 186, 16, 155.5
-AT_W2_SCALE_FIRST = 17
+AT_CUB = 0
+AT_W4_HIGH_RAW, AT_WGS = 1, 3
+AT_TABLE = (2, 20)
+AT_PAIRS = (19, 124)
+AT_SHELF = {0: 222, 1: 35, 2: 222, 3: 43, 5: 43, 7: 35}
+AT_STAGED = 50
+AT_CODES, AT_W4, AT_SCALES = 52, 60, 64
+AT_PAGE = (68, 76, 84)
+AT_W4_LOW_RAW = 83
+AT_BANNER = (92, 100)
+AT_W2_GROUPED = 100
+AT_RING, AT_LAST_TWO = 108, 186
+AT_WGS_FIRST, AT_BASE, AT_WGO = 230, 230, 52
+AT_TURNED, AT_IDENTITY = 145, 153
+AT_GROUPED = (154, 170)
+AT_TAB_SCALES, AT_PICKED, AT_W4_SCALES = 154, 91.5, 159
+AT_Z_CODES, AT_W2_CODES = 186, (202, 170, 172)
+AT_W2_RAW, AT_FACTOR_FIRST = 206, 228
+AT_Z_SCALE, AT_W2_SCALE = (76, 78), 80
+AT_Y = (3, 11, 206, 214)
+AT_PICKS = (108, 116, 132, 43)
+AT_SCORE = (112, 170, 172, 136, 47)
 
 
 def tile_list_audiobook_banner_scores_kernel(
@@ -67,10 +66,13 @@ def tile_list_audiobook_banner_scores_kernel(
     with ExitStack() as ctx:
         list_pool = ctx.enter_context(tc.tile_pool(name="lists", bufs=1))
         pool = ctx.enter_context(tc.tile_pool(name="sbuf", bufs=1))
-        psum = ctx.enter_context(tc.psum_pool(name="psum", bufs=BANKS))
+        psum = ctx.enter_context(tc.psum_pool(name="psum", bufs=1))
 
         def place(name, shape, dtype, kib):
             return pool.tile(shape, dtype, name=name, offset=int(1024 * kib), align_bytes=64)
+
+        def bank(name, index):
+            return psum.tile([P, BANK], F32, name=name, offset=4 * BANK * index)
 
         def part(list_tile, lo, hi):
             return list_tile[:, lo // PER_COLUMN : hi // PER_COLUMN]
@@ -80,362 +82,341 @@ def tile_list_audiobook_banner_scores_kernel(
             nc.sync.dma_start(list_tile[:], src)
             return list_tile
 
-        def load_table(a):
+        def load_scale_rows(name, src, width, kib):
+            rows = place(name, [P, width], U8, kib)
+            nc.sync.dma_start(rows[SCALES_AT:, :].bitcast(I32), src.rearrange("a r n -> r a n").bitcast(I32))
+            nc.vector.memset(rows[:SCALES_AT, :].bitcast(I32), 0)
+            return rows
+
+        def load_w4(name, b, kib):
+            raw = place(name, [P, K_PASSES, H], U8, kib)
+            nc.sync.dma_start(raw[:].bitcast(I32), w4_words.rearrange("a q n -> q a n")[:, :, H * b : H * (b + 1)].bitcast(I32))
+            return raw
+
+        def deal(copy, b, raw):
+            dealt = place("w4_dealt%d" % b, [P, K_PASSES, H], U8, AT_W4 + 2 * b)
+            copy(
+                dealt[:].bitcast(U16).rearrange("q a (t m) -> q a t m", m=P),
+                raw[:].bitcast(U16).rearrange("q a (m t) -> q a t m", t=PACK),
+            )
+            return dealt
+
+        wgs_rows = wgs.rearrange("(q t) j -> q (t j)", t=PACK)
+        listed = load_list("listed", offs)
+        tab_scale_sb = load_scale_rows("tab_scale_sb", tab_scales, T, AT_TAB_SCALES)
+        w4_scale_raw = load_scale_rows("w4_scale_raw", w4_scales, H, AT_W4_SCALES)
+        wgs_first = place("wgs_first", [P, BANK], F32, AT_WGS_FIRST)
+        nc.sync.dma_start(wgs_first[:QUADRANT, :], wgs_rows[:, :BANK])
+        w4_low_raw = load_w4("w4_low_raw", 0, AT_W4_LOW_RAW)
+        shelved = load_list("shelved", offs2)
+        tab_sb = []
+        for a in range(K_PASSES):
             words = place("tab_sb%d" % a, [P, T], U32, AT_TABLE[a])
             nc.sync.dma_start(words[:].bitcast(I32), tab_words[a].rearrange("q n t -> q (n t)").bitcast(I32))
-            return words
-
-        listed = load_list("listed", offs)
-        shelved = load_list("shelved", offs2)
-        promoted = load_list("promoted", offs3)
-        banner_slots = load_list("banner_slots", offs4)
+            tab_sb.append(words)
         cub_sb = place("cub_sb", [P, H_PASSES, PACK], F32, AT_CUB)
         nc.sync.dma_start(cub_sb[:], cub.rearrange("(b q t) -> q b t", b=H_PASSES, t=PACK))
-        w4_raw = place("w4_raw", [P, K_PASSES, 2 * H], U8, AT_W4_RAW)
-        nc.sync.dma_start(w4_raw[:].bitcast(I32), w4_words.rearrange("a q n -> q a n").bitcast(I32))
-        tab_scale_sb = place("tab_scale_sb", [P, T], U8, AT_TAB_SCALES)
-        nc.vector.memset(tab_scale_sb[:].bitcast(I32), 0)
-        nc.sync.dma_start(
-            tab_scale_sb[0:P:SCALE_ROWS, :].bitcast(I32), tab_scales.rearrange("a r n -> r a n").bitcast(I32)
-        )
-        w4_scale_raw = place("w4_scale_raw", [P, H], U8, AT_W4_SCALES)
-        nc.vector.memset(w4_scale_raw[:].bitcast(I32), 0)
-        nc.sync.dma_start(
-            w4_scale_raw[0:P:SCALE_ROWS, :].bitcast(I32), w4_scales.rearrange("a r n -> r a n").bitcast(I32)
-        )
-        wgs_rows = wgs.rearrange("(q t) j -> q (t j)", t=PACK)
-
-        def load_wgs(queue, tile, cols):
-            for quadrant in (0, 2, 1, 3):
-                queue.dma_start(tile[QUADRANT * quadrant : QUADRANT * (quadrant + 1), cols], wgs_rows[:, cols])
-
-        tab_sb = [load_table(a) for a in range(K_PASSES)]
-
-        pages = [place("page%d" % i, [P, T2], F32, AT_PAGE[i]) for i in range(PAGES)]
-        nc.vector.memset(pages[0][:], 0.0)
+        promoted = load_list("promoted", offs3)
+        banner_slots = load_list("banner_slots", offs4)
 
         scales1 = place("scales1", [P, K_PASSES * 2 * S], U8, AT_SCALES)
-        nc.vector.memset(scales1[:, 2 * S :].bitcast(I32), 0)
-        w4_scale = [scales1[:, 2 * S * a : 2 * S * a + S] for a in range(K_PASSES)]
-        v_scale = [scales1[:, 2 * S * a + S : 2 * S * (a + 1)] for a in range(K_PASSES)]
+        nc.vector.memset(scales1[:].bitcast(I32), 0)
+        pages = [place("page0", [P, T2], F32, AT_PAGE[0])]
+        nc.gpsimd.memset(pages[0][:], 0.0)
+
+        picked_scales = place("picked_scales", [P, S], U8, AT_PICKED)
+        staged = place("staged", [P, 2 * S], U8, AT_STAGED)
+        nc.vector.tensor_copy(picked_scales[:], tab_scale_sb[:].indirect(listed[:]))
+
+        def double_wgs_first(filled):
+            nc.vector.tensor_copy(wgs_first[filled : 2 * filled, :].bitcast(I32), wgs_first[:filled, :].bitcast(I32))
+
+        double_wgs_first(QUADRANT)
         nc.vector.tensor_copy(
-            w4_scale[0].rearrange("q (b t m) -> q b t m", t=PACK, m=P),
+            staged[:, :S].rearrange("q (b t m) -> q b t m", t=PACK, m=P),
             w4_scale_raw[:].rearrange("q (b m t) -> q b t m", b=H_PASSES, t=PACK),
         )
-        wgs_first = place("wgs_first", [P, BANK], F32, AT_WGS_FIRST)
-        load_wgs(nc.gpsimd, wgs_first, slice(0, BANK))
-        picked_scales = place("picked_scales", [P, S], U8, AT_PICKED_SCALES)
-        nc.vector.tensor_copy(picked_scales[:], tab_scale_sb[:].indirect(listed[:]))
-        nc.vector.tensor_copy(v_scale[0].bitcast(I32), picked_scales[:].bitcast(I32))
-        banners = [place("banner0", [P, T2], F32, AT_BANNER[0])]
-        nc.vector.memset(banners[0][:], 0.0)
-        for a in range(K_PASSES):
-            for row in range(1 - a, SCALE_ROWS):
-                nc.scalar.dma_start(
-                    scales1[row:P:QUADRANT, 2 * S * a : 2 * S * (a + 1)].bitcast(I32),
-                    scales1[SPREAD * row + SCALE_ROWS * a : P : QUADRANT, : 2 * S].bitcast(I32),
-                )
+        double_wgs_first(2 * QUADRANT)
+        nc.vector.tensor_copy(staged[:, S:].bitcast(I32), picked_scales[:].bitcast(I32))
+        rows = K_PASSES * SCALE_ROWS
+        for quadrant in range(QUADRANTS):
+            nc.scalar.dma_start(
+                scales1[QUADRANT * quadrant : QUADRANT * quadrant + SCALE_ROWS, :].bitcast(I32),
+                staged[SCALES_AT + rows * quadrant : SCALES_AT + rows * (quadrant + 1), :].bitcast(I32),
+            )
+        w4_scale = [scales1[:, 2 * S * a : 2 * S * a + S] for a in range(K_PASSES)]
+        v_scale = [scales1[:, 2 * S * a + S : 2 * S * (a + 1)] for a in range(K_PASSES)]
 
-        def deal(dst, b, slots, passes=slice(0, K_PASSES)):
-            words = w4_raw[:].bitcast(U16).rearrange("q a (b m t) -> q a b t m", b=H_PASSES, t=PACK)
-            nc.vector.tensor_copy(dst.bitcast(U16).rearrange("q a (t m) -> q a t m", m=P), words[:, passes, b, slots, :])
-
-        w4_first = place("w4_first", [P, K_PASSES, 2 * P], U8, AT_W4)
-        deal(w4_first[:], 0, slice(0, 1))
-        w4_high = place("w4_high", [P, K_PASSES, 2 * P * PACK], U8, AT_W4 + 1)
-        deal(w4_high[:], 1, slice(0, PACK))
-
-        w4_low_first = place("w4_low_first", [P, 1, 2 * P * (PACK - 1)], U8, AT_W4_LOW_FIRST)
-        deal(w4_low_first[:], 0, slice(1, PACK), slice(0, 1))
-
-        wgs_sb = place("wgs_sb", [P, PACK * S], F32, AT_WGS)
-        for lo in range(BANK, BANK + 3 * S, S):
-            load_wgs(nc.sync, wgs_sb, slice(lo, lo + S if lo < BANK + 2 * S else PACK * S))
+        w4_dealt = {0: deal(nc.vector.tensor_copy, 0, w4_low_raw)}
 
         v_codes = []
         for a in range(K_PASSES):
-            codes = place("v_codes%d" % a, [P, S], U32, AT_CODES[a])
+            codes = place("v_codes%d" % a, [P, S], U32, AT_CODES + 4 * a)
             width = S if a < K_PASSES - 1 else BANK
             for lo in range(0, S, width):
                 nc.vector.tensor_copy(codes[:, lo : lo + width], tab_sb[a][:].indirect(part(listed, lo, lo + width)))
             v_codes.append(codes)
 
-        w4_low = place("w4_low", [P, 1, 2 * P * (PACK - 1)], U8, AT_W4_LOW)
-
-        def w4_columns(a, i):
-            if 0 < i < PACK:
-                return (w4_low_first, w4_low)[a][:, 0, 2 * P * (i - 1) : 2 * P * i].bitcast(FP4X4)
-            tile, at = (w4_first, 0) if i == 0 else (w4_high, i - PACK)
-            return tile[:, a, 2 * P * at : 2 * P * (at + 1)].bitcast(FP4X4)
-
-        def load_shelf(i, h=None):
-            lo, hi = (0, T2) if h is None else (S * h, S * (h + 1))
-            rows = place("shelf%d_%d" % (i, lo), [P, hi - lo], F32, AT_SHELF[i] + lo // 256)
-            by_tile = shelf.rearrange("(b q t) c -> b t q c", b=H_PASSES, t=PACK)
-            nc.sync.dma_start(rows[:], by_tile[i // PACK, i % PACK][:, lo:hi])
-            return rows
-
-        for page in pages[1:]:
+        for i in range(1, PAGES):
+            page = place("page%d" % i, [P, T2], F32, AT_PAGE[i])
             nc.gpsimd.memset(page[:], 0.0)
+            pages.append(page)
+        banners = [place("banner0", [P, T2], F32, AT_BANNER[0])]
+        nc.gpsimd.memset(banners[0][:], 0.0)
+        identity = place("identity", [P, P], F32, AT_IDENTITY)
+        make_identity(nc, identity[:])
 
-        z_pass0 = place("z_pass0", [P, (PACK + 1) * T2], BF16, AT_Z_PASS0)
-        z45 = place("z45", [P, 2 * T2], BF16, AT_Z45)
-        z_rows = [z_pass0[:, T2 * t : T2 * (t + 1)] for t in range(PACK)]
-        z_rows.extend(z45[:, T2 * t : T2 * (t + 1)] for t in range(2))
+        wgs_sb = place("wgs_sb", [P, PACK * S], F32, AT_WGS)
+        for lo, hi in ((BANK, S), (S, 2 * S), (2 * S, 3 * S), (3 * S, 4 * S), (0, BANK)):
+            for quadrant in (0, 2, 1, 3):
+                nc.sync.dma_start(wgs_sb[QUADRANT * quadrant : QUADRANT * (quadrant + 1), lo:hi], wgs_rows[:, lo:hi])
+        w4_high_raw = load_w4("w4_high_raw", 1, AT_W4_HIGH_RAW)
 
-        groups = [range(1, 3), range(3, 5), range(5, 7), range(7, 9), range(9, OWN), range(OWN, HALVES)]
-        group_of = {u: j for j, group in enumerate(groups) for u in group}
-        factor0 = place("factor0", [P, BANK], F32, AT_SHELF[1] - 1)
-        words0 = z_pass0[:].bitcast(F32)
-        hosts = [place("factor1", [P, S], F32, AT_SHELF[2])[:], z_rows[5].bitcast(F32)]
-        hosts.extend(words0[:, S * t : S * t + BANK * len(groups[t + 2])] for t in range(PACK))
-        held = z45[:].bitcast(F32)
-        placed = {0: place("placed0", [P, S], F32, AT_PLACED[0])[:]}
+        by_tile = shelf.rearrange("(b q t) c -> b t q c", b=H_PASSES, t=PACK)
+        pairs = [place("pairs%d" % b, [P, 2 * T2], F32, AT_PAIRS[b]) for b in range(H_PASSES)]
+        shelf_sb = {}
 
-        def factor_of(u):
-            if u == 0:
-                return factor0[:]
-            e = u - groups[group_of[u]][0]
-            return hosts[group_of[u]][:, BANK * e : BANK * (e + 1)]
+        def shelf_rows(i):
+            b, t = divmod(i, PACK)
+            if i not in shelf_sb and i in AT_SHELF:
+                shelf_sb[i] = place("shelf%d" % i, [P, T2], F32, AT_SHELF[i])[:]
+            elif i not in shelf_sb:
+                shelf_sb[i] = pairs[b][:, T2:]
+            return shelf_sb[i]
 
-        banks = {}
+        def load_shelf(i):
+            nc.sync.dma_start(shelf_rows(i), by_tile[i // PACK, i % PACK])
+
+        def z_of(i, lo, hi):
+            b, t = divmod(i, PACK)
+            halves = pairs[b][:].bitcast(BF16).rearrange("q (c e) -> q c e", e=2)
+            return halves[:, T2 * (t // 2) + lo : T2 * (t // 2) + hi, t % 2]
+
+        ring = place("ring", [P, PACK * S], F32, AT_RING)
+        last_two = place("last_two", [P, 2 * S], F32, AT_LAST_TWO)
+        held = pairs[1][:, :T2]
+        factor_first = place("factor_first", [P, BANK], F32, AT_FACTOR_FIRST)
         first_steps = [slice(0, BANK // 2), slice(BANK // 2, BANK)]
+        banks = {}
 
-        def product(u):
-            i, h = divmod(u, 2)
+        def feature_rows(i):
+            if i >= OWN:
+                return last_two[:, S * (i - OWN) : S * (i - OWN + 1)]
+            return ring[:, S * (i % PACK) : S * (i % PACK + 1)]
+
+        w2_raw = place("w2_raw", [P, H_PASSES * PACK * N], F32, AT_W2_RAW)
+        hosts = {1: shelf_rows(3), 2: shelf_rows(PACK), 3: pairs[0][:], 4: w2_raw[:], 5: pairs[0][:, T2:]}
+
+        def factor_rows(i):
+            return hosts[i][:, :S] if i in hosts else feature_rows(i)
+
+        def product(i, h):
             b, t = divmod(i, PACK)
             cols = slice(BANK * h, BANK * (h + 1))
-            acc = psum.tile([P, BANK], F32, name="acc", tag="bank")
-            order = (0, 1) if u == 0 else (1, 0)
+            acc = bank("p%d_%d" % (i, h), 2 * t + h)
+            first = i == 0 and h == 0
+            order = (0, 1) if first else (1, 0)
             for a in order:
                 nc.tensor.matmul_mx(
                     out=acc[:],
-                    lhsT=w4_columns(a, i),
+                    lhsT=w4_dealt[b][:, a, 2 * P * t : 2 * P * (t + 1)].bitcast(FP4X4),
                     lhsT_scale=w4_scale[a][:, P * i : P * (i + 1)],
                     rhs=v_codes[a][:, cols].bitcast(FP8X4),
                     rhs_scale=v_scale[a][:, cols],
                     start=(a == order[0]),
                     stop=(a == order[1]),
                 )
-            factor = factor_of(u)
-            square = place("square0", [P, BANK], F32, AT_SQUARE)[:] if u == 0 else factor
-            steps = first_steps if u == 0 else [slice(0, BANK)]
+            factor = factor_first[:] if first else factor_rows(i)[:, cols]
+            steps = first_steps if first else [slice(0, BANK)]
             for step in steps:
-                nc.scalar.activation(square[:, step], acc[:, step], ACT.Square)
+                nc.scalar.activation(factor[:, step], acc[:, step], ACT.Square)
             for step in steps:
-                nc.scalar.activation(factor[:, step], square[:, step], ACT.Identity, bias=1.0, scale=cub_sb[:, b, t : t + 1])
-            if u >= OWN:
-                nc.scalar.copy(held[:, BANK * (u - OWN) : BANK * (u - OWN + 1)], acc[:])
-            banks[u] = acc
+                nc.scalar.activation(factor[:, step], factor[:, step], ACT.Identity, bias=1.0, scale=cub_sb[:, b, t : t + 1])
+            if i >= OWN:
+                at = S * (i - OWN) + BANK * h
+                nc.scalar.copy(held[:, at : at + BANK], acc[:])
+            banks[i, h] = acc
 
-        gains = {}
+        def gains(i, lo=0):
+            at = S * (i % PACK)
+            nc.gpsimd.tensor_tensor(feature_rows(i)[:, lo:], factor_rows(i)[:, lo:], wgs_sb[:, at + lo : at + S], MULT)
 
-        gain_tiles = {}
+        def features(i, h):
+            dst = feature_rows(i)[:, BANK * h : BANK * (h + 1)]
+            nc.vector.tensor_tensor(dst, banks[i, h][:], dst, MULT)
 
-        def group_gains(j):
-            halves = groups[j]
-            width = BANK * len(halves)
-            gain = gain_tiles[j] = place("gain%d" % j, [P, width], F32, AT_GAIN[j])
-            first = BANK * halves[0] % (PACK * S)
-            whole = j > 0 and first + width <= PACK * S
-            for e, u in enumerate(halves):
-                product(u)
-                gains[u] = gain[:, BANK * e : BANK * (e + 1)]
-                if not whole:
-                    at = BANK * u % (PACK * S)
-                    nc.gpsimd.tensor_tensor(gains[u], factor_of(u), (wgs_sb if at else wgs_first)[:, at : at + BANK], MULT)
-            if whole:
-                nc.gpsimd.tensor_tensor(gain[:], hosts[j], wgs_sb[:, first : first + width], MULT)
+        def shelve(i, lo=0, hi=S):
+            nc.vector.tensor_copy(pages[i % PAGES][:].indirect(part(shelved, lo, hi)), feature_rows(i)[:, lo:hi])
 
-        def features(u):
-            i, h = divmod(u, 2)
-            if i not in placed:
-                placed[i] = place("placed%d" % (i % 2), [P, S], F32, AT_PLACED[i % 2])[:]
-            dst = placed[i][:, BANK * h : BANK * (h + 1)]
-            if u == 0:
-                for step in first_steps:
-                    nc.vector.tensor_tensor(dst[:, step], banks[u][:, step], wgs_first[:, step], MULT)
-                for step in first_steps:
-                    nc.vector.tensor_tensor(dst[:, step], dst[:, step], factor0[:, step], MULT)
-            else:
-                nc.vector.tensor_tensor(dst, banks[u][:], gains[u], MULT)
+        def shelf_product(i, lo=0, hi=T2):
+            nc.gpsimd.tensor_tensor(z_of(i, lo, hi), pages[i % PAGES][:, lo:hi], shelf_sb[i][:, lo:hi], MULT)
 
-        def shelve(i, lo, hi):
-            nc.vector.tensor_copy(pages[i % PAGES][:].indirect(part(shelved, lo, hi)), placed[i][:, lo:hi])
+        grouped = {}
 
-        def interleave(dst, src):
+        def merge(b, lo, hi):
+            if b not in grouped:
+                grouped[b] = place("grouped%d" % b, [P, PACK * T2], BF16, AT_GROUPED[b])
             nc.scalar.copy(
-                dst.rearrange("q (c i) t -> q c t i", i=RUN),
-                src.rearrange("q t (c i) -> q c t i", i=RUN),
+                grouped[b][:, PACK * lo : PACK * hi].bitcast(U32).rearrange("q (c w) -> q c w", w=2),
+                pairs[b][:].bitcast(U32).rearrange("q (w c) -> q c w", w=2)[:, lo:hi, :],
             )
 
-        def four_to_a_column(flat):
-            return flat.rearrange("q (c t) -> q c t", t=PACK)
+        def whole_tile(i):
+            for h in range(2):
+                product(i, h)
 
-        def zeroed_banner(n):
-            banner = place("banner%d" % n, [P, T2], F32, AT_BANNER[n])
-            nc.gpsimd.memset(banner[:], 0.0)
-            return banner
-
-        chunks = range(0, T2, BANK)
-        cuts = (0, BANK, 2 * BANK, 3 * BANK, T2 - BANK // 2, T2)
-        pieces = list(zip(cuts, cuts[1:]))
-        product(0)
-        deal(w4_low[:], 0, slice(1, PACK), slice(1, 2))
-        group_gains(0)
-        group_gains(1)
-        features(0)
-        shelf_sb = {i: load_shelf(i) for i in range(2)}
+        product(0, 0)
+        for step in first_steps:
+            nc.vector.tensor_tensor(ring[:, step], banks[0, 0][:, step], wgs_first[:, step], MULT)
+        for step in first_steps:
+            nc.vector.tensor_tensor(ring[:, step], ring[:, step], factor_first[:, step], MULT)
         shelve(0, 0, BANK)
-        w2_grouped = z_grouped = grouped = z67 = w2_raw = base_sb = wgo_sb = shelf_last = None
-        for i in range(ROW_TILES):
-            page = pages[i % PAGES]
-            for u in groups[i] if i < len(groups) - 1 else ():
-                features(u)
-            if i < 2:
-                if i == 0:
-                    shelf_sb[2] = load_shelf(2)
-                    base_sb = place("base_sb", [P, N_TILES], F32, AT_BASE)
-                    with nc.allow_non_contiguous_dma(reason="one bias value a partition"):
-                        nc.sync.dma_start(base_sb[:], base.rearrange("(c q) -> q c", q=P))
-                    wgo_sb = place("wgo_sb", [P, PICKS], F32, AT_WGO)
-                    nc.sync.dma_start(wgo_sb[:], wgo)
-            elif i == 2:
-                shelf_sb[3] = load_shelf(3)
-                w2_raw = place("w2_raw", [P, H_PASSES, PACK * N], F32, AT_W2_RAW)
-                nc.sync.dma_start(w2_raw[:], w2.rearrange("(b q t) n -> q b (t n)", b=H_PASSES, t=PACK))
-                shelf_last = [load_shelf(LAST, h) for h in range(2)]
-            elif i < LAST - 2:
-                shelf_sb[i + 1] = load_shelf(i + 1)
-            shelve(i, BANK if i == 0 else 0, S)
-            if i + 2 < len(groups):
-                group_gains(i + 2)
-            if i + 3 == len(groups):
+        product(0, 1)
+        gains(0, BANK)
+        features(0, 1)
+        shelve(0, BANK, S)
+        for i in range(2):
+            load_shelf(i)
+        for i in range(1, PACK):
+            whole_tile(i)
+            gains(i)
+        w4_dealt[1] = deal(nc.scalar.copy, 1, w4_high_raw)
+
+        load_shelf(3)
+        w2_by_pass = w2_raw[:].rearrange("q (b c) -> q b c", b=H_PASSES)
+        base_sb = place("base_sb", [P, N_TILES], F32, AT_BASE)
+        with nc.allow_non_contiguous_dma(reason="one bias value a partition"):
+            nc.sync.dma_start(base_sb[:], base.rearrange("(c q) -> q c", q=P))
+
+        shelf_banks = []
+        w2_grouped = wgo_sb = None
+        for i in range(1, OWN):
+            shelf_product(i - 1)
+            if i + 3 < LAST:
+                whole_tile(i + 3)
+            if i + 3 < OWN:
+                gains(i + 3)
+            if i == 1:
+                load_shelf(2)
+                nc.sync.dma_start(w2_by_pass, w2.rearrange("(b q t) n -> q b (t n)", b=H_PASSES, t=PACK))
+            if i == 2:
+                load_shelf(LAST)
+                load_shelf(PACK)
+            if i == PACK + 1:
+                load_shelf(OWN)
+            for h in range(2):
+                features(i, h)
+            shelve(i)
+            if i == PACK - 1:
+                whole_tile(LAST)
+                nc.gpsimd.tensor_tensor(last_two[:], last_two[:], wgs_sb[:, S * (OWN % PACK) :], MULT)
+                wgo_sb = place("wgo_sb", [P, PICKS], F32, AT_WGO)
+                nc.sync.dma_start(wgo_sb[:], wgo)
                 w2_grouped = place("w2_grouped", [P, N_TILES * H_PASSES * P * PACK], BF16, AT_W2_GROUPED)
                 for b in range(H_PASSES):
                     nc.scalar.copy(
                         w2_grouped[:].rearrange("q (n b c i t) -> q b n c t i", b=H_PASSES, n=N_TILES, i=RUN, t=PACK)[:, b],
-                        w2_raw[:, b, :].rearrange("q (t n c i) -> q n c t i", t=PACK, n=N_TILES, i=RUN),
+                        w2_by_pass[:, b, :].rearrange("q (t n c i) -> q n c t i", t=PACK, n=N_TILES, i=RUN),
                     )
-            if i + 2 == len(groups):
-                placed_last = place("placed_last", [P, 2 * S], F32, AT_PLACED_LAST)
-                nc.gpsimd.tensor_tensor(placed_last[:], held, gain_tiles[i + 1][:], MULT)
-                placed.update({LAST - 1: placed_last[:, :S], LAST: placed_last[:, S:]})
-                shelf_sb[LAST - 1] = load_shelf(LAST - 1)
-            if i < LAST - 1:
-                width = S if i == LAST - 2 else T2
-                for lo in range(0, T2, width):
-                    cols = slice(lo, lo + width)
-                    nc.gpsimd.tensor_tensor(z_rows[i][:, cols], page[:, cols], shelf_sb[i][:, cols], MULT)
-            if i == PACK - 1:
-                z_grouped = place("z_grouped", [P, PACK * T2], BF16, AT_Z_GROUPED)
-                for lo in chunks:
-                    interleave(
-                        four_to_a_column(z_grouped[:, PACK * lo : PACK * (lo + BANK)]),
-                        z_pass0[:, : PACK * T2].rearrange("q (t c) -> q t c", t=PACK)[:, :, lo : lo + BANK],
-                    )
-            elif i == LAST - 2:
-                grouped = {
-                    lo: place("grouped%d" % lo, [P, hi - lo, PACK], BF16, AT_Z_PASS0 + lo // P) for lo, hi in pieces
-                }
-                for lo, hi in pieces:
-                    interleave(grouped[lo][:, :, 0:2], z45[:].rearrange("q (t c) -> q t c", t=2)[:, :, lo:hi])
-            elif i == LAST - 1:
-                z67 = place("z67", [P, 2, T2], BF16, AT_Z67)
-                nc.gpsimd.tensor_tensor(z67[:, 0, :], page[:], shelf_sb[i][:], MULT)
+            if i == PACK:
+                load_shelf(PACK + 1)
+                nc.gpsimd.tensor_tensor(last_two[:], last_two[:], held, MULT)
+                turned = place("turned", [P, SHARED], F32, AT_TURNED)
+                for c in range(SHARED // BANK):
+                    there = bank("there%d" % c, c % 2)
+                    for at in range(0, BANK, P):
+                        nc.tensor.transpose(there[:, at : at + P], shelf_sb[LAST][:, BANK * c + at : BANK * c + at + P], identity[:])
+                    nc.scalar.copy(turned[:, BANK * c : BANK * (c + 1)], there[:])
+                for c in range(SHARED // BANK):
+                    back = bank("back%d" % c, PACK + c)
+                    for at in range(0, BANK, P):
+                        nc.tensor.transpose(back[:, at : at + P], turned[:, BANK * c + at : BANK * c + at + P], identity[:])
+                    shelf_banks.append(back)
+                for lo in range(0, T2, S):
+                    merge(0, lo, lo + S)
+        shelve(OWN)
+        shelf_product(OWN - 1)
+        shelve(LAST)
+        for lo in range(0, T2, S):
+            shelf_product(OWN, lo, lo + S)
+        shelf_product(LAST, SHARED, T2)
 
-        def last_product(c):
-            lo = chunks[c]
-            steps = [(lo, lo + BANK // 2), (lo + BANK // 2, lo + BANK)] if c == 0 else [(lo, lo + BANK)]
-            for at, hi in steps:
-                rows = shelf_last[at // S][:, at % S : at % S + hi - at]
-                nc.vector.tensor_tensor(z67[:, 1, at:hi], pages[LAST % PAGES][:, at:hi], rows, MULT)
-            for at, hi in pieces:
-                if lo <= at < lo + BANK:
-                    for left, right in steps if c == 0 else [(at, hi)]:
-                        interleave(grouped[at][:, left - at : right - at, 2:PACK], z67[:, :, left:right])
+        cuts = (0, BANK // 2, BANK, 2 * BANK, 3 * BANK, T2 - BANK // 2, T2)
+        for lo, hi in zip(cuts, cuts[1:]):
+            if lo < SHARED:
+                rows_last = shelf_banks[lo // BANK][:, lo % BANK : lo % BANK + hi - lo]
+                nc.vector.tensor_tensor(z_of(LAST, lo, hi), rows_last, pages[LAST % PAGES][:, lo:hi], MULT)
+            merge(1, lo, hi)
 
         z_codes = place("z_codes", [P, H_PASSES, T2], U32, AT_Z_CODES)
-        w2_first = place("w2_first", [P, H_PASSES * P], U32, AT_W2_CODES)
-        w2_rest = place("w2_rest", [P, (N_TILES - 1) * H_PASSES * P], U32, AT_Z67 + 6)
-
-        def w2_codes(lo, hi):
-            first = H_PASSES * P
-            return (w2_first[:, lo:hi] if hi <= first else w2_rest[:, lo - first : hi - first]).bitcast(FP8X4)
-
         z_scale = [place("z_scale%d" % b, [P, T2], U8, AT_Z_SCALE[b]) for b in range(H_PASSES)]
-        w2_scale_first = place("w2_scale_first", [P, H_PASSES * P], U8, AT_W2_SCALE_FIRST)
-        w2_scale_rest = place("w2_scale_rest", [P, (N_TILES - 1) * H_PASSES * P], U8, AT_W2_SCALE)
-
-        def w2_scale(lo, hi):
-            first = H_PASSES * P
-            return w2_scale_first[:, lo:hi] if hi <= first else w2_scale_rest[:, lo - first : hi - first]
+        w2_parts = ((0, 1), (1, 2), (2, N_TILES))
+        w2_tiles = {
+            first: place("w2_codes%d" % first, [P, (last - first) * H_PASSES * P], U32, AT_W2_CODES[first])
+            for first, last in w2_parts
+        }
+        w2_scale = place("w2_scale", [P, N_TILES * H_PASSES * P], U8, AT_W2_SCALE)
 
         def quantise_w2(first, last):
             lo, hi = H_PASSES * P * first, H_PASSES * P * last
             nc.vector.quantize_mx(
-                out=w2_codes(lo, hi), scales=w2_scale(lo, hi), in_=w2_grouped[:, PACK * lo : PACK * hi]
+                out=w2_tiles[first][:].bitcast(FP8X4), scales=w2_scale[:, lo:hi], in_=w2_grouped[:, PACK * lo : PACK * hi]
             )
 
-        quantise_w2(0, 1)
-        for c in range(3):
-            last_product(c)
-        for lo in range(0, T2, 2 * BANK):
+        def quantise_z(b, lo, hi):
             nc.vector.quantize_mx(
-                out=z_codes[:, 0, lo : lo + 2 * BANK].bitcast(FP8X4),
-                scales=z_scale[0][:, lo : lo + 2 * BANK],
-                in_=z_grouped[:, PACK * lo : PACK * (lo + 2 * BANK)],
+                out=z_codes[:, b, lo:hi].bitcast(FP8X4), scales=z_scale[b][:, lo:hi], in_=grouped[b][:, PACK * lo : PACK * hi]
             )
-            if lo == 0:
-                last_product(3)
 
         def second_pass(acc, n, b, lo, hi):
             at = P * (H_PASSES * n + b)
+            first = min(n, w2_parts[-1][0])
+            within = at - P * H_PASSES * first
             nc.tensor.matmul_mx(
                 out=acc[:, lo % BANK : lo % BANK + hi - lo],
-                lhsT=w2_codes(at, at + P),
-                lhsT_scale=w2_scale(at, at + P),
+                lhsT=w2_tiles[first][:, within : within + P].bitcast(FP8X4),
+                lhsT_scale=w2_scale[:, at : at + P],
                 rhs=z_codes[:, b, lo:hi].bitcast(FP8X4),
                 rhs_scale=z_scale[b][:, lo:hi],
                 start=(b == 0),
                 stop=(b == H_PASSES - 1 and hi % BANK == 0),
             )
 
-        y_first = place("y0", [P, T2], F32, AT_Y[0])
-        accs_first = [psum.tile([P, BANK], F32, name="acc", tag="bank") for lo in chunks]
-        for acc, lo in zip(accs_first, chunks):
-            second_pass(acc, 0, 0, lo, lo + BANK)
-        for lo, hi in pieces:
-            nc.vector.quantize_mx(
-                out=z_codes[:, 1, lo:hi].bitcast(FP8X4),
-                scales=z_scale[1][:, lo:hi],
-                in_=grouped[lo][:].rearrange("q c t -> q (c t)"),
-            )
+        chunks = range(0, T2, BANK)
+        accs_first = [bank("y0_%d" % c, c) for c in range(len(chunks))]
+        quantise_w2(0, 1)
+        pieces = (0, BANK, 2 * BANK, 3 * BANK, T2 - BANK // 2, T2)
+        for lo, hi in zip(pieces, pieces[1:]):
+            if lo % S == 0:
+                quantise_z(0, lo, lo + S)
+                for at in (lo, lo + BANK):
+                    second_pass(accs_first[at // BANK], 0, 0, at, at + BANK)
+            quantise_z(1, lo, hi)
             second_pass(accs_first[lo // BANK], 0, 1, lo, hi)
         quantise_w2(1, 2)
-        nc.vector.tensor_copy(y_first[:, :BANK], accs_first[0][:])
         quantise_w2(2, N_TILES)
-        banners.append(zeroed_banner(1))
+        banner = place("banner1", [P, T2], F32, AT_BANNER[1])
+        nc.gpsimd.memset(banner[:], 0.0)
+        banners.append(banner)
 
-        def second_product(n):
-            if n == 0:
-                y, accs = y_first, accs_first
-            else:
-                y = place("y%d" % n, [P, T2], F32, AT_Y[n])
-                accs = [psum.tile([P, BANK], F32, name="acc", tag="bank") for lo in chunks]
+        both = {}
+
+        def picked(n, width):
+            y = place("y%d" % n, [P, T2], F32, AT_Y[n])
+            accs = accs_first
+            if n > 0:
+                accs = [bank("y%d_%d" % (n, c), PACK * (n % 2) + c) for c in range(len(chunks))]
                 for b in range(H_PASSES):
                     for acc, lo in zip(accs, chunks):
                         second_pass(acc, n, b, lo, lo + BANK)
             for acc, lo in zip(accs, chunks):
-                if n > 0 or lo > 0:
-                    nc.scalar.copy(y[:, lo : lo + BANK], acc[:])
-            return y
-
-        def pick(n, y, lo, hi):
-            nc.vector.tensor_copy(both[n][:, lo:hi], y[:].indirect(part(promoted, lo, hi)))
+                nc.scalar.copy(y[:, lo : lo + BANK], acc[:])
+            both[n] = place("picks%d" % n, [P, PICKS], F32, AT_PICKS[n])
+            for lo in range(0, PICKS, width):
+                nc.vector.tensor_copy(both[n][:, lo : lo + width], y[:].indirect(part(promoted, lo, lo + width)))
 
         def show(n, lo, hi):
-            score = both[n][:, PICKS + lo : PICKS + hi]
+            score = place("score%d_%d" % (n, lo), [P, hi - lo], F32, AT_SCORE[n + (hi == PICKS)])[:]
             nc.scalar.activation(score, both[n][:, lo:hi], ACT.Sigmoid, bias=base_sb[:, n : n + 1])
             nc.vector.tensor_tensor(banners[n % 2][:].indirect(part(banner_slots, lo, hi)), score, wgo_sb[:, lo:hi], MULT)
             if hi == PICKS:
@@ -445,13 +426,6 @@ def tile_list_audiobook_banner_scores_kernel(
                     cols = slice(width * k, width * (k + 1))
                     queue.dma_start(out[P * n : P * (n + 1), cols], banners[n % 2][:, cols])
 
-        def picked(n, width):
-            y = second_product(n)
-            both[n] = place("both%d" % n, [P, 2 * PICKS], F32, AT_SCORE[n])
-            for lo in range(0, PICKS, width):
-                pick(n, y, lo, lo + width)
-
-        both = {}
         picked(0, PICKS // 2)
         show(0, 0, PICKS // 2)
         picked(1, PICKS)

@@ -33,28 +33,28 @@ PAGES = 3
 RUN = 4
 SCALES_AT = P - K_PASSES * QUADRANTS * SCALE_ROWS
 OWN = 6
-SHARED = 3 * BANK
+SHARED = 5 * BANK // 2
 
 AT_CUB = 0
 AT_W4_HIGH_RAW, AT_WGS = 1, 3
-AT_TABLE = (2, 20)
+AT_TABLE = (2, 19)
 AT_PAIRS = (19, 124)
-AT_SHELF = {0: 222, 1: 35, 2: 222, 3: 43, 5: 43, 7: 35}
+AT_SHELF = {0: 222, 1: 35, 3: 43, 5: 43, 7: 35}
 AT_STAGED = 50
 AT_CODES, AT_W4, AT_SCALES = 52, 60, 64
 AT_PAGE = (68, 76, 84)
 AT_W4_LOW_RAW = 83
 AT_BANNER = (92, 100)
 AT_W2_GROUPED = 100
-AT_RING, AT_LAST_TWO = 108, 186
+AT_RING, AT_LAST_TWO = 108, 190
 AT_WGS_FIRST, AT_BASE, AT_WGO = 230, 230, 52
-AT_TURNED, AT_IDENTITY = 145, 153
+AT_TURNED, AT_IDENTITY, AT_SQUARES = 145, 153, 232
 AT_GROUPED = (154, 170)
 AT_TAB_SCALES, AT_PICKED, AT_W4_SCALES = 154, 91.5, 159
-AT_Z_CODES, AT_W2_CODES = 186, (202, 170, 172)
+AT_Z_CODES, AT_W2_CODES = 206, (202, 170, 172)
 AT_W2_RAW, AT_FACTOR_FIRST = 206, 228
-AT_Z_SCALE, AT_W2_SCALE = (76, 78), 80
-AT_Y = (3, 11, 206, 214)
+AT_Z_SCALE, AT_W2_SCALE = (76, 78), (194, 80)
+AT_Y = (3, 11, 186, 222)
 AT_PICKS = (108, 116, 132, 43)
 AT_SCORE = (112, 170, 172, 136, 47)
 
@@ -152,9 +152,9 @@ def tile_list_audiobook_banner_scores_kernel(
         v_codes = []
         for a in range(K_PASSES):
             codes = place("v_codes%d" % a, [P, S], U32, AT_CODES + 4 * a)
-            width = S if a < K_PASSES - 1 else BANK
-            for lo in range(0, S, width):
-                nc.vector.tensor_copy(codes[:, lo : lo + width], tab_sb[a][:].indirect(part(listed, lo, lo + width)))
+            cuts = (0, S) if a < K_PASSES - 1 else (0, BANK // 2, BANK, S)
+            for lo, hi in zip(cuts, cuts[1:]):
+                nc.vector.tensor_copy(codes[:, lo:hi], tab_sb[a][:].indirect(part(listed, lo, hi)))
             v_codes.append(codes)
 
         for i in range(1, PAGES):
@@ -205,20 +205,19 @@ def tile_list_audiobook_banner_scores_kernel(
             return ring[:, S * (i % PACK) : S * (i % PACK + 1)]
 
         w2_raw = place("w2_raw", [P, H_PASSES * PACK * N], F32, AT_W2_RAW)
-        hosts = {1: shelf_rows(3), 2: shelf_rows(PACK), 3: pairs[0][:], 4: w2_raw[:], 5: pairs[0][:, T2:]}
+        groups = [range(1, 3), range(3, 5), range(5, 8), range(8, 10), range(10, 12), range(12, 16)]
+        hosts = [shelf_rows(1), shelf_rows(3), shelf_rows(PACK), pairs[0][:], shelf_rows(2), w2_raw[:]]
 
-        def factor_rows(i):
-            return hosts[i][:, :S] if i in hosts else feature_rows(i)
+        def factor_of(u):
+            j = max(j for j, group in enumerate(groups) if group[0] <= u)
+            e = u - groups[j][0]
+            return hosts[j][:, BANK * e : BANK * (e + 1)]
 
-        def product(i, h):
+        def first_product(acc, i, cols, order):
             b, t = divmod(i, PACK)
-            cols = slice(BANK * h, BANK * (h + 1))
-            acc = bank("p%d_%d" % (i, h), 2 * t + h)
-            first = i == 0 and h == 0
-            order = (0, 1) if first else (1, 0)
             for a in order:
                 nc.tensor.matmul_mx(
-                    out=acc[:],
+                    out=acc,
                     lhsT=w4_dealt[b][:, a, 2 * P * t : 2 * P * (t + 1)].bitcast(FP4X4),
                     lhsT_scale=w4_scale[a][:, P * i : P * (i + 1)],
                     rhs=v_codes[a][:, cols].bitcast(FP8X4),
@@ -226,24 +225,40 @@ def tile_list_audiobook_banner_scores_kernel(
                     start=(a == order[0]),
                     stop=(a == order[1]),
                 )
-            factor = factor_first[:] if first else factor_rows(i)[:, cols]
-            steps = first_steps if first else [slice(0, BANK)]
-            for step in steps:
-                nc.scalar.activation(factor[:, step], acc[:, step], ACT.Square)
-            for step in steps:
-                nc.scalar.activation(factor[:, step], factor[:, step], ACT.Identity, bias=1.0, scale=cub_sb[:, b, t : t + 1])
+
+        squares = place("squares", [P, 2 * BANK], F32, AT_SQUARES)
+        made = []
+
+        def make_factor(factor, acc, i):
+            b, t = divmod(i, PACK)
+            at = BANK * (len(made) % 2)
+            made.append(i)
+            square = squares[:, at : at + acc.shape[1]]
+            nc.scalar.activation(square, acc, ACT.Square)
+            nc.scalar.activation(factor, square, ACT.Identity, bias=1.0, scale=cub_sb[:, b, t : t + 1])
+
+        def product(i, h):
+            acc = bank("p%d_%d" % (i, h), 2 * (i % PACK) + h)
+            first_product(acc[:], i, slice(BANK * h, BANK * (h + 1)), (1, 0))
+            make_factor(factor_of(2 * i + h), acc[:], i)
             if i >= OWN:
                 at = S * (i - OWN) + BANK * h
                 nc.scalar.copy(held[:, at : at + BANK], acc[:])
             banks[i, h] = acc
 
-        def gains(i, lo=0):
-            at = S * (i % PACK)
-            nc.gpsimd.tensor_tensor(feature_rows(i)[:, lo:], factor_rows(i)[:, lo:], wgs_sb[:, at + lo : at + S], MULT)
+        def gains(j):
+            for u in sorted(groups[j], key=lambda u: u % 2) if j == 0 else groups[j]:
+                product(*divmod(u, 2))
+            width = BANK * len(groups[j])
+            at = BANK * groups[j][0] % (PACK * S)
+            gain = last_two[:] if groups[j][0] == 2 * OWN else ring[:, at : at + width]
+            nc.gpsimd.tensor_tensor(gain, hosts[j][:, :width], wgs_sb[:, at : at + width], MULT)
 
-        def features(i, h):
-            dst = feature_rows(i)[:, BANK * h : BANK * (h + 1)]
-            nc.vector.tensor_tensor(dst, banks[i, h][:], dst, MULT)
+        def features(j):
+            for u in groups[j]:
+                i, h = divmod(u, 2)
+                dst = feature_rows(i)[:, BANK * h : BANK * (h + 1)]
+                nc.vector.tensor_tensor(dst, banks[i, h][:], dst, MULT)
 
         def shelve(i, lo=0, hi=S):
             nc.vector.tensor_copy(pages[i % PAGES][:].indirect(part(shelved, lo, hi)), feature_rows(i)[:, lo:hi])
@@ -261,92 +276,80 @@ def tile_list_audiobook_banner_scores_kernel(
                 pairs[b][:].bitcast(U32).rearrange("q (w c) -> q c w", w=2)[:, lo:hi, :],
             )
 
-        def whole_tile(i):
-            for h in range(2):
-                product(i, h)
-
-        product(0, 0)
-        for step in first_steps:
-            nc.vector.tensor_tensor(ring[:, step], banks[0, 0][:, step], wgs_first[:, step], MULT)
+        first_banks = [bank("first%d" % e, index)[:, : BANK // 2] for e, index in enumerate((4, 6))]
+        for step, acc in zip(first_steps, first_banks):
+            first_product(acc, 0, step, (0, 1))
+            make_factor(factor_first[:, step], acc, 0)
+        for step, acc in zip(first_steps, first_banks):
+            nc.vector.tensor_tensor(ring[:, step], acc, wgs_first[:, step], MULT)
         for step in first_steps:
             nc.vector.tensor_tensor(ring[:, step], ring[:, step], factor_first[:, step], MULT)
         shelve(0, 0, BANK)
-        product(0, 1)
-        gains(0, BANK)
-        features(0, 1)
-        shelve(0, BANK, S)
-        for i in range(2):
+        for j in range(3):
+            gains(j)
+        for i in (0, 1, 3, PACK):
             load_shelf(i)
-        for i in range(1, PACK):
-            whole_tile(i)
-            gains(i)
-        w4_dealt[1] = deal(nc.scalar.copy, 1, w4_high_raw)
-
-        load_shelf(3)
-        w2_by_pass = w2_raw[:].rearrange("q (b c) -> q b c", b=H_PASSES)
         base_sb = place("base_sb", [P, N_TILES], F32, AT_BASE)
         with nc.allow_non_contiguous_dma(reason="one bias value a partition"):
             nc.sync.dma_start(base_sb[:], base.rearrange("(c q) -> q c", q=P))
+        features(0)
+        shelve(0, BANK, S)
+        w4_dealt[1] = deal(nc.scalar.copy, 1, w4_high_raw)
+        gains(3)
+        shelf_product(0)
+        features(1)
+        shelve(1)
+        gains(4)
+        load_shelf(2)
+        shelf_product(1)
+        load_shelf(LAST)
+        features(2)
+        shelve(2)
+        gains(5)
+        w2_by_pass = w2_raw[:].rearrange("q (b c) -> q b c", b=H_PASSES)
+        nc.sync.dma_start(w2_by_pass, w2.rearrange("(b q t) n -> q b (t n)", b=H_PASSES, t=PACK))
+        wgo_sb = place("wgo_sb", [P, PICKS], F32, AT_WGO)
+        nc.sync.dma_start(wgo_sb[:], wgo)
+        features(3)
+        shelve(3)
+        shelf_product(2)
+        nc.gpsimd.tensor_tensor(last_two[:], last_two[:], held, MULT)
 
+        turned = place("turned", [P, SHARED], F32, AT_TURNED)
+        spans = [(lo, min(lo + BANK, SHARED)) for lo in range(0, SHARED, BANK)]
+        for c, (lo, hi) in enumerate(spans):
+            there = bank("there%d" % c, c % 2)
+            for at in range(lo, hi, P):
+                nc.tensor.transpose(there[:, at - lo : at - lo + P], shelf_sb[LAST][:, at : at + P], identity[:])
+            nc.scalar.copy(turned[:, lo:hi], there[:, : hi - lo])
         shelf_banks = []
-        w2_grouped = wgo_sb = None
-        for i in range(1, OWN):
-            shelf_product(i - 1)
-            if i + 3 < LAST:
-                whole_tile(i + 3)
-            if i + 3 < OWN:
-                gains(i + 3)
-            if i == 1:
-                load_shelf(2)
-                nc.sync.dma_start(w2_by_pass, w2.rearrange("(b q t) n -> q b (t n)", b=H_PASSES, t=PACK))
-            if i == 2:
-                load_shelf(LAST)
-                load_shelf(PACK)
-            if i == PACK + 1:
-                load_shelf(OWN)
-            for h in range(2):
-                features(i, h)
-            shelve(i)
-            if i == PACK - 1:
-                whole_tile(LAST)
-                nc.gpsimd.tensor_tensor(last_two[:], last_two[:], wgs_sb[:, S * (OWN % PACK) :], MULT)
-                wgo_sb = place("wgo_sb", [P, PICKS], F32, AT_WGO)
-                nc.sync.dma_start(wgo_sb[:], wgo)
-                w2_grouped = place("w2_grouped", [P, N_TILES * H_PASSES * P * PACK], BF16, AT_W2_GROUPED)
-                for b in range(H_PASSES):
-                    nc.scalar.copy(
-                        w2_grouped[:].rearrange("q (n b c i t) -> q b n c t i", b=H_PASSES, n=N_TILES, i=RUN, t=PACK)[:, b],
-                        w2_by_pass[:, b, :].rearrange("q (t n c i) -> q n c t i", t=PACK, n=N_TILES, i=RUN),
-                    )
-            if i == PACK:
-                load_shelf(PACK + 1)
-                nc.gpsimd.tensor_tensor(last_two[:], last_two[:], held, MULT)
-                turned = place("turned", [P, SHARED], F32, AT_TURNED)
-                for c in range(SHARED // BANK):
-                    there = bank("there%d" % c, c % 2)
-                    for at in range(0, BANK, P):
-                        nc.tensor.transpose(there[:, at : at + P], shelf_sb[LAST][:, BANK * c + at : BANK * c + at + P], identity[:])
-                    nc.scalar.copy(turned[:, BANK * c : BANK * (c + 1)], there[:])
-                for c in range(SHARED // BANK):
-                    back = bank("back%d" % c, PACK + c)
-                    for at in range(0, BANK, P):
-                        nc.tensor.transpose(back[:, at : at + P], turned[:, BANK * c + at : BANK * c + at + P], identity[:])
-                    shelf_banks.append(back)
-                for lo in range(0, T2, S):
-                    merge(0, lo, lo + S)
+        for c, (lo, hi) in enumerate(spans):
+            back = bank("back%d" % c, PACK + c)
+            for at in range(lo, hi, P):
+                nc.tensor.transpose(back[:, at - lo : at - lo + P], turned[:, at : at + P], identity[:])
+            shelf_banks.append(back)
+
+        features(4)
+        shelve(4)
+        shelf_product(3)
+        load_shelf(5)
+        w2_grouped = place("w2_grouped", [P, N_TILES * H_PASSES * P * PACK], BF16, AT_W2_GROUPED)
+        for b in range(H_PASSES):
+            nc.scalar.copy(
+                w2_grouped[:].rearrange("q (n b c i t) -> q b n c t i", b=H_PASSES, n=N_TILES, i=RUN, t=PACK)[:, b],
+                w2_by_pass[:, b, :].rearrange("q (t n c i) -> q n c t i", t=PACK, n=N_TILES, i=RUN),
+            )
+        for lo in range(0, T2, S):
+            merge(0, lo, lo + S)
+        shelve(5)
+        shelf_product(4)
+        load_shelf(OWN)
         shelve(OWN)
-        shelf_product(OWN - 1)
+        shelf_product(5)
         shelve(LAST)
         for lo in range(0, T2, S):
             shelf_product(OWN, lo, lo + S)
         shelf_product(LAST, SHARED, T2)
-
-        cuts = (0, BANK // 2, BANK, 2 * BANK, 3 * BANK, T2 - BANK // 2, T2)
-        for lo, hi in zip(cuts, cuts[1:]):
-            if lo < SHARED:
-                rows_last = shelf_banks[lo // BANK][:, lo % BANK : lo % BANK + hi - lo]
-                nc.vector.tensor_tensor(z_of(LAST, lo, hi), rows_last, pages[LAST % PAGES][:, lo:hi], MULT)
-            merge(1, lo, hi)
 
         z_codes = place("z_codes", [P, H_PASSES, T2], U32, AT_Z_CODES)
         z_scale = [place("z_scale%d" % b, [P, T2], U8, AT_Z_SCALE[b]) for b in range(H_PASSES)]
@@ -355,12 +358,19 @@ def tile_list_audiobook_banner_scores_kernel(
             first: place("w2_codes%d" % first, [P, (last - first) * H_PASSES * P], U32, AT_W2_CODES[first])
             for first, last in w2_parts
         }
-        w2_scale = place("w2_scale", [P, N_TILES * H_PASSES * P], U8, AT_W2_SCALE)
+        first_cols = H_PASSES * P
+        scale_tiles = [
+            place("w2_scale%d" % e, [P, width], U8, AT_W2_SCALE[e])
+            for e, width in enumerate((first_cols, (N_TILES - 1) * first_cols))
+        ]
+
+        def w2_scale(lo, hi):
+            return scale_tiles[0][:, lo:hi] if hi <= first_cols else scale_tiles[1][:, lo - first_cols : hi - first_cols]
 
         def quantise_w2(first, last):
             lo, hi = H_PASSES * P * first, H_PASSES * P * last
             nc.vector.quantize_mx(
-                out=w2_tiles[first][:].bitcast(FP8X4), scales=w2_scale[:, lo:hi], in_=w2_grouped[:, PACK * lo : PACK * hi]
+                out=w2_tiles[first][:].bitcast(FP8X4), scales=w2_scale(lo, hi), in_=w2_grouped[:, PACK * lo : PACK * hi]
             )
 
         def quantise_z(b, lo, hi):
@@ -375,7 +385,7 @@ def tile_list_audiobook_banner_scores_kernel(
             nc.tensor.matmul_mx(
                 out=acc[:, lo % BANK : lo % BANK + hi - lo],
                 lhsT=w2_tiles[first][:, within : within + P].bitcast(FP8X4),
-                lhsT_scale=w2_scale[:, at : at + P],
+                lhsT_scale=w2_scale(at, at + P),
                 rhs=z_codes[:, b, lo:hi].bitcast(FP8X4),
                 rhs_scale=z_scale[b][:, lo:hi],
                 start=(b == 0),
@@ -385,6 +395,14 @@ def tile_list_audiobook_banner_scores_kernel(
         chunks = range(0, T2, BANK)
         accs_first = [bank("y0_%d" % c, c) for c in range(len(chunks))]
         quantise_w2(0, 1)
+        cuts = (0, BANK // 2, BANK, 2 * BANK, 3 * BANK, T2 - BANK // 2, T2)
+        for lo, hi in zip(cuts, cuts[1:]):
+            if lo < SHARED:
+                end = min(hi, SHARED)
+                rows_last = shelf_banks[lo // BANK][:, lo % BANK : lo % BANK + end - lo]
+                nc.vector.tensor_tensor(z_of(LAST, lo, end), rows_last, pages[LAST % PAGES][:, lo:end], MULT)
+            merge(1, lo, hi)
+
         pieces = (0, BANK, 2 * BANK, 3 * BANK, T2 - BANK // 2, T2)
         for lo, hi in zip(pieces, pieces[1:]):
             if lo % S == 0:

@@ -38,7 +38,7 @@ SHARED = 5 * BANK // 2
 AT_CUB = 0
 AT_W4_HIGH_RAW, AT_WGS = 1, 3
 AT_TABLE = (2, 19)
-AT_PAIRS = (19, 124)
+AT_Z_ROWS, AT_PAIRS = (19, 206), 124
 AT_SHELF = {0: 222, 1: 35, 3: 43, 5: 43, 7: 35}
 AT_STAGED = 50
 AT_CODES, AT_W4, AT_SCALES = 52, 60, 64
@@ -47,14 +47,14 @@ AT_W4_LOW_RAW = 83
 AT_BANNER = (92, 100)
 AT_W2_GROUPED = 100
 AT_RING, AT_LAST_TWO = 108, 190
-AT_WGS_FIRST, AT_BASE, AT_WGO = 230, 230, 52
+AT_WGS_FIRST, AT_BASE, AT_WGO = 230, 230, 232
 AT_TURNED, AT_IDENTITY, AT_SQUARES = 145, 153, 232
 AT_GROUPED = (154, 170)
 AT_TAB_SCALES, AT_PICKED, AT_W4_SCALES = 154, 91.5, 159
 AT_Z_CODES, AT_W2_CODES = 206, (202, 170, 172)
-AT_W2_RAW, AT_FACTOR_FIRST = 206, 228
+AT_W2_RAW, AT_FACTOR_FIRST = 52, 228
 AT_Z_SCALE, AT_W2_SCALE = (76, 78), (194, 80)
-AT_Y = (3, 11, 186, 222)
+AT_Y = (3, 3, 186, 222)
 AT_PICKS = (108, 116, 132, 43)
 AT_SCORE = (112, 170, 172, 136, 47)
 
@@ -167,21 +167,21 @@ def tile_list_audiobook_banner_scores_kernel(
         make_identity(nc, identity[:])
 
         wgs_sb = place("wgs_sb", [P, PACK * S], F32, AT_WGS)
-        for lo, hi in ((BANK, S), (S, 2 * S), (2 * S, 3 * S), (3 * S, 4 * S), (0, BANK)):
+        for lo, hi in ((BANK, 3 * BANK), (3 * BANK, 5 * BANK), (5 * BANK, PACK * S), (0, BANK)):
             for quadrant in (0, 2, 1, 3):
                 nc.sync.dma_start(wgs_sb[QUADRANT * quadrant : QUADRANT * (quadrant + 1), lo:hi], wgs_rows[:, lo:hi])
         w4_high_raw = load_w4("w4_high_raw", 1, AT_W4_HIGH_RAW)
 
         by_tile = shelf.rearrange("(b q t) c -> b t q c", b=H_PASSES, t=PACK)
-        pairs = [place("pairs%d" % b, [P, 2 * T2], F32, AT_PAIRS[b]) for b in range(H_PASSES)]
+        pairs = place("pairs", [P, 2 * T2], F32, AT_PAIRS)
+        z_rows = [place("z_rows%d" % b, [P, width * T2], BF16, AT_Z_ROWS[b]) for b, width in enumerate((PACK, 2))]
         shelf_sb = {}
 
         def shelf_rows(i):
-            b, t = divmod(i, PACK)
             if i not in shelf_sb and i in AT_SHELF:
                 shelf_sb[i] = place("shelf%d" % i, [P, T2], F32, AT_SHELF[i])[:]
             elif i not in shelf_sb:
-                shelf_sb[i] = pairs[b][:, T2:]
+                shelf_sb[i] = pairs[:, T2:]
             return shelf_sb[i]
 
         def load_shelf(i):
@@ -189,12 +189,13 @@ def tile_list_audiobook_banner_scores_kernel(
 
         def z_of(i, lo, hi):
             b, t = divmod(i, PACK)
-            halves = pairs[b][:].bitcast(BF16).rearrange("q (c e) -> q c e", e=2)
-            return halves[:, T2 * (t // 2) + lo : T2 * (t // 2) + hi, t % 2]
+            if i < OWN:
+                return z_rows[b][:, T2 * t + lo : T2 * t + hi]
+            return pairs[:].bitcast(BF16).rearrange("q (c e) -> q c e", e=2)[:, T2 + lo : T2 + hi, t % 2]
 
         ring = place("ring", [P, PACK * S], F32, AT_RING)
         last_two = place("last_two", [P, 2 * S], F32, AT_LAST_TWO)
-        held = pairs[1][:, :T2]
+        held = z_rows[1][:].bitcast(F32)
         factor_first = place("factor_first", [P, BANK], F32, AT_FACTOR_FIRST)
         first_steps = [slice(0, BANK // 2), slice(BANK // 2, BANK)]
         banks = {}
@@ -204,9 +205,9 @@ def tile_list_audiobook_banner_scores_kernel(
                 return last_two[:, S * (i - OWN) : S * (i - OWN + 1)]
             return ring[:, S * (i % PACK) : S * (i % PACK + 1)]
 
-        w2_raw = place("w2_raw", [P, H_PASSES * PACK * N], F32, AT_W2_RAW)
         groups = [range(1, 3), range(3, 5), range(5, 8), range(8, 10), range(10, 12), range(12, 16)]
-        hosts = [shelf_rows(1), shelf_rows(3), shelf_rows(PACK), pairs[0][:], shelf_rows(2), w2_raw[:]]
+        words0 = z_rows[0][:].bitcast(F32)
+        hosts = [shelf_rows(1), shelf_rows(3), shelf_rows(2), words0[:, BANK:], held, words0[:, 2 * S :]]
 
         def factor_of(u):
             j = max(j for j, group in enumerate(groups) if group[0] <= u)
@@ -266,14 +267,18 @@ def tile_list_audiobook_banner_scores_kernel(
         def shelf_product(i, lo=0, hi=T2):
             nc.gpsimd.tensor_tensor(z_of(i, lo, hi), pages[i % PAGES][:, lo:hi], shelf_sb[i][:, lo:hi], MULT)
 
-        grouped = {}
+        grouped = [place("grouped%d" % b, [P, PACK * T2], BF16, AT_GROUPED[b]) for b in range(H_PASSES)]
 
-        def merge(b, lo, hi):
-            if b not in grouped:
-                grouped[b] = place("grouped%d" % b, [P, PACK * T2], BF16, AT_GROUPED[b])
+        def interleave(dst, rows, count, lo, hi):
             nc.scalar.copy(
-                grouped[b][:, PACK * lo : PACK * hi].bitcast(U32).rearrange("q (c w) -> q c w", w=2),
-                pairs[b][:].bitcast(U32).rearrange("q (w c) -> q c w", w=2)[:, lo:hi, :],
+                dst[:, count * lo : count * hi].rearrange("q (c i t) -> q c t i", i=RUN, t=count),
+                rows[:].rearrange("q (t c) -> q t c", t=count)[:, :, lo:hi].rearrange("q t (c i) -> q c t i", i=RUN),
+            )
+
+        def merge(lo, hi):
+            nc.scalar.copy(
+                grouped[1][:, PACK * lo : PACK * hi].bitcast(U32).rearrange("q (c w) -> q c w", w=2),
+                pairs[:].bitcast(U32).rearrange("q (w c) -> q c w", w=2)[:, lo:hi, :],
             )
 
         first_banks = [bank("first%d" % e, index)[:, : BANK // 2] for e, index in enumerate((4, 6))]
@@ -287,7 +292,7 @@ def tile_list_audiobook_banner_scores_kernel(
         shelve(0, 0, BANK)
         for j in range(3):
             gains(j)
-        for i in (0, 1, 3, PACK):
+        for i in range(PACK):
             load_shelf(i)
         base_sb = place("base_sb", [P, N_TILES], F32, AT_BASE)
         with nc.allow_non_contiguous_dma(reason="one bias value a partition"):
@@ -300,19 +305,19 @@ def tile_list_audiobook_banner_scores_kernel(
         features(1)
         shelve(1)
         gains(4)
-        load_shelf(2)
         shelf_product(1)
         load_shelf(LAST)
         features(2)
         shelve(2)
         gains(5)
-        w2_by_pass = w2_raw[:].rearrange("q (b c) -> q b c", b=H_PASSES)
-        nc.sync.dma_start(w2_by_pass, w2.rearrange("(b q t) n -> q b (t n)", b=H_PASSES, t=PACK))
+        w2_raw = place("w2_raw", [P, H_PASSES, PACK * N], F32, AT_W2_RAW)
+        nc.sync.dma_start(w2_raw[:], w2.rearrange("(b q t) n -> q b (t n)", b=H_PASSES, t=PACK))
         wgo_sb = place("wgo_sb", [P, PICKS], F32, AT_WGO)
         nc.sync.dma_start(wgo_sb[:], wgo)
         features(3)
         shelve(3)
         shelf_product(2)
+        load_shelf(PACK)
         nc.gpsimd.tensor_tensor(last_two[:], last_two[:], held, MULT)
 
         turned = place("turned", [P, SHARED], F32, AT_TURNED)
@@ -337,15 +342,16 @@ def tile_list_audiobook_banner_scores_kernel(
         for b in range(H_PASSES):
             nc.scalar.copy(
                 w2_grouped[:].rearrange("q (n b c i t) -> q b n c t i", b=H_PASSES, n=N_TILES, i=RUN, t=PACK)[:, b],
-                w2_by_pass[:, b, :].rearrange("q (t n c i) -> q n c t i", t=PACK, n=N_TILES, i=RUN),
+                w2_raw[:, b, :].rearrange("q (t n c i) -> q n c t i", t=PACK, n=N_TILES, i=RUN),
             )
         for lo in range(0, T2, S):
-            merge(0, lo, lo + S)
+            interleave(grouped[0], z_rows[0], PACK, lo, lo + S)
         shelve(5)
         shelf_product(4)
         load_shelf(OWN)
         shelve(OWN)
         shelf_product(5)
+        interleave(pairs[:, :T2].bitcast(BF16), z_rows[1], 2, 0, T2)
         shelve(LAST)
         for lo in range(0, T2, S):
             shelf_product(OWN, lo, lo + S)
@@ -401,7 +407,7 @@ def tile_list_audiobook_banner_scores_kernel(
                 end = min(hi, SHARED)
                 rows_last = shelf_banks[lo // BANK][:, lo % BANK : lo % BANK + end - lo]
                 nc.vector.tensor_tensor(z_of(LAST, lo, end), rows_last, pages[LAST % PAGES][:, lo:end], MULT)
-            merge(1, lo, hi)
+            merge(lo, hi)
 
         pieces = (0, BANK, 2 * BANK, 3 * BANK, T2 - BANK // 2, T2)
         for lo, hi in zip(pieces, pieces[1:]):

@@ -50,7 +50,7 @@ AT_RING, AT_LAST_TWO = 108, 190
 AT_WGS_FIRST, AT_BASE, AT_WGO = 230, 230, 232
 AT_TURNED, AT_IDENTITY, AT_SQUARES = 145, 153, 232
 AT_GROUPED = (154, 170)
-AT_TAB_SCALES, AT_PICKED, AT_W4_SCALES = 154, 91.5, 159
+AT_TAB_SCALES, AT_PICKED, AT_W4_SCALES = 154, 158, 159
 AT_Z_CODES, AT_W2_CODES = 206, (202, 170, 172)
 AT_W2_RAW, AT_FACTOR_FIRST = 52, 228
 AT_Z_SCALE, AT_W2_SCALE = (76, 78), (194, 80)
@@ -123,6 +123,8 @@ def tile_list_audiobook_banner_scores_kernel(
         nc.vector.memset(scales1[:].bitcast(I32), 0)
         pages = [place("page0", [P, T2], F32, AT_PAGE[0])]
         nc.gpsimd.memset(pages[0][:], 0.0)
+        banners = [place("banner0", [P, T2], F32, AT_BANNER[0])]
+        nc.gpsimd.memset(banners[0][:], 0.0)
 
         picked_scales = place("picked_scales", [P, S], U8, AT_PICKED)
         staged = place("staged", [P, 2 * S], U8, AT_STAGED)
@@ -161,8 +163,6 @@ def tile_list_audiobook_banner_scores_kernel(
             page = place("page%d" % i, [P, T2], F32, AT_PAGE[i])
             nc.gpsimd.memset(page[:], 0.0)
             pages.append(page)
-        banners = [place("banner0", [P, T2], F32, AT_BANNER[0])]
-        nc.gpsimd.memset(banners[0][:], 0.0)
         identity = place("identity", [P, P], F32, AT_IDENTITY)
         make_identity(nc, identity[:])
 

@@ -248,18 +248,22 @@ def tile_list_audiobook_banner_scores_kernel(
             banks[i, h] = acc
 
         def gains(j):
-            for u in sorted(groups[j], key=lambda u: u % 2) if j == 0 else groups[j]:
-                product(*divmod(u, 2))
-            width = BANK * len(groups[j])
-            at = BANK * groups[j][0] % (PACK * S)
-            gain = last_two[:] if groups[j][0] == 2 * OWN else ring[:, at : at + width]
-            nc.gpsimd.tensor_tensor(gain, hosts[j][:, :width], wgs_sb[:, at : at + width], MULT)
+            runs = [[u] for u in reversed(groups[0])] if j == 0 else [groups[j]]
+            for run in runs:
+                for u in run:
+                    product(*divmod(u, 2))
+                width = BANK * len(run)
+                at = BANK * run[0] % (PACK * S)
+                within = BANK * (run[0] - groups[j][0])
+                gain = last_two[:] if run[0] == 2 * OWN else ring[:, at : at + width]
+                gain = factor_first[:] if run[0] == 2 else gain
+                nc.gpsimd.tensor_tensor(gain, hosts[j][:, within : within + width], wgs_sb[:, at : at + width], MULT)
 
         def features(j):
             for u in groups[j]:
                 i, h = divmod(u, 2)
                 dst = feature_rows(i)[:, BANK * h : BANK * (h + 1)]
-                nc.vector.tensor_tensor(dst, banks[i, h][:], dst, MULT)
+                nc.vector.tensor_tensor(dst, banks[i, h][:], factor_first[:] if u == 2 else dst, MULT)
 
         def shelve(i, lo=0, hi=S):
             nc.vector.tensor_copy(pages[i % PAGES][:].indirect(part(shelved, lo, hi)), feature_rows(i)[:, lo:hi])

@@ -48,7 +48,7 @@ AT_BANNER = (92, 100)
 AT_W2_GROUPED = 100
 AT_RING, AT_LAST_TWO = 108, 190
 AT_WGS_FIRST, AT_BASE, AT_WGO = 230, 230, 232
-AT_TURNED, AT_IDENTITY, AT_SQUARES = 145, 153, 232
+AT_TURNED, AT_IDENTITY, AT_SQUARES = 145, 158.25, 232
 AT_GROUPED = (154, 170)
 AT_TAB_SCALES, AT_PICKED, AT_W4_SCALES = 154, 158, 159
 AT_Z_CODES, AT_W2_CODES = 206, (202, 170, 172)
@@ -85,7 +85,7 @@ def tile_list_audiobook_banner_scores_kernel(
         def load_scale_rows(name, src, width, kib):
             rows = place(name, [P, width], U8, kib)
             nc.sync.dma_start(rows[SCALES_AT:, :].bitcast(I32), src.rearrange("a r n -> r a n").bitcast(I32))
-            nc.vector.memset(rows[:SCALES_AT, :].bitcast(I32), 0)
+            nc.gpsimd.memset(rows[:SCALES_AT, :].bitcast(I32), 0)
             return rows
 
         def load_w4(name, b, kib):
@@ -120,11 +120,11 @@ def tile_list_audiobook_banner_scores_kernel(
         banner_slots = load_list("banner_slots", offs4)
 
         scales1 = place("scales1", [P, K_PASSES * 2 * S], U8, AT_SCALES)
-        nc.vector.memset(scales1[:].bitcast(I32), 0)
+        nc.gpsimd.memset(scales1[:].bitcast(I32), 0)
         pages = [place("page0", [P, T2], F32, AT_PAGE[0])]
         nc.gpsimd.memset(pages[0][:], 0.0)
         banners = [place("banner0", [P, T2], F32, AT_BANNER[0])]
-        nc.gpsimd.memset(banners[0][:], 0.0)
+        nc.vector.memset(banners[0][:], 0.0)
 
         picked_scales = place("picked_scales", [P, S], U8, AT_PICKED)
         staged = place("staged", [P, 2 * S], U8, AT_STAGED)
@@ -141,7 +141,7 @@ def tile_list_audiobook_banner_scores_kernel(
         double_wgs_first(2 * QUADRANT)
         nc.vector.tensor_copy(staged[:, S:].bitcast(I32), picked_scales[:].bitcast(I32))
         rows = K_PASSES * SCALE_ROWS
-        for quadrant in range(QUADRANTS):
+        for quadrant in (0, 2, 1, 3):
             nc.scalar.dma_start(
                 scales1[QUADRANT * quadrant : QUADRANT * quadrant + SCALE_ROWS, :].bitcast(I32),
                 staged[SCALES_AT + rows * quadrant : SCALES_AT + rows * (quadrant + 1), :].bitcast(I32),

@@ -23,6 +23,7 @@ QUADRANTS = P // QUADRANT
 SCALE_ROWS = 4
 PACK = 4
 BANK = 512
+STEP = BANK // 2
 PER_COLUMN = 16
 K_PASSES = K // (P * PACK)
 H_PASSES = H // (P * PACK)
@@ -32,31 +33,35 @@ N_TILES = N // P
 PAGES = 3
 RUN = 4
 SCALES_AT = P - K_PASSES * QUADRANTS * SCALE_ROWS
-OWN = 6
+OWN = 12
 SHARED = 5 * BANK // 2
+EARLY_W4, EARLY_V = 2 * P, BANK
+EARLY = EARLY_W4 + EARLY_V
+LATE = 2 * S - EARLY
 
 AT_CUB = 0
-AT_W4_HIGH_RAW, AT_WGS = 1, 3
-AT_TABLE = (2, 19)
-AT_Z_ROWS, AT_PAIRS = (19, 206), 124
-AT_SHELF = {0: 222, 1: 35, 3: 43, 5: 43, 7: 35}
-AT_STAGED = 50
-AT_CODES, AT_W4, AT_SCALES = 52, 60, 64
-AT_PAGE = (68, 76, 84)
-AT_W4_LOW_RAW = 83
-AT_BANNER = (92, 100)
-AT_W2_GROUPED = 100
-AT_RING, AT_LAST_TWO = 108, 190
-AT_WGS_FIRST, AT_BASE, AT_WGO = 230, 230, 232
-AT_TURNED, AT_IDENTITY, AT_SQUARES = 145, 158.25, 232
-AT_GROUPED = (154, 170)
-AT_TAB_SCALES, AT_PICKED, AT_W4_SCALES = 154, 158, 159
-AT_Z_CODES, AT_W2_CODES = 206, (202, 170, 172)
-AT_W2_RAW, AT_FACTOR_FIRST = 52, 228
-AT_Z_SCALE, AT_W2_SCALE = (76, 78), (194, 80)
-AT_Y = (3, 3, 186, 222)
-AT_PICKS = (108, 116, 132, 43)
-AT_SCORE = (112, 170, 172, 136, 47)
+AT_WGS, AT_TAB_SCALES, AT_PICKED, AT_W4_SCALES, AT_W4_LOW_RAW = 1, 2, 0, 6, 7
+AT_TABLE = (15, 31)
+AT_STAGED_LATE, AT_IDENTITY, AT_SQUARES = 17, 19.5, 22
+AT_LATE = 230
+AT_W4_HIGH_RAW = 31
+AT_CODES, AT_W4, AT_EARLY, AT_STAGED = (47, 51), (55, 57), 59, 61
+AT_PAGE = (63, 71, 79)
+AT_BANNER = (87, 9)
+AT_FEATURES = (95, 111)
+AT_PAIRS = (119, 135)
+AT_ODD_SHELF, AT_SHELF_5, AT_SHELF_LAST = 151, 1, 22
+AT_TURNED, AT_WGS_FIRST, AT_BASE = 159, 164, 168
+AT_FACTOR_FIRST, AT_GAIN_FIRST = (166, 168), 168
+AT_Z_ROWS = 222
+AT_W2_RAW, AT_W2_GROUPED, AT_WGO = 47, 9, 47
+AT_GROUPED = (31, 119)
+AT_Z_CODES, AT_Z_SCALE = (111, 151), (71, 73)
+AT_W2_CODES, AT_W2_SCALE = (99, 119, 121), (100, 75)
+AT_Y = (170, 170, 178, 186)
+AT_PICKS = (194, 198, 202, 206)
+AT_SCORE = (210, 119, 121, 214, 218)
+BANK_OF = (None, 3, 2, 4, 5, 6, 7, 0, 1, 2, 3, 4, 5, 6, 5, 7)
 
 
 def tile_list_audiobook_banner_scores_kernel(
@@ -94,7 +99,7 @@ def tile_list_audiobook_banner_scores_kernel(
             return raw
 
         def deal(copy, b, raw):
-            dealt = place("w4_dealt%d" % b, [P, K_PASSES, H], U8, AT_W4 + 2 * b)
+            dealt = place("w4_dealt%d" % b, [P, K_PASSES, H], U8, AT_W4[b])
             copy(
                 dealt[:].bitcast(U16).rearrange("q a (t m) -> q a t m", m=P),
                 raw[:].bitcast(U16).rearrange("q a (m t) -> q a t m", t=PACK),
@@ -109,55 +114,73 @@ def tile_list_audiobook_banner_scores_kernel(
         nc.sync.dma_start(wgs_first[:QUADRANT, :], wgs_rows[:, :BANK])
         w4_low_raw = load_w4("w4_low_raw", 0, AT_W4_LOW_RAW)
         shelved = load_list("shelved", offs2)
-        tab_sb = []
-        for a in range(K_PASSES):
+
+        def load_table(a):
             words = place("tab_sb%d" % a, [P, T], U32, AT_TABLE[a])
             nc.sync.dma_start(words[:].bitcast(I32), tab_words[a].rearrange("q n t -> q (n t)").bitcast(I32))
-            tab_sb.append(words)
-        cub_sb = place("cub_sb", [P, H_PASSES, PACK], F32, AT_CUB)
-        nc.sync.dma_start(cub_sb[:], cub.rearrange("(b q t) -> q b t", b=H_PASSES, t=PACK))
+            return words
+
+        tab_sb = [load_table(0)]
         promoted = load_list("promoted", offs3)
         banner_slots = load_list("banner_slots", offs4)
+        tab_sb.append(load_table(1))
 
-        scales1 = place("scales1", [P, K_PASSES * 2 * S], U8, AT_SCALES)
-        nc.gpsimd.memset(scales1[:].bitcast(I32), 0)
+        early = place("early", [P, K_PASSES * EARLY], U8, AT_EARLY)
+        nc.gpsimd.memset(early[:].bitcast(I32), 0)
+        late = place("late", [P, K_PASSES * LATE], U8, AT_LATE)
+        nc.gpsimd.memset(late[:].bitcast(I32), 0)
         pages = [place("page0", [P, T2], F32, AT_PAGE[0])]
         nc.gpsimd.memset(pages[0][:], 0.0)
         banners = [place("banner0", [P, T2], F32, AT_BANNER[0])]
         nc.vector.memset(banners[0][:], 0.0)
 
-        picked_scales = place("picked_scales", [P, S], U8, AT_PICKED)
-        staged = place("staged", [P, 2 * S], U8, AT_STAGED)
-        nc.vector.tensor_copy(picked_scales[:], tab_scale_sb[:].indirect(listed[:]))
+        picked_scales = place("picked_scales", [P, 2 * S], U8, AT_PICKED)[:, :S]
+        staged = place("staged", [P, EARLY_V + H], U8, AT_STAGED)
+        nc.vector.tensor_copy(picked_scales, tab_scale_sb[:].indirect(listed[:]))
 
         def double_wgs_first(filled):
             nc.vector.tensor_copy(wgs_first[filled : 2 * filled, :].bitcast(I32), wgs_first[:filled, :].bitcast(I32))
 
         double_wgs_first(QUADRANT)
         nc.vector.tensor_copy(
-            staged[:, :S].rearrange("q (b t m) -> q b t m", t=PACK, m=P),
+            staged[:, EARLY_V : EARLY_V + H].rearrange("q (b t m) -> q b t m", t=PACK, m=P),
             w4_scale_raw[:].rearrange("q (b m t) -> q b t m", b=H_PASSES, t=PACK),
         )
         double_wgs_first(2 * QUADRANT)
-        nc.vector.tensor_copy(staged[:, S:].bitcast(I32), picked_scales[:].bitcast(I32))
-        rows = K_PASSES * SCALE_ROWS
-        for quadrant in (0, 2, 1, 3):
-            nc.scalar.dma_start(
-                scales1[QUADRANT * quadrant : QUADRANT * quadrant + SCALE_ROWS, :].bitcast(I32),
-                staged[SCALES_AT + rows * quadrant : SCALES_AT + rows * (quadrant + 1), :].bitcast(I32),
-            )
-        w4_scale = [scales1[:, 2 * S * a : 2 * S * a + S] for a in range(K_PASSES)]
-        v_scale = [scales1[:, 2 * S * a + S : 2 * S * (a + 1)] for a in range(K_PASSES)]
+        nc.vector.tensor_copy(staged[:, :EARLY_V].bitcast(I32), picked_scales[:, :EARLY_V].bitcast(I32))
 
+        def move_scales(queue, planes, source):
+            rows = K_PASSES * SCALE_ROWS
+            for quadrant in (0, 2, 1, 3):
+                queue.dma_start(
+                    planes[QUADRANT * quadrant : QUADRANT * quadrant + SCALE_ROWS, :].bitcast(I32),
+                    source[SCALES_AT + rows * quadrant : SCALES_AT + rows * (quadrant + 1), :].bitcast(I32),
+                )
+
+        move_scales(nc.scalar, early, staged[:, :EARLY])
         w4_dealt = {0: deal(nc.vector.tensor_copy, 0, w4_low_raw)}
 
-        v_codes = []
-        for a in range(K_PASSES):
-            codes = place("v_codes%d" % a, [P, S], U32, AT_CODES + 4 * a)
-            cuts = (0, S) if a < K_PASSES - 1 else (0, BANK // 2, BANK, S)
-            for lo, hi in zip(cuts, cuts[1:]):
-                nc.vector.tensor_copy(codes[:, lo:hi], tab_sb[a][:].indirect(part(listed, lo, hi)))
-            v_codes.append(codes)
+        codes = [place("v_codes%d" % a, [P, S], U32, AT_CODES[a]) for a in range(K_PASSES)]
+        nc.vector.tensor_copy(codes[0][:], tab_sb[0][:].indirect(listed[:]))
+        staged_late = place("staged_late", [P, LATE], U8, AT_STAGED_LATE)
+        nc.vector.tensor_copy(staged_late[:, : H - EARLY_W4].bitcast(I32), staged[:, EARLY:].bitcast(I32))
+        nc.vector.tensor_copy(staged_late[:, H - EARLY_W4 :].bitcast(I32), picked_scales[:, EARLY_V:].bitcast(I32))
+        move_scales(nc.sync, late, staged_late[:])
+        cub_sb = place("cub_sb", [P, H_PASSES, PACK], F32, AT_CUB)
+        nc.scalar.dma_start(cub_sb[:], cub.rearrange("(b q t) -> q b t", b=H_PASSES, t=PACK))
+        for lo, hi in ((0, STEP), (STEP, BANK), (BANK, S)):
+            nc.vector.tensor_copy(codes[1][:, lo:hi], tab_sb[1][:].indirect(part(listed, lo, hi)))
+
+        def w4_scale(a, i):
+            at = P * i - EARLY_W4
+            if at < 0:
+                return early[:, EARLY * (a + 1) + at : EARLY * (a + 1) + at + P]
+            return late[:, LATE * a + at : LATE * a + at + P]
+
+        def v_scale(a, lo, hi):
+            if hi <= EARLY_V:
+                return early[:, EARLY * a + lo : EARLY * a + hi]
+            return late[:, LATE * (a + 1) - S + lo : LATE * (a + 1) - S + hi]
 
         for i in range(1, PAGES):
             page = place("page%d" % i, [P, T2], F32, AT_PAGE[i])
@@ -170,65 +193,48 @@ def tile_list_audiobook_banner_scores_kernel(
         for lo, hi in ((BANK, 3 * BANK), (3 * BANK, 5 * BANK), (5 * BANK, PACK * S), (0, BANK)):
             for quadrant in (0, 2, 1, 3):
                 nc.sync.dma_start(wgs_sb[QUADRANT * quadrant : QUADRANT * (quadrant + 1), lo:hi], wgs_rows[:, lo:hi])
-        w4_high_raw = load_w4("w4_high_raw", 1, AT_W4_HIGH_RAW)
 
         by_tile = shelf.rearrange("(b q t) c -> b t q c", b=H_PASSES, t=PACK)
-        pairs = place("pairs", [P, 2 * T2], F32, AT_PAIRS)
-        z_rows = [place("z_rows%d" % b, [P, width * T2], BF16, AT_Z_ROWS[b]) for b, width in enumerate((PACK, 2))]
-        shelf_sb = {}
-
-        def shelf_rows(i):
-            if i not in shelf_sb and i in AT_SHELF:
-                shelf_sb[i] = place("shelf%d" % i, [P, T2], F32, AT_SHELF[i])[:]
-            elif i not in shelf_sb:
-                shelf_sb[i] = pairs[:, T2:]
-            return shelf_sb[i]
+        pairs = [place("pairs%d" % b, [P, 2 * T2], F32, AT_PAIRS[b]) for b in range(H_PASSES)]
+        odd_shelf = place("odd_shelf", [P, T2], F32, AT_ODD_SHELF)
+        z_rows = place("z_rows", [P, 2 * T2], BF16, AT_Z_ROWS)
+        shelf_sb = {0: pairs[0][:, :T2], 1: odd_shelf[:], 2: pairs[0][:, T2:], 3: odd_shelf[:], 4: pairs[1][:, :T2], 6: pairs[1][:, T2:]}
 
         def load_shelf(i):
-            nc.sync.dma_start(shelf_rows(i), by_tile[i // PACK, i % PACK])
+            if i not in shelf_sb:
+                shelf_sb[i] = place("shelf%d" % i, [P, T2], F32, AT_SHELF_LAST if i == LAST else AT_SHELF_5)[:]
+            nc.sync.dma_start(shelf_sb[i], by_tile[i // PACK, i % PACK])
 
         def z_of(i, lo, hi):
             b, t = divmod(i, PACK)
-            if i < OWN:
-                return z_rows[b][:, T2 * t + lo : T2 * t + hi]
-            return pairs[:].bitcast(BF16).rearrange("q (c e) -> q c e", e=2)[:, T2 + lo : T2 + hi, t % 2]
+            if i in (4, 5):
+                return z_rows[:, T2 * t + lo : T2 * t + hi]
+            at = T2 * (t // 2)
+            return pairs[b][:].bitcast(BF16).rearrange("q (c e) -> q c e", e=2)[:, at + lo : at + hi, t % 2]
 
-        ring = place("ring", [P, PACK * S], F32, AT_RING)
-        last_two = place("last_two", [P, 2 * S], F32, AT_LAST_TWO)
-        held = z_rows[1][:].bitcast(F32)
-        factor_first = place("factor_first", [P, BANK], F32, AT_FACTOR_FIRST)
-        first_steps = [slice(0, BANK // 2), slice(BANK // 2, BANK)]
-        banks = {}
-
-        def feature_rows(i):
-            if i >= OWN:
-                return last_two[:, S * (i - OWN) : S * (i - OWN + 1)]
-            return ring[:, S * (i % PACK) : S * (i % PACK + 1)]
-
-        groups = [range(1, 3), range(3, 5), range(5, 8), range(8, 10), range(10, 12), range(12, 16)]
-        words0 = z_rows[0][:].bitcast(F32)
-        hosts = [shelf_rows(1), shelf_rows(3), shelf_rows(2), words0[:, BANK:], held, words0[:, 2 * S :]]
-
-        def factor_of(u):
-            j = max(j for j, group in enumerate(groups) if group[0] <= u)
-            e = u - groups[j][0]
-            return hosts[j][:, BANK * e : BANK * (e + 1)]
-
-        def first_product(acc, i, cols, order):
-            b, t = divmod(i, PACK)
-            for a in order:
-                nc.tensor.matmul_mx(
-                    out=acc,
-                    lhsT=w4_dealt[b][:, a, 2 * P * t : 2 * P * (t + 1)].bitcast(FP4X4),
-                    lhsT_scale=w4_scale[a][:, P * i : P * (i + 1)],
-                    rhs=v_codes[a][:, cols].bitcast(FP8X4),
-                    rhs_scale=v_scale[a][:, cols],
-                    start=(a == order[0]),
-                    stop=(a == order[1]),
-                )
-
+        rows_low = place("rows_low", [P, PACK * S], F32, AT_FEATURES[0])
+        rows_mid = place("rows_mid", [P, 2 * S], F32, AT_FEATURES[1])
+        held = shelf_sb[6]
         squares = place("squares", [P, 2 * BANK], F32, AT_SQUARES)
         made = []
+        banks = {}
+
+        def feature_cols(u, count):
+            if u in range(8, 12):
+                return rows_mid[:, BANK * (u - 8) : BANK * (u - 8 + count)]
+            return rows_low[:, BANK * (u % 12) : BANK * (u % 12 + count)]
+
+        def first_pass(acc, i, a, moving, lo, hi, start, stop):
+            b, t = divmod(i, PACK)
+            nc.tensor.matmul_mx(
+                out=acc,
+                lhsT=w4_dealt[b][:, a, 2 * P * t : 2 * P * (t + 1)].bitcast(FP4X4),
+                lhsT_scale=w4_scale(a, i),
+                rhs=moving.bitcast(FP8X4),
+                rhs_scale=v_scale(a, lo, hi),
+                start=start,
+                stop=stop,
+            )
 
         def make_factor(factor, acc, i):
             b, t = divmod(i, PACK)
@@ -238,130 +244,132 @@ def tile_list_audiobook_banner_scores_kernel(
             nc.scalar.activation(square, acc, ACT.Square)
             nc.scalar.activation(factor, square, ACT.Identity, bias=1.0, scale=cub_sb[:, b, t : t + 1])
 
-        def product(i, h):
-            acc = bank("p%d_%d" % (i, h), 2 * (i % PACK) + h)
-            first_product(acc[:], i, slice(BANK * h, BANK * (h + 1)), (1, 0))
-            make_factor(factor_of(2 * i + h), acc[:], i)
-            if i >= OWN:
-                at = S * (i - OWN) + BANK * h
-                nc.scalar.copy(held[:, at : at + BANK], acc[:])
-            banks[i, h] = acc
+        first_banks = [bank("first%d" % e, e)[:, :STEP] for e in range(2)]
+        first_factors = [place("factor_first%d" % e, [P, BANK], F32, AT_FACTOR_FIRST[e])[:, :STEP] for e in range(2)]
+        first_rows = [rows_low[:, STEP * e : STEP * (e + 1)] for e in range(2)]
+        for e in range(2):
+            lo, hi = STEP * e, STEP * (e + 1)
+            for a in range(K_PASSES):
+                first_pass(first_banks[e], 0, a, codes[a][:, lo:hi], lo, hi, a == 0, a == K_PASSES - 1)
+            make_factor(first_factors[e], first_banks[e], 0)
+        for e in range(2):
+            nc.vector.tensor_tensor(first_rows[e], first_banks[e], wgs_first[:, STEP * e : STEP * (e + 1)], MULT)
+        for e in range(2):
+            nc.vector.tensor_tensor(first_rows[e], first_rows[e], first_factors[e], MULT)
+        gain_first = place("gain_first", [P, BANK], F32, AT_GAIN_FIRST)
+        w4_high_raw = load_w4("w4_high_raw", 1, AT_W4_HIGH_RAW)
 
-        def gains(j):
-            runs = [[u] for u in reversed(groups[0])] if j == 0 else [groups[j]]
-            for run in runs:
-                for u in run:
-                    product(*divmod(u, 2))
-                width = BANK * len(run)
-                at = BANK * run[0] % (PACK * S)
-                within = BANK * (run[0] - groups[j][0])
-                gain = last_two[:] if run[0] == 2 * OWN else ring[:, at : at + width]
-                gain = factor_first[:] if run[0] == 2 else gain
-                nc.gpsimd.tensor_tensor(gain, hosts[j][:, within : within + width], wgs_sb[:, at : at + width], MULT)
+        def product(u, factor):
+            i, h = divmod(u, 2)
+            acc = bank("p%d" % u, BANK_OF[u])
+            lo, hi = BANK * h, BANK * (h + 1)
+            for a in (1, 0):
+                first_pass(acc[:], i, a, codes[a][:, lo:hi], lo, hi, a == 1, a == 0)
+            make_factor(factor, acc[:], i)
+            if u >= OWN:
+                nc.scalar.copy(held[:, BANK * (u - OWN) : BANK * (u - OWN + 1)], acc[:])
+            banks[u] = acc
 
-        def features(j):
-            for u in groups[j]:
-                i, h = divmod(u, 2)
-                dst = feature_rows(i)[:, BANK * h : BANK * (h + 1)]
-                nc.vector.tensor_tensor(dst, banks[i, h][:], factor_first[:] if u == 2 else dst, MULT)
+        def gains(first, count, host, gain):
+            for e in range(count):
+                product(first + e, host[:, BANK * e : BANK * (e + 1)])
+            at = BANK * first % (PACK * S)
+            nc.gpsimd.tensor_tensor(gain, host[:, : BANK * count], wgs_sb[:, at : at + BANK * count], MULT)
+
+        def features(first, count):
+            for u in range(first, first + count):
+                nc.vector.tensor_tensor(feature_cols(u, 1), banks[u][:], gain_first[:] if u == 2 else feature_cols(u, 1), MULT)
 
         def shelve(i, lo=0, hi=S):
-            nc.vector.tensor_copy(pages[i % PAGES][:].indirect(part(shelved, lo, hi)), feature_rows(i)[:, lo:hi])
+            nc.vector.tensor_copy(pages[i % PAGES][:].indirect(part(shelved, lo, hi)), feature_cols(2 * i, 2)[:, lo:hi])
 
         def shelf_product(i, lo=0, hi=T2):
             nc.gpsimd.tensor_tensor(z_of(i, lo, hi), pages[i % PAGES][:, lo:hi], shelf_sb[i][:, lo:hi], MULT)
 
-        grouped = [place("grouped%d" % b, [P, PACK * T2], BF16, AT_GROUPED[b]) for b in range(H_PASSES)]
+        grouped = {}
 
-        def interleave(dst, rows, count, lo, hi):
+        def merge(b, lo, hi):
+            if b not in grouped:
+                grouped[b] = place("grouped%d" % b, [P, PACK * T2], BF16, AT_GROUPED[b])
             nc.scalar.copy(
-                dst[:, count * lo : count * hi].rearrange("q (c i t) -> q c t i", i=RUN, t=count),
-                rows[:].rearrange("q (t c) -> q t c", t=count)[:, :, lo:hi].rearrange("q t (c i) -> q c t i", i=RUN),
+                grouped[b][:, PACK * lo : PACK * hi].bitcast(U32).rearrange("q (c w) -> q c w", w=2),
+                pairs[b][:].bitcast(U32).rearrange("q (w c) -> q c w", w=2)[:, lo:hi, :],
             )
 
-        def merge(lo, hi):
-            nc.scalar.copy(
-                grouped[1][:, PACK * lo : PACK * hi].bitcast(U32).rearrange("q (c w) -> q c w", w=2),
-                pairs[:].bitcast(U32).rearrange("q (w c) -> q c w", w=2)[:, lo:hi, :],
-            )
-
-        first_banks = [bank("first%d" % e, index)[:, : BANK // 2] for e, index in enumerate((4, 6))]
-        for step, acc in zip(first_steps, first_banks):
-            first_product(acc, 0, step, (0, 1))
-            make_factor(factor_first[:, step], acc, 0)
-        for step, acc in zip(first_steps, first_banks):
-            nc.vector.tensor_tensor(ring[:, step], acc, wgs_first[:, step], MULT)
-        for step in first_steps:
-            nc.vector.tensor_tensor(ring[:, step], ring[:, step], factor_first[:, step], MULT)
         shelve(0, 0, BANK)
-        for j in range(3):
-            gains(j)
-        for i in range(PACK):
-            load_shelf(i)
+        gains(2, 1, feature_cols(2, 1), gain_first[:])
+        gains(1, 1, feature_cols(1, 1), feature_cols(1, 1))
+        gains(3, 2, shelf_sb[0], feature_cols(3, 2))
+        load_shelf(0)
+        features(2, 1)
+        features(1, 1)
+        shelve(0, BANK, S)
         base_sb = place("base_sb", [P, N_TILES], F32, AT_BASE)
         with nc.allow_non_contiguous_dma(reason="one bias value a partition"):
             nc.sync.dma_start(base_sb[:], base.rearrange("(c q) -> q c", q=P))
-        features(0)
-        shelve(0, BANK, S)
+        gains(5, 3, shelf_sb[1], feature_cols(5, 3))
+        load_shelf(1)
         w4_dealt[1] = deal(nc.scalar.copy, 1, w4_high_raw)
-        gains(3)
-        shelf_product(0)
-        features(1)
+        features(3, 2)
         shelve(1)
-        gains(4)
-        shelf_product(1)
-        load_shelf(LAST)
-        features(2)
+        shelf_product(0)
+        gains(8, 4, shelf_sb[2], feature_cols(8, 4))
+        load_shelf(2)
+        features(5, 3)
         shelve(2)
-        gains(5)
+        shelve(3)
+        shelf_product(1)
+        load_shelf(3)
+        gains(12, 4, shelf_sb[4], feature_cols(12, 4))
+        load_shelf(LAST)
         w2_raw = place("w2_raw", [P, H_PASSES, PACK * N], F32, AT_W2_RAW)
         nc.sync.dma_start(w2_raw[:], w2.rearrange("(b q t) n -> q b (t n)", b=H_PASSES, t=PACK))
-        wgo_sb = place("wgo_sb", [P, PICKS], F32, AT_WGO)
-        nc.sync.dma_start(wgo_sb[:], wgo)
-        features(3)
-        shelve(3)
+        load_shelf(4)
+        load_shelf(5)
+        features(8, 4)
+        shelve(4)
         shelf_product(2)
-        load_shelf(PACK)
-        nc.gpsimd.tensor_tensor(last_two[:], last_two[:], held, MULT)
+        shelve(5)
+        nc.gpsimd.tensor_tensor(feature_cols(OWN, 4), feature_cols(OWN, 4), held, MULT)
+        load_shelf(6)
 
         turned = place("turned", [P, SHARED], F32, AT_TURNED)
         spans = [(lo, min(lo + BANK, SHARED)) for lo in range(0, SHARED, BANK)]
         for c, (lo, hi) in enumerate(spans):
-            there = bank("there%d" % c, c % 2)
+            there = bank("there%d" % c, 5 + c)
             for at in range(lo, hi, P):
                 nc.tensor.transpose(there[:, at - lo : at - lo + P], shelf_sb[LAST][:, at : at + P], identity[:])
             nc.scalar.copy(turned[:, lo:hi], there[:, : hi - lo])
         shelf_banks = []
         for c, (lo, hi) in enumerate(spans):
-            back = bank("back%d" % c, PACK + c)
+            back = bank("back%d" % c, 5 + c)
             for at in range(lo, hi, P):
                 nc.tensor.transpose(back[:, at - lo : at - lo + P], turned[:, at : at + P], identity[:])
             shelf_banks.append(back)
 
-        features(4)
-        shelve(4)
         shelf_product(3)
-        load_shelf(5)
+        shelve(6)
         w2_grouped = place("w2_grouped", [P, N_TILES * H_PASSES * P * PACK], BF16, AT_W2_GROUPED)
         for b in range(H_PASSES):
             nc.scalar.copy(
                 w2_grouped[:].rearrange("q (n b c i t) -> q b n c t i", b=H_PASSES, n=N_TILES, i=RUN, t=PACK)[:, b],
                 w2_raw[:, b, :].rearrange("q (t n c i) -> q n c t i", t=PACK, n=N_TILES, i=RUN),
             )
+        wgo_sb = place("wgo_sb", [P, PICKS], F32, AT_WGO)
+        nc.sync.dma_start(wgo_sb[:], wgo)
         for lo in range(0, T2, S):
-            interleave(grouped[0], z_rows[0], PACK, lo, lo + S)
-        shelve(5)
+            merge(0, lo, lo + S)
         shelf_product(4)
-        load_shelf(OWN)
-        shelve(OWN)
-        shelf_product(5)
-        interleave(pairs[:, :T2].bitcast(BF16), z_rows[1], 2, 0, T2)
         shelve(LAST)
-        for lo in range(0, T2, S):
-            shelf_product(OWN, lo, lo + S)
+        shelf_product(5)
+        nc.scalar.copy(
+            pairs[1][:, :T2].bitcast(BF16).rearrange("q (c i t) -> q c t i", i=RUN, t=2),
+            z_rows[:].rearrange("q (t c i) -> q c t i", t=2, i=RUN),
+        )
+        shelf_product(6)
         shelf_product(LAST, SHARED, T2)
 
-        z_codes = place("z_codes", [P, H_PASSES, T2], U32, AT_Z_CODES)
+        z_codes = [place("z_codes%d" % b, [P, T2], U32, AT_Z_CODES[b]) for b in range(H_PASSES)]
         z_scale = [place("z_scale%d" % b, [P, T2], U8, AT_Z_SCALE[b]) for b in range(H_PASSES)]
         w2_parts = ((0, 1), (1, 2), (2, N_TILES))
         w2_tiles = {
@@ -385,7 +393,7 @@ def tile_list_audiobook_banner_scores_kernel(
 
         def quantise_z(b, lo, hi):
             nc.vector.quantize_mx(
-                out=z_codes[:, b, lo:hi].bitcast(FP8X4), scales=z_scale[b][:, lo:hi], in_=grouped[b][:, PACK * lo : PACK * hi]
+                out=z_codes[b][:, lo:hi].bitcast(FP8X4), scales=z_scale[b][:, lo:hi], in_=grouped[b][:, PACK * lo : PACK * hi]
             )
 
         def second_pass(acc, n, b, lo, hi):
@@ -396,7 +404,7 @@ def tile_list_audiobook_banner_scores_kernel(
                 out=acc[:, lo % BANK : lo % BANK + hi - lo],
                 lhsT=w2_tiles[first][:, within : within + P].bitcast(FP8X4),
                 lhsT_scale=w2_scale(at, at + P),
-                rhs=z_codes[:, b, lo:hi].bitcast(FP8X4),
+                rhs=z_codes[b][:, lo:hi].bitcast(FP8X4),
                 rhs_scale=z_scale[b][:, lo:hi],
                 start=(b == 0),
                 stop=(b == H_PASSES - 1 and hi % BANK == 0),
@@ -411,7 +419,7 @@ def tile_list_audiobook_banner_scores_kernel(
                 end = min(hi, SHARED)
                 rows_last = shelf_banks[lo // BANK][:, lo % BANK : lo % BANK + end - lo]
                 nc.vector.tensor_tensor(z_of(LAST, lo, end), rows_last, pages[LAST % PAGES][:, lo:end], MULT)
-            merge(lo, hi)
+            merge(1, lo, hi)
 
         pieces = (0, BANK, 2 * BANK, 3 * BANK, T2 - BANK // 2, T2)
         for lo, hi in zip(pieces, pieces[1:]):

@@ -35,17 +35,14 @@ RUN = 4
 SCALES_AT = P - K_PASSES * QUADRANTS * SCALE_ROWS
 OWN = 12
 SHARED = 5 * BANK // 2
-EARLY_W4, EARLY_V = 2 * P, BANK
-EARLY = EARLY_W4 + EARLY_V
-LATE = 2 * S - EARLY
 
 AT_CUB = 0
-AT_WGS, AT_TAB_SCALES, AT_PICKED, AT_W4_SCALES, AT_W4_LOW_RAW = 1, 2, 0, 6, 7
+AT_PLANES = 59
+AT_WGS, AT_TAB_SCALES, AT_PICKED, AT_W4_SCALES, AT_W4_LOW_RAW = 1, 2, 233, 6, 7
 AT_TABLE = (15, 31)
-AT_STAGED_LATE, AT_IDENTITY, AT_SQUARES = 17, 19.5, 22
-AT_LATE = 230
+AT_IDENTITY, AT_SQUARES = 233.5, 22
 AT_W4_HIGH_RAW = 31
-AT_CODES, AT_W4, AT_EARLY, AT_STAGED = (47, 51), (55, 57), 59, 61
+AT_CODES, AT_W4, AT_STAGED = (47, 51), (55, 57), 230
 AT_PAGE = (63, 71, 79)
 AT_BANNER = (87, 9)
 AT_FEATURES = (95, 111)
@@ -121,66 +118,51 @@ def tile_list_audiobook_banner_scores_kernel(
             return words
 
         tab_sb = [load_table(0)]
+        tab_sb.append(load_table(1))
+        cub_sb = place("cub_sb", [P, H_PASSES, PACK], F32, AT_CUB)
+        nc.sync.dma_start(cub_sb[:], cub.rearrange("(b q t) -> q b t", b=H_PASSES, t=PACK))
         promoted = load_list("promoted", offs3)
         banner_slots = load_list("banner_slots", offs4)
-        tab_sb.append(load_table(1))
 
-        early = place("early", [P, K_PASSES * EARLY], U8, AT_EARLY)
-        nc.gpsimd.memset(early[:].bitcast(I32), 0)
-        late = place("late", [P, K_PASSES * LATE], U8, AT_LATE)
-        nc.gpsimd.memset(late[:].bitcast(I32), 0)
+        planes = place("planes", [P, K_PASSES * 2 * S], U8, AT_PLANES)
+        nc.gpsimd.memset(planes[:].bitcast(I32), 0)
         pages = [place("page0", [P, T2], F32, AT_PAGE[0])]
         nc.gpsimd.memset(pages[0][:], 0.0)
         banners = [place("banner0", [P, T2], F32, AT_BANNER[0])]
         nc.vector.memset(banners[0][:], 0.0)
 
-        picked_scales = place("picked_scales", [P, 2 * S], U8, AT_PICKED)[:, :S]
-        staged = place("staged", [P, EARLY_V + H], U8, AT_STAGED)
-        nc.vector.tensor_copy(picked_scales, tab_scale_sb[:].indirect(listed[:]))
+        picked_scales = place("picked_scales", [P, S], U8, AT_PICKED)
+        staged = place("staged", [P, 2 * S], U8, AT_STAGED)
+        nc.vector.tensor_copy(picked_scales[:], tab_scale_sb[:].indirect(listed[:]))
 
         def double_wgs_first(filled):
             nc.vector.tensor_copy(wgs_first[filled : 2 * filled, :].bitcast(I32), wgs_first[:filled, :].bitcast(I32))
 
         double_wgs_first(QUADRANT)
         nc.vector.tensor_copy(
-            staged[:, EARLY_V : EARLY_V + H].rearrange("q (b t m) -> q b t m", t=PACK, m=P),
+            staged[:, :H].rearrange("q (b t m) -> q b t m", t=PACK, m=P),
             w4_scale_raw[:].rearrange("q (b m t) -> q b t m", b=H_PASSES, t=PACK),
         )
         double_wgs_first(2 * QUADRANT)
-        nc.vector.tensor_copy(staged[:, :EARLY_V].bitcast(I32), picked_scales[:, :EARLY_V].bitcast(I32))
-
-        def move_scales(queue, planes, source):
-            rows = K_PASSES * SCALE_ROWS
-            for quadrant in (0, 2, 1, 3):
-                queue.dma_start(
-                    planes[QUADRANT * quadrant : QUADRANT * quadrant + SCALE_ROWS, :].bitcast(I32),
-                    source[SCALES_AT + rows * quadrant : SCALES_AT + rows * (quadrant + 1), :].bitcast(I32),
-                )
-
-        move_scales(nc.scalar, early, staged[:, :EARLY])
+        nc.vector.tensor_copy(staged[:, H:].bitcast(I32), picked_scales[:].bitcast(I32))
+        rows = K_PASSES * SCALE_ROWS
+        for quadrant in (0, 2, 1, 3):
+            nc.scalar.dma_start(
+                planes[QUADRANT * quadrant : QUADRANT * quadrant + SCALE_ROWS, :].bitcast(I32),
+                staged[SCALES_AT + rows * quadrant : SCALES_AT + rows * (quadrant + 1), :].bitcast(I32),
+            )
         w4_dealt = {0: deal(nc.vector.tensor_copy, 0, w4_low_raw)}
 
         codes = [place("v_codes%d" % a, [P, S], U32, AT_CODES[a]) for a in range(K_PASSES)]
         nc.vector.tensor_copy(codes[0][:], tab_sb[0][:].indirect(listed[:]))
-        staged_late = place("staged_late", [P, LATE], U8, AT_STAGED_LATE)
-        nc.vector.tensor_copy(staged_late[:, : H - EARLY_W4].bitcast(I32), staged[:, EARLY:].bitcast(I32))
-        nc.vector.tensor_copy(staged_late[:, H - EARLY_W4 :].bitcast(I32), picked_scales[:, EARLY_V:].bitcast(I32))
-        move_scales(nc.sync, late, staged_late[:])
-        cub_sb = place("cub_sb", [P, H_PASSES, PACK], F32, AT_CUB)
-        nc.scalar.dma_start(cub_sb[:], cub.rearrange("(b q t) -> q b t", b=H_PASSES, t=PACK))
         for lo, hi in ((0, STEP), (STEP, BANK), (BANK, S)):
             nc.vector.tensor_copy(codes[1][:, lo:hi], tab_sb[1][:].indirect(part(listed, lo, hi)))
 
         def w4_scale(a, i):
-            at = P * i - EARLY_W4
-            if at < 0:
-                return early[:, EARLY * (a + 1) + at : EARLY * (a + 1) + at + P]
-            return late[:, LATE * a + at : LATE * a + at + P]
+            return planes[:, 2 * S * a + P * i : 2 * S * a + P * (i + 1)]
 
         def v_scale(a, lo, hi):
-            if hi <= EARLY_V:
-                return early[:, EARLY * a + lo : EARLY * a + hi]
-            return late[:, LATE * (a + 1) - S + lo : LATE * (a + 1) - S + hi]
+            return planes[:, 2 * S * a + H + lo : 2 * S * a + H + hi]
 
         for i in range(1, PAGES):
             page = place("page%d" % i, [P, T2], F32, AT_PAGE[i])

@@ -38,7 +38,7 @@ SHARED = 5 * BANK // 2
 
 AT_CUB = 0
 AT_PLANES = 59
-AT_WGS, AT_TAB_SCALES, AT_PICKED, AT_W4_SCALES, AT_W4_LOW_RAW = 1, 2, 233, 6, 7
+AT_WGS, AT_TAB_SCALES, AT_PICKED, AT_W4_SCALES, AT_W4_LOW_RAW = 1, 2, 233, 6, 78
 AT_TABLE = (15, 31)
 AT_IDENTITY, AT_SQUARES = 233.5, 22
 AT_W4_HIGH_RAW = 31
@@ -226,7 +226,7 @@ def tile_list_audiobook_banner_scores_kernel(
             nc.scalar.activation(square, acc, ACT.Square)
             nc.scalar.activation(factor, square, ACT.Identity, bias=1.0, scale=cub_sb[:, b, t : t + 1])
 
-        first_banks = [bank("first%d" % e, e)[:, :STEP] for e in range(2)]
+        first_banks = [bank("first%d" % e, BANK_OF[4 + 2 * e])[:, :STEP] for e in range(2)]
         first_factors = [place("factor_first%d" % e, [P, BANK], F32, AT_FACTOR_FIRST[e])[:, :STEP] for e in range(2)]
         first_rows = [rows_low[:, STEP * e : STEP * (e + 1)] for e in range(2)]
         for e in range(2):

@@ -35,9 +35,12 @@ RUN = 4
 SCALES_AT = P - K_PASSES * QUADRANTS * SCALE_ROWS
 OWN = 12
 SHARED = 5 * BANK // 2
+EARLY_W4, EARLY_V = 2 * P, BANK
+EARLY = EARLY_W4 + EARLY_V
+LATE = 2 * S - EARLY
 
 AT_CUB = 0
-AT_PLANES = 59
+AT_EARLY, AT_LATE = 59, 60.5
 AT_WGS, AT_TAB_SCALES, AT_PICKED, AT_W4_SCALES, AT_W4_LOW_RAW = 1, 2, 233, 6, 78
 AT_TABLE = (15, 31)
 AT_IDENTITY, AT_SQUARES = 233.5, 22
@@ -90,16 +93,16 @@ def tile_list_audiobook_banner_scores_kernel(
             nc.gpsimd.memset(rows[:SCALES_AT, :].bitcast(I32), 0)
             return rows
 
-        def load_w4(name, b, kib):
-            raw = place(name, [P, K_PASSES, H], U8, kib)
-            nc.sync.dma_start(raw[:].bitcast(I32), w4_words.rearrange("a q n -> q a n")[:, :, H * b : H * (b + 1)].bitcast(I32))
+        def load_w4(name, b, kib, span=K_PASSES):
+            raw = place(name, [P, span, H], U8, kib)[:, :K_PASSES, :]
+            nc.sync.dma_start(raw.bitcast(I32), w4_words.rearrange("a q n -> q a n")[:, :, H * b : H * (b + 1)].bitcast(I32))
             return raw
 
         def deal(copy, b, raw):
             dealt = place("w4_dealt%d" % b, [P, K_PASSES, H], U8, AT_W4[b])
             copy(
                 dealt[:].bitcast(U16).rearrange("q a (t m) -> q a t m", m=P),
-                raw[:].bitcast(U16).rearrange("q a (m t) -> q a t m", t=PACK),
+                raw.bitcast(U16).rearrange("q a (m t) -> q a t m", t=PACK),
             )
             return dealt
 
@@ -109,7 +112,7 @@ def tile_list_audiobook_banner_scores_kernel(
         w4_scale_raw = load_scale_rows("w4_scale_raw", w4_scales, H, AT_W4_SCALES)
         wgs_first = place("wgs_first", [P, BANK], F32, AT_WGS_FIRST)
         nc.sync.dma_start(wgs_first[:QUADRANT, :], wgs_rows[:, :BANK])
-        w4_low_raw = load_w4("w4_low_raw", 0, AT_W4_LOW_RAW)
+        w4_low_raw = load_w4("w4_low_raw", 0, AT_W4_LOW_RAW, 10)
         shelved = load_list("shelved", offs2)
 
         def load_table(a):
@@ -118,18 +121,18 @@ def tile_list_audiobook_banner_scores_kernel(
             return words
 
         tab_sb = [load_table(0)]
+        promoted = load_list("promoted", offs3)
+        banner_slots = load_list("banner_slots", offs4)
         tab_sb.append(load_table(1))
         cub_sb = place("cub_sb", [P, H_PASSES, PACK], F32, AT_CUB)
         nc.sync.dma_start(cub_sb[:], cub.rearrange("(b q t) -> q b t", b=H_PASSES, t=PACK))
-        promoted = load_list("promoted", offs3)
-        banner_slots = load_list("banner_slots", offs4)
 
-        planes = place("planes", [P, K_PASSES * 2 * S], U8, AT_PLANES)
-        nc.gpsimd.memset(planes[:].bitcast(I32), 0)
+        early = place("early", [P, K_PASSES * EARLY], U8, AT_EARLY)
+        late = place("late", [P, K_PASSES * LATE], U8, AT_LATE)
+        for planes in (early, late):
+            nc.gpsimd.memset(planes[:].bitcast(I32), 0)
         pages = [place("page0", [P, T2], F32, AT_PAGE[0])]
         nc.gpsimd.memset(pages[0][:], 0.0)
-        banners = [place("banner0", [P, T2], F32, AT_BANNER[0])]
-        nc.vector.memset(banners[0][:], 0.0)
 
         picked_scales = place("picked_scales", [P, S], U8, AT_PICKED)
         staged = place("staged", [P, 2 * S], U8, AT_STAGED)
@@ -138,19 +141,24 @@ def tile_list_audiobook_banner_scores_kernel(
         def double_wgs_first(filled):
             nc.vector.tensor_copy(wgs_first[filled : 2 * filled, :].bitcast(I32), wgs_first[:filled, :].bitcast(I32))
 
-        double_wgs_first(QUADRANT)
+        def move_scales(queue, planes, lo, hi):
+            rows = K_PASSES * SCALE_ROWS
+            for quadrant in (0, 2, 1, 3):
+                queue.dma_start(
+                    planes[QUADRANT * quadrant : QUADRANT * quadrant + SCALE_ROWS, :].bitcast(I32),
+                    staged[SCALES_AT + rows * quadrant : SCALES_AT + rows * (quadrant + 1), lo:hi].bitcast(I32),
+                )
+
         nc.vector.tensor_copy(
-            staged[:, :H].rearrange("q (b t m) -> q b t m", t=PACK, m=P),
+            staged[:, EARLY_V : EARLY_V + H].rearrange("q (b t m) -> q b t m", t=PACK, m=P),
             w4_scale_raw[:].rearrange("q (b m t) -> q b t m", b=H_PASSES, t=PACK),
         )
+        nc.vector.tensor_copy(staged[:, :EARLY_V].bitcast(I32), picked_scales[:, :EARLY_V].bitcast(I32))
+        move_scales(nc.scalar, early, 0, EARLY)
+        double_wgs_first(QUADRANT)
         double_wgs_first(2 * QUADRANT)
-        nc.vector.tensor_copy(staged[:, H:].bitcast(I32), picked_scales[:].bitcast(I32))
-        rows = K_PASSES * SCALE_ROWS
-        for quadrant in (0, 2, 1, 3):
-            nc.scalar.dma_start(
-                planes[QUADRANT * quadrant : QUADRANT * quadrant + SCALE_ROWS, :].bitcast(I32),
-                staged[SCALES_AT + rows * quadrant : SCALES_AT + rows * (quadrant + 1), :].bitcast(I32),
-            )
+        nc.vector.tensor_copy(staged[:, EARLY_V + H :].bitcast(I32), picked_scales[:, EARLY_V:].bitcast(I32))
+        move_scales(nc.sync, late, EARLY, 2 * S)
         w4_dealt = {0: deal(nc.vector.tensor_copy, 0, w4_low_raw)}
 
         codes = [place("v_codes%d" % a, [P, S], U32, AT_CODES[a]) for a in range(K_PASSES)]
@@ -159,10 +167,15 @@ def tile_list_audiobook_banner_scores_kernel(
             nc.vector.tensor_copy(codes[1][:, lo:hi], tab_sb[1][:].indirect(part(listed, lo, hi)))
 
         def w4_scale(a, i):
-            return planes[:, 2 * S * a + P * i : 2 * S * a + P * (i + 1)]
+            at = P * i - EARLY_W4
+            if at < 0:
+                return early[:, EARLY * (a + 1) + at : EARLY * (a + 1) + at + P]
+            return late[:, LATE * a + at : LATE * a + at + P]
 
         def v_scale(a, lo, hi):
-            return planes[:, 2 * S * a + H + lo : 2 * S * a + H + hi]
+            if hi <= EARLY_V:
+                return early[:, EARLY * a + lo : EARLY * a + hi]
+            return late[:, LATE * (a + 1) - S + lo : LATE * (a + 1) - S + hi]
 
         for i in range(1, PAGES):
             page = place("page%d" % i, [P, T2], F32, AT_PAGE[i])
@@ -170,6 +183,8 @@ def tile_list_audiobook_banner_scores_kernel(
             pages.append(page)
         identity = place("identity", [P, P], F32, AT_IDENTITY)
         make_identity(nc, identity[:])
+        banners = [place("banner0", [P, T2], F32, AT_BANNER[0])]
+        nc.gpsimd.memset(banners[0][:], 0.0)
 
         wgs_sb = place("wgs_sb", [P, PACK * S], F32, AT_WGS)
         for lo, hi in ((BANK, 3 * BANK), (3 * BANK, 5 * BANK), (5 * BANK, PACK * S), (0, BANK)):

@@ -39,7 +39,7 @@ EARLY_W4, EARLY_V = 2 * P, BANK
 EARLY = EARLY_W4 + EARLY_V
 LATE = 2 * S - EARLY
 
-AT_CUB = 0
+AT_CUB, AT_WARM = 0, 0.5
 AT_EARLY, AT_LATE = 59, 60.5
 AT_WGS, AT_TAB_SCALES, AT_PICKED, AT_W4_SCALES, AT_W4_LOW_RAW = 1, 2, 233, 6, 78
 AT_TABLE = (15, 31)
@@ -48,19 +48,20 @@ AT_W4_HIGH_RAW = 31
 AT_CODES, AT_W4, AT_STAGED = (47, 51), (55, 57), 230
 AT_PAGE = (63, 71, 79)
 AT_BANNER = (87, 9)
-AT_FEATURES = (95, 111)
-AT_PAIRS = (119, 135)
-AT_ODD_SHELF, AT_SHELF_5, AT_SHELF_LAST = 151, 1, 22
-AT_TURNED, AT_WGS_FIRST, AT_BASE = 159, 164, 168
-AT_FACTOR_FIRST, AT_GAIN_FIRST = (166, 168), 168
+AT_FEATURES = 95
+AT_PAIRS = (119, 137)
+AT_ODD_SHELF, AT_SHELF_5, AT_SHELF_LAST = 153, 1, 22
+AT_TURNED, AT_WGS_FIRST, AT_BASE = 161, 166, 170
+AT_FACTOR_FIRST, AT_GAIN_FIRST = (168, 170), 170
 AT_Z_ROWS = 222
 AT_W2_RAW, AT_W2_GROUPED, AT_WGO = 47, 9, 47
 AT_GROUPED = (31, 119)
-AT_Z_CODES, AT_Z_SCALE = (111, 151), (71, 73)
-AT_W2_CODES, AT_W2_SCALE = (99, 119, 121), (100, 75)
-AT_Y = (170, 170, 178, 186)
-AT_PICKS = (194, 198, 202, 206)
-AT_SCORE = (210, 119, 121, 214, 218)
+AT_Z_CODES, AT_Z_SCALE = (103, 153), (22, 24)
+AT_Z_TAIL = 137
+AT_W2_CODES, AT_W2_SCALE = (63, 119, 121), (64, 26)
+AT_Y = (172, 172, 180, 188)
+AT_PICKS = (196, 200, 204, 208)
+AT_SCORE = (212, 119, 121, 214, 218)
 BANK_OF = (None, 3, 2, 4, 5, 6, 7, 0, 1, 2, 3, 4, 5, 6, 5, 7)
 
 
@@ -159,6 +160,8 @@ def tile_list_audiobook_banner_scores_kernel(
         double_wgs_first(2 * QUADRANT)
         nc.vector.tensor_copy(staged[:, EARLY_V + H :].bitcast(I32), picked_scales[:, EARLY_V:].bitcast(I32))
         move_scales(nc.sync, late, EARLY, 2 * S)
+        warm = place("warm", [P, 1], F32, AT_WARM)
+        nc.scalar.activation(warm[:], wgs_first[:, :1], ACT.Sigmoid)
         w4_dealt = {0: deal(nc.vector.tensor_copy, 0, w4_low_raw)}
 
         codes = [place("v_codes%d" % a, [P, S], U32, AT_CODES[a]) for a in range(K_PASSES)]
@@ -186,16 +189,19 @@ def tile_list_audiobook_banner_scores_kernel(
         banners = [place("banner0", [P, T2], F32, AT_BANNER[0])]
         nc.gpsimd.memset(banners[0][:], 0.0)
 
-        wgs_sb = place("wgs_sb", [P, PACK * S], F32, AT_WGS)
+        wgs_all = place("wgs_all", [P, BANK + PACK * S], F32, AT_WGS)
+        wgs_sb = wgs_all[:, BANK:]
         for lo, hi in ((BANK, 3 * BANK), (3 * BANK, 5 * BANK), (5 * BANK, PACK * S), (0, BANK)):
             for quadrant in (0, 2, 1, 3):
                 nc.sync.dma_start(wgs_sb[QUADRANT * quadrant : QUADRANT * (quadrant + 1), lo:hi], wgs_rows[:, lo:hi])
+        for quadrant in (0, 2, 1, 3):
+            nc.sync.dma_start(wgs_all[QUADRANT * quadrant : QUADRANT * (quadrant + 1), :BANK], wgs_rows[:, PACK * S - BANK :])
 
         by_tile = shelf.rearrange("(b q t) c -> b t q c", b=H_PASSES, t=PACK)
-        pairs = [place("pairs%d" % b, [P, 2 * T2], F32, AT_PAIRS[b]) for b in range(H_PASSES)]
+        pairs = [place("pairs%d" % b, [P, 2 * T2 + spare], F32, AT_PAIRS[b]) for b, spare in enumerate((BANK, 0))]
         odd_shelf = place("odd_shelf", [P, T2], F32, AT_ODD_SHELF)
         z_rows = place("z_rows", [P, 2 * T2], BF16, AT_Z_ROWS)
-        shelf_sb = {0: pairs[0][:, :T2], 1: odd_shelf[:], 2: pairs[0][:, T2:], 3: odd_shelf[:], 4: pairs[1][:, :T2], 6: pairs[1][:, T2:]}
+        shelf_sb = {0: odd_shelf[:], 1: odd_shelf[:], 2: pairs[0][:, T2 : 2 * T2], 3: odd_shelf[:], 4: pairs[1][:, :T2], 6: pairs[1][:, T2:]}
 
         def load_shelf(i):
             if i not in shelf_sb:
@@ -207,18 +213,15 @@ def tile_list_audiobook_banner_scores_kernel(
             if i in (4, 5):
                 return z_rows[:, T2 * t + lo : T2 * t + hi]
             at = T2 * (t // 2)
-            return pairs[b][:].bitcast(BF16).rearrange("q (c e) -> q c e", e=2)[:, at + lo : at + hi, t % 2]
+            return pairs[b][:, : 2 * T2].bitcast(BF16).rearrange("q (c e) -> q c e", e=2)[:, at + lo : at + hi, t % 2]
 
-        rows_low = place("rows_low", [P, PACK * S], F32, AT_FEATURES[0])
-        rows_mid = place("rows_mid", [P, 2 * S], F32, AT_FEATURES[1])
+        rows_low = place("rows_low", [P, 6 * S], F32, AT_FEATURES)
         held = shelf_sb[6]
         squares = place("squares", [P, 2 * BANK], F32, AT_SQUARES)
         made = []
         banks = {}
 
         def feature_cols(u, count):
-            if u in range(8, 12):
-                return rows_mid[:, BANK * (u - 8) : BANK * (u - 8 + count)]
             return rows_low[:, BANK * (u % 12) : BANK * (u % 12 + count)]
 
         def first_pass(acc, i, a, moving, lo, hi, start, stop):
@@ -270,8 +273,8 @@ def tile_list_audiobook_banner_scores_kernel(
         def gains(first, count, host, gain):
             for e in range(count):
                 product(first + e, host[:, BANK * e : BANK * (e + 1)])
-            at = BANK * first % (PACK * S)
-            nc.gpsimd.tensor_tensor(gain, host[:, : BANK * count], wgs_sb[:, at : at + BANK * count], MULT)
+            at = BANK * ((first + 1) % 8 if first == 7 else first % 8 + 1)
+            nc.gpsimd.tensor_tensor(gain, host[:, : BANK * count], wgs_all[:, at : at + BANK * count], MULT)
 
         def features(first, count):
             for u in range(first, first + count):
@@ -290,30 +293,31 @@ def tile_list_audiobook_banner_scores_kernel(
                 grouped[b] = place("grouped%d" % b, [P, PACK * T2], BF16, AT_GROUPED[b])
             nc.scalar.copy(
                 grouped[b][:, PACK * lo : PACK * hi].bitcast(U32).rearrange("q (c w) -> q c w", w=2),
-                pairs[b][:].bitcast(U32).rearrange("q (w c) -> q c w", w=2)[:, lo:hi, :],
+                pairs[b][:, : 2 * T2].bitcast(U32).rearrange("q (w c) -> q c w", w=2)[:, lo:hi, :],
             )
 
         shelve(0, 0, BANK)
         gains(2, 1, feature_cols(2, 1), gain_first[:])
-        gains(1, 1, feature_cols(1, 1), feature_cols(1, 1))
-        gains(3, 2, shelf_sb[0], feature_cols(3, 2))
+        gains(1, 1, shelf_sb[0], feature_cols(1, 1))
         load_shelf(0)
+        gains(3, 2, feature_cols(3, 2), feature_cols(3, 2))
         features(2, 1)
         features(1, 1)
         shelve(0, BANK, S)
         base_sb = place("base_sb", [P, N_TILES], F32, AT_BASE)
         with nc.allow_non_contiguous_dma(reason="one bias value a partition"):
             nc.sync.dma_start(base_sb[:], base.rearrange("(c q) -> q c", q=P))
-        gains(5, 3, shelf_sb[1], feature_cols(5, 3))
-        load_shelf(1)
+        gains(5, 2, feature_cols(5, 2), feature_cols(5, 2))
         w4_dealt[1] = deal(nc.scalar.copy, 1, w4_high_raw)
         features(3, 2)
         shelve(1)
         shelf_product(0)
-        gains(8, 4, shelf_sb[2], feature_cols(8, 4))
+        load_shelf(1)
+        gains(7, 5, pairs[0][:, T2:], feature_cols(7, 5))
         load_shelf(2)
-        features(5, 3)
+        features(5, 2)
         shelve(2)
+        features(7, 2)
         shelve(3)
         shelf_product(1)
         load_shelf(3)
@@ -323,7 +327,7 @@ def tile_list_audiobook_banner_scores_kernel(
         nc.sync.dma_start(w2_raw[:], w2.rearrange("(b q t) n -> q b (t n)", b=H_PASSES, t=PACK))
         load_shelf(4)
         load_shelf(5)
-        features(8, 4)
+        features(9, 3)
         shelve(4)
         shelf_product(2)
         shelve(5)
@@ -366,7 +370,14 @@ def tile_list_audiobook_banner_scores_kernel(
         shelf_product(6)
         shelf_product(LAST, SHARED, T2)
 
-        z_codes = [place("z_codes%d" % b, [P, T2], U32, AT_Z_CODES[b]) for b in range(H_PASSES)]
+        z_tiles = [place("z_codes%d" % b, [P, T2], U32, AT_Z_CODES[b]) for b in range(H_PASSES)]
+        z_tail = place("z_tail", [P, BANK], U32, AT_Z_TAIL)
+
+        def z_codes(b, lo, hi):
+            if b == 0 and lo >= T2 - BANK:
+                return z_tail[:, lo - T2 + BANK : hi - T2 + BANK]
+            return z_tiles[b][:, lo:hi]
+
         z_scale = [place("z_scale%d" % b, [P, T2], U8, AT_Z_SCALE[b]) for b in range(H_PASSES)]
         w2_parts = ((0, 1), (1, 2), (2, N_TILES))
         w2_tiles = {
@@ -390,7 +401,7 @@ def tile_list_audiobook_banner_scores_kernel(
 
         def quantise_z(b, lo, hi):
             nc.vector.quantize_mx(
-                out=z_codes[b][:, lo:hi].bitcast(FP8X4), scales=z_scale[b][:, lo:hi], in_=grouped[b][:, PACK * lo : PACK * hi]
+                out=z_codes(b, lo, hi).bitcast(FP8X4), scales=z_scale[b][:, lo:hi], in_=grouped[b][:, PACK * lo : PACK * hi]
             )
 
         def second_pass(acc, n, b, lo, hi):
@@ -398,17 +409,19 @@ def tile_list_audiobook_banner_scores_kernel(
             first = min(n, w2_parts[-1][0])
             within = at - P * H_PASSES * first
             nc.tensor.matmul_mx(
-                out=acc[:, lo % BANK : lo % BANK + hi - lo],
+                out=acc[:, : hi - lo],
                 lhsT=w2_tiles[first][:, within : within + P].bitcast(FP8X4),
                 lhsT_scale=w2_scale(at, at + P),
-                rhs=z_codes[b][:, lo:hi].bitcast(FP8X4),
+                rhs=z_codes(b, lo, hi).bitcast(FP8X4),
                 rhs_scale=z_scale[b][:, lo:hi],
                 start=(b == 0),
-                stop=(b == H_PASSES - 1 and hi % BANK == 0),
+                stop=(b == H_PASSES - 1),
             )
 
         chunks = range(0, T2, BANK)
-        accs_first = [bank("y0_%d" % c, c) for c in range(len(chunks))]
+        pieces = (0, BANK, 2 * BANK, 3 * BANK, T2 - BANK // 2, T2)
+        spans_first = list(zip(pieces, pieces[1:]))
+        accs_first = [bank("y0_%d" % c, c) for c in range(len(spans_first))]
         quantise_w2(0, 1)
         cuts = (0, BANK // 2, BANK, 2 * BANK, 3 * BANK, T2 - BANK // 2, T2)
         for lo, hi in zip(cuts, cuts[1:]):
@@ -418,14 +431,13 @@ def tile_list_audiobook_banner_scores_kernel(
                 nc.vector.tensor_tensor(z_of(LAST, lo, end), rows_last, pages[LAST % PAGES][:, lo:end], MULT)
             merge(1, lo, hi)
 
-        pieces = (0, BANK, 2 * BANK, 3 * BANK, T2 - BANK // 2, T2)
-        for lo, hi in zip(pieces, pieces[1:]):
-            if lo % S == 0:
-                quantise_z(0, lo, lo + S)
-                for at in (lo, lo + BANK):
-                    second_pass(accs_first[at // BANK], 0, 0, at, at + BANK)
+        ahead = {0: S, S: 3 * BANK, 3 * BANK: T2}
+        for acc, (lo, hi) in zip(accs_first, spans_first):
+            if lo in ahead:
+                quantise_z(0, lo, ahead[lo])
+            second_pass(acc, 0, 0, lo, hi)
             quantise_z(1, lo, hi)
-            second_pass(accs_first[lo // BANK], 0, 1, lo, hi)
+            second_pass(acc, 0, 1, lo, hi)
         quantise_w2(1, 2)
         quantise_w2(2, N_TILES)
         banner = place("banner1", [P, T2], F32, AT_BANNER[1])
@@ -436,14 +448,15 @@ def tile_list_audiobook_banner_scores_kernel(
 
         def picked(n, width):
             y = place("y%d" % n, [P, T2], F32, AT_Y[n])
-            accs = accs_first
+            accs, cols = accs_first, spans_first
             if n > 0:
+                cols = [(lo, lo + BANK) for lo in chunks]
                 accs = [bank("y%d_%d" % (n, c), PACK * (n % 2) + c) for c in range(len(chunks))]
                 for b in range(H_PASSES):
                     for acc, lo in zip(accs, chunks):
                         second_pass(acc, n, b, lo, lo + BANK)
-            for acc, lo in zip(accs, chunks):
-                nc.scalar.copy(y[:, lo : lo + BANK], acc[:])
+            for acc, (lo, hi) in zip(accs, cols):
+                nc.scalar.copy(y[:, lo:hi], acc[:, : hi - lo])
             both[n] = place("picks%d" % n, [P, PICKS], F32, AT_PICKS[n])
             for lo in range(0, PICKS, width):
                 nc.vector.tensor_copy(both[n][:, lo : lo + width], y[:].indirect(part(promoted, lo, lo + width)))

@@ -45,14 +45,15 @@ AT_WGS, AT_TAB_SCALES, AT_PICKED, AT_W4_SCALES, AT_W4_LOW_RAW = 1, 2, 233, 6, 78
 AT_TABLE = (15, 31)
 AT_IDENTITY, AT_SQUARES = 233.5, 22
 AT_W4_HIGH_RAW = 31
-AT_CODES, AT_W4, AT_STAGED = (47, 51), (55, 57), 230
+AT_CODES, AT_W4, AT_STAGED = (47, 51), (55, 57, 236), 230
 AT_PAGE = (63, 71, 79)
 AT_BANNER = (87, 9)
 AT_FEATURES = 95
 AT_PAIRS = (119, 137)
 AT_ODD_SHELF, AT_SHELF_5, AT_SHELF_LAST = 153, 1, 22
-AT_TURNED, AT_WGS_FIRST, AT_BASE = 161, 166, 170
-AT_FACTOR_FIRST, AT_GAIN_FIRST = (168, 170), 170
+AT_TURNED, AT_WGS_FIRST, AT_BASE = 161, 166, 168
+AT_FACTOR_FIRST, AT_GAIN_FIRST = (168, 153), 153
+AT_HOSTS = (226, 222, 234)
 AT_Z_ROWS = 222
 AT_W2_RAW, AT_W2_GROUPED, AT_WGO = 47, 9, 47
 AT_GROUPED = (31, 119)
@@ -99,13 +100,16 @@ def tile_list_audiobook_banner_scores_kernel(
             nc.sync.dma_start(raw.bitcast(I32), w4_words.rearrange("a q n -> q a n")[:, :, H * b : H * (b + 1)].bitcast(I32))
             return raw
 
-        def deal(copy, b, raw):
-            dealt = place("w4_dealt%d" % b, [P, K_PASSES, H], U8, AT_W4[b])
+        def deal(copy, name, raw, first, count, kib):
+            dealt = place(name, [P, K_PASSES, 2 * P * count], U8, kib)
             copy(
                 dealt[:].bitcast(U16).rearrange("q a (t m) -> q a t m", m=P),
-                raw.bitcast(U16).rearrange("q a (m t) -> q a t m", t=PACK),
+                raw.bitcast(U16).rearrange("q a (m t) -> q a t m", t=PACK)[:, :, first % PACK : first % PACK + count],
             )
-            return dealt
+            for e in range(count):
+                w4_dealt[first + e] = dealt[:, :, 2 * P * e : 2 * P * (e + 1)]
+
+        w4_dealt = {}
 
         wgs_rows = wgs.rearrange("(q t) j -> q (t j)", t=PACK)
         listed = load_list("listed", offs)
@@ -162,7 +166,7 @@ def tile_list_audiobook_banner_scores_kernel(
         move_scales(nc.sync, late, EARLY, 2 * S)
         warm = place("warm", [P, 1], F32, AT_WARM)
         nc.scalar.activation(warm[:], wgs_first[:, :1], ACT.Sigmoid)
-        w4_dealt = {0: deal(nc.vector.tensor_copy, 0, w4_low_raw)}
+        deal(nc.vector.tensor_copy, "w4_low", w4_low_raw, 0, PACK, AT_W4[0])
 
         codes = [place("v_codes%d" % a, [P, S], U32, AT_CODES[a]) for a in range(K_PASSES)]
         nc.vector.tensor_copy(codes[0][:], tab_sb[0][:].indirect(listed[:]))
@@ -225,10 +229,9 @@ def tile_list_audiobook_banner_scores_kernel(
             return rows_low[:, BANK * (u % 12) : BANK * (u % 12 + count)]
 
         def first_pass(acc, i, a, moving, lo, hi, start, stop):
-            b, t = divmod(i, PACK)
             nc.tensor.matmul_mx(
                 out=acc,
-                lhsT=w4_dealt[b][:, a, 2 * P * t : 2 * P * (t + 1)].bitcast(FP4X4),
+                lhsT=w4_dealt[i][:, a, :].bitcast(FP4X4),
                 lhsT_scale=w4_scale(a, i),
                 rhs=moving.bitcast(FP8X4),
                 rhs_scale=v_scale(a, lo, hi),
@@ -278,7 +281,7 @@ def tile_list_audiobook_banner_scores_kernel(
 
         def features(first, count):
             for u in range(first, first + count):
-                nc.vector.tensor_tensor(feature_cols(u, 1), banks[u][:], gain_first[:] if u == 2 else feature_cols(u, 1), MULT)
+                nc.vector.tensor_tensor(feature_cols(u, 1), banks[u][:], feature_cols(u, 1), MULT)
 
         def shelve(i, lo=0, hi=S):
             nc.vector.tensor_copy(pages[i % PAGES][:].indirect(part(shelved, lo, hi)), feature_cols(2 * i, 2)[:, lo:hi])
@@ -297,18 +300,19 @@ def tile_list_audiobook_banner_scores_kernel(
             )
 
         shelve(0, 0, BANK)
-        gains(2, 1, feature_cols(2, 1), gain_first[:])
-        gains(1, 1, shelf_sb[0], feature_cols(1, 1))
-        load_shelf(0)
-        gains(3, 2, feature_cols(3, 2), feature_cols(3, 2))
-        features(2, 1)
+        gains(2, 1, place("host2", [P, BANK], F32, AT_HOSTS[0])[:], gain_first[:])
+        nc.vector.tensor_tensor(feature_cols(2, 1)[:, :STEP], banks[2][:, :STEP], gain_first[:, :STEP], MULT)
+        gains(1, 1, feature_cols(2, 2)[:, STEP : STEP + BANK], feature_cols(1, 1))
+        gains(3, 2, place("host3", [P, S], F32, AT_HOSTS[1])[:], feature_cols(3, 2))
         features(1, 1)
+        nc.vector.tensor_tensor(feature_cols(2, 1)[:, STEP:], banks[2][:, STEP:], gain_first[:, STEP:], MULT)
+        load_shelf(0)
         shelve(0, BANK, S)
         base_sb = place("base_sb", [P, N_TILES], F32, AT_BASE)
         with nc.allow_non_contiguous_dma(reason="one bias value a partition"):
             nc.sync.dma_start(base_sb[:], base.rearrange("(c q) -> q c", q=P))
-        gains(5, 2, feature_cols(5, 2), feature_cols(5, 2))
-        w4_dealt[1] = deal(nc.scalar.copy, 1, w4_high_raw)
+        gains(5, 2, place("host5", [P, S], F32, AT_HOSTS[2])[:], feature_cols(5, 2))
+        deal(nc.scalar.copy, "w4_mid", w4_high_raw, PACK, 2, AT_W4[1])
         features(3, 2)
         shelve(1)
         shelf_product(0)
@@ -321,6 +325,7 @@ def tile_list_audiobook_banner_scores_kernel(
         shelve(3)
         shelf_product(1)
         load_shelf(3)
+        deal(nc.scalar.copy, "w4_high", w4_high_raw, PACK + 2, 2, AT_W4[2])
         gains(12, 4, shelf_sb[4], feature_cols(12, 4))
         load_shelf(LAST)
         w2_raw = place("w2_raw", [P, H_PASSES, PACK * N], F32, AT_W2_RAW)

from contextlib import ExitStack

import concourse.mybir as mybir
from concourse.masks import make_identity

K, T, S, H, T2, PICKS, N = 1024, 4096, 1024, 1024, 2048, 1024, 512
FLOPS = 2 * K * H * S + 2 * H * N * T2

F32 = mybir.dt.float32
BF16 = mybir.dt.bfloat16
I32 = mybir.dt.int32
U32 = mybir.dt.uint32
U16 = mybir.dt.uint16
U8 = mybir.dt.uint8
FP8X4 = mybir.dt.float8_e4m3fn_x4
FP4X4 = mybir.dt.float4_e2m1fn_x4
ACT = mybir.ActivationFunctionType
MULT = mybir.AluOpType.mult

P = 128
QUADRANT = 32
QUADRANTS = P // QUADRANT
SCALE_ROWS = 4
PACK = 4
BANK = 512
STEP = BANK // 2
PER_COLUMN = 16
K_PASSES = K // (P * PACK)
H_PASSES = H // (P * PACK)
ROW_TILES = H_PASSES * PACK
LAST = ROW_TILES - 1
N_TILES = N // P
PAGES = 3
RUN = 4
SCALES_AT = P - K_PASSES * QUADRANTS * SCALE_ROWS
OWN = 12
SHARED = 5 * BANK // 2
EARLY_W4, EARLY_V = 2 * P, BANK
EARLY = EARLY_W4 + EARLY_V
LATE = 2 * S - EARLY

AT_CUB, AT_WARM = 0, 0.5
AT_EARLY, AT_LATE = 59, 60.5
AT_WGS, AT_TAB_SCALES, AT_PICKED, AT_W4_SCALES, AT_W4_LOW_RAW = 1, 2, 233, 6, 78
AT_TABLE = (15, 31)
AT_IDENTITY, AT_SQUARES = 233.5, 22
AT_W4_HIGH_RAW = 31
AT_CODES, AT_W4, AT_STAGED = (47, 51), (55, 57, 236), 230
AT_PAGE = (63, 71, 79)
AT_BANNER = (87, 9)
AT_FEATURES = 95
AT_PAIRS = (119, 137)
AT_ODD_SHELF, AT_SHELF_5, AT_SHELF_LAST = 153, 1, 22
AT_TURNED, AT_WGS_FIRST, AT_BASE = 161, 166, 168
AT_FACTOR_FIRST, AT_GAIN_FIRST = (168, 153), 153
AT_HOSTS = (226, 222, 234)
AT_Z_ROWS = 222
AT_W2_RAW, AT_W2_GROUPED, AT_WGO = 47, 9, 47
AT_GROUPED = (31, 119)
AT_Z_CODES, AT_Z_SCALE = (103, 153), (22, 24)
AT_Z_TAIL = 137
AT_W2_CODES, AT_W2_SCALE = (63, 119, 121), (64, 26)
AT_Y = (172, 172, 180, 188)
AT_PICKS = (196, 200, 204, 208)
AT_SCORE = (212, 119, 121, 214, 218)
BANK_OF = (None, 3, 2, 4, 5, 6, 7, 0, 1, 2, 3, 4, 5, 6, 5, 7)


def tile_list_audiobook_banner_scores_kernel(
    tc, tab_words, tab_scales, offs, w4_words, w4_scales, cub, offs2, wgs, shelf, w2, offs3, base, offs4, wgo, out
):
    nc = tc.nc
    with ExitStack() as ctx:
        list_pool = ctx.enter_context(tc.tile_pool(name="lists", bufs=1))
        pool = ctx.enter_context(tc.tile_pool(name="sbuf", bufs=1))
        psum = ctx.enter_context(tc.psum_pool(name="psum", bufs=1))

        def place(name, shape, dtype, kib):
            return pool.tile(shape, dtype, name=name, offset=int(1024 * kib), align_bytes=64)

        def bank(name, index):
            return psum.tile([P, BANK], F32, name=name, offset=4 * BANK * index)

        def part(list_tile, lo, hi):
            return list_tile[:, lo // PER_COLUMN : hi // PER_COLUMN]

        def load_list(name, src):
            list_tile = list_pool.tile([P, S // PER_COLUMN], U16, name=name)
            nc.sync.dma_start(list_tile[:], src)
            return list_tile

        def load_scale_rows(name, src, width, kib):
            rows = place(name, [P, width], U8, kib)
            nc.sync.dma_start(rows[SCALES_AT:, :].bitcast(I32), src.rearrange("a r n -> r a n").bitcast(I32))
            nc.gpsimd.memset(rows[:SCALES_AT, :].bitcast(I32), 0)
            return rows

        def load_w4(name, b, kib, span=K_PASSES):
            raw = place(name, [P, span, H], U8, kib)[:, :K_PASSES, :]
            nc.sync.dma_start(raw.bitcast(I32), w4_words.rearrange("a q n -> q a n")[:, :, H * b : H * (b + 1)].bitcast(I32))
            return raw

        def deal(copy, name, raw, first, count, kib):
            dealt = place(name, [P, K_PASSES, 2 * P * count], U8, kib)
            copy(
                dealt[:].bitcast(U16).rearrange("q a (t m) -> q a t m", m=P),
                raw.bitcast(U16).rearrange("q a (m t) -> q a t m", t=PACK)[:, :, first % PACK : first % PACK + count],
            )
            for e in range(count):
                w4_dealt[first + e] = dealt[:, :, 2 * P * e : 2 * P * (e + 1)]

        w4_dealt = {}

        wgs_rows = wgs.rearrange("(q t) j -> q (t j)", t=PACK)
        listed = load_list("listed", offs)
        tab_scale_sb = load_scale_rows("tab_scale_sb", tab_scales, T, AT_TAB_SCALES)
        w4_scale_raw = load_scale_rows("w4_scale_raw", w4_scales, H, AT_W4_SCALES)
        wgs_first = place("wgs_first", [P, BANK], F32, AT_WGS_FIRST)
        nc.sync.dma_start(wgs_first[:QUADRANT, :], wgs_rows[:, :BANK])
        w4_low_raw = load_w4("w4_low_raw", 0, AT_W4_LOW_RAW, 10)
        shelved = load_list("shelved", offs2)

        def load_table(a):
            words = place("tab_sb%d" % a, [P, T], U32, AT_TABLE[a])
            nc.sync.dma_start(words[:].bitcast(I32), tab_words[a].rearrange("q n t -> q (n t)").bitcast(I32))
            return words

        tab_sb = [load_table(0)]
        promoted = load_list("promoted", offs3)
        banner_slots = load_list("banner_slots", offs4)
        tab_sb.append(load_table(1))
        cub_sb = place("cub_sb", [P, H_PASSES, PACK], F32, AT_CUB)
        nc.sync.dma_start(cub_sb[:], cub.rearrange("(b q t) -> q b t", b=H_PASSES, t=PACK))

        early = place("early", [P, K_PASSES * EARLY], U8, AT_EARLY)
        late = place("late", [P, K_PASSES * LATE], U8, AT_LATE)
        for planes in (early, late):
            nc.gpsimd.memset(planes[:].bitcast(I32), 0)
        pages = [place("page0", [P, T2], F32, AT_PAGE[0])]
        nc.gpsimd.memset(pages[0][:], 0.0)

        picked_scales = place("picked_scales", [P, S], U8, AT_PICKED)
        staged = place("staged", [P, 2 * S], U8, AT_STAGED)
        nc.vector.tensor_copy(picked_scales[:], tab_scale_sb[:].indirect(listed[:]))

        def double_wgs_first(filled):
            nc.vector.tensor_copy(wgs_first[filled : 2 * filled, :].bitcast(I32), wgs_first[:filled, :].bitcast(I32))

        def move_scales(queue, planes, lo, hi):
            rows = K_PASSES * SCALE_ROWS
            for quadrant in (0, 2, 1, 3):
                queue.dma_start(
                    planes[QUADRANT * quadrant : QUADRANT * quadrant + SCALE_ROWS, :].bitcast(I32),
                    staged[SCALES_AT + rows * quadrant : SCALES_AT + rows * (quadrant + 1), lo:hi].bitcast(I32),
                )

        nc.vector.tensor_copy(
            staged[:, EARLY_V : EARLY_V + H].rearrange("q (b t m) -> q b t m", t=PACK, m=P),
            w4_scale_raw[:].rearrange("q (b m t) -> q b t m", b=H_PASSES, t=PACK),
        )
        nc.vector.tensor_copy(staged[:, :EARLY_V].bitcast(I32), picked_scales[:, :EARLY_V].bitcast(I32))
        move_scales(nc.scalar, early, 0, EARLY)
        double_wgs_first(QUADRANT)
        double_wgs_first(2 * QUADRANT)
        nc.vector.tensor_copy(staged[:, EARLY_V + H :].bitcast(I32), picked_scales[:, EARLY_V:].bitcast(I32))
        move_scales(nc.sync, late, EARLY, 2 * S)
        warm = place("warm", [P, 1], F32, AT_WARM)
        nc.scalar.activation(warm[:], wgs_first[:, :1], ACT.Sigmoid)
        deal(nc.vector.tensor_copy, "w4_low", w4_low_raw, 0, PACK, AT_W4[0])

        codes = [place("v_codes%d" % a, [P, S], U32, AT_CODES[a]) for a in range(K_PASSES)]
        nc.vector.tensor_copy(codes[0][:], tab_sb[0][:].indirect(listed[:]))
        for lo, hi in ((0, STEP), (STEP, BANK), (BANK, S)):
            nc.vector.tensor_copy(codes[1][:, lo:hi], tab_sb[1][:].indirect(part(listed, lo, hi)))

        def w4_scale(a, i):
            at = P * i - EARLY_W4
            if at < 0:
                return early[:, EARLY * (a + 1) + at : EARLY * (a + 1) + at + P]
            return late[:, LATE * a + at : LATE * a + at + P]

        def v_scale(a, lo, hi):
            if hi <= EARLY_V:
                return early[:, EARLY * a + lo : EARLY * a + hi]
            return late[:, LATE * (a + 1) - S + lo : LATE * (a + 1) - S + hi]

        for i in range(1, PAGES):
            page = place("page%d" % i, [P, T2], F32, AT_PAGE[i])
            nc.gpsimd.memset(page[:], 0.0)
            pages.append(page)
        identity = place("identity", [P, P], F32, AT_IDENTITY)
        make_identity(nc, identity[:])
        banners = [place("banner0", [P, T2], F32, AT_BANNER[0])]
        nc.gpsimd.memset(banners[0][:], 0.0)

        wgs_all = place("wgs_all", [P, BANK + PACK * S], F32, AT_WGS)
        wgs_sb = wgs_all[:, BANK:]
        for lo, hi in ((BANK, 3 * BANK), (3 * BANK, 5 * BANK), (5 * BANK, PACK * S), (0, BANK)):
            for quadrant in (0, 2, 1, 3):
                nc.sync.dma_start(wgs_sb[QUADRANT * quadrant : QUADRANT * (quadrant + 1), lo:hi], wgs_rows[:, lo:hi])
        for quadrant in (0, 2, 1, 3):
            nc.sync.dma_start(wgs_all[QUADRANT * quadrant : QUADRANT * (quadrant + 1), :BANK], wgs_rows[:, PACK * S - BANK :])

        by_tile = shelf.rearrange("(b q t) c -> b t q c", b=H_PASSES, t=PACK)
        pairs = [place("pairs%d" % b, [P, 2 * T2 + spare], F32, AT_PAIRS[b]) for b, spare in enumerate((BANK, 0))]
        odd_shelf = place("odd_shelf", [P, T2], F32, AT_ODD_SHELF)
        z_rows = place("z_rows", [P, 2 * T2], BF16, AT_Z_ROWS)
        shelf_sb = {0: odd_shelf[:], 1: odd_shelf[:], 2: pairs[0][:, T2 : 2 * T2], 3: odd_shelf[:], 4: pairs[1][:, :T2], 6: pairs[1][:, T2:]}

        def load_shelf(i):
            if i not in shelf_sb:
                shelf_sb[i] = place("shelf%d" % i, [P, T2], F32, AT_SHELF_LAST if i == LAST else AT_SHELF_5)[:]
            nc.sync.dma_start(shelf_sb[i], by_tile[i // PACK, i % PACK])

        def z_of(i, lo, hi):
            b, t = divmod(i, PACK)
            if i in (4, 5):
                return z_rows[:, T2 * t + lo : T2 * t + hi]
            at = T2 * (t // 2)
            return pairs[b][:, : 2 * T2].bitcast(BF16).rearrange("q (c e) -> q c e", e=2)[:, at + lo : at + hi, t % 2]

        rows_low = place("rows_low", [P, 6 * S], F32, AT_FEATURES)
        held = shelf_sb[6]
        squares = place("squares", [P, 2 * BANK], F32, AT_SQUARES)
        made = []
        banks = {}

        def feature_cols(u, count):
            return rows_low[:, BANK * (u % 12) : BANK * (u % 12 + count)]

        def first_pass(acc, i, a, moving, lo, hi, start, stop):
            nc.tensor.matmul_mx(
                out=acc,
                lhsT=w4_dealt[i][:, a, :].bitcast(FP4X4),
                lhsT_scale=w4_scale(a, i),
                rhs=moving.bitcast(FP8X4),
                rhs_scale=v_scale(a, lo, hi),
                start=start,
                stop=stop,
            )

        def make_factor(factor, acc, i):
            b, t = divmod(i, PACK)
            at = BANK * (len(made) % 2)
            made.append(i)
            square = squares[:, at : at + acc.shape[1]]
            nc.scalar.activation(square, acc, ACT.Square)
            nc.scalar.activation(factor, square, ACT.Identity, bias=1.0, scale=cub_sb[:, b, t : t + 1])

        first_banks = [bank("first%d" % e, BANK_OF[4 + 2 * e])[:, :STEP] for e in range(2)]
        first_factors = [place("factor_first%d" % e, [P, BANK], F32, AT_FACTOR_FIRST[e])[:, :STEP] for e in range(2)]
        first_rows = [rows_low[:, STEP * e : STEP * (e + 1)] for e in range(2)]
        for e in range(2):
            lo, hi = STEP * e, STEP * (e + 1)
            for a in range(K_PASSES):
                first_pass(first_banks[e], 0, a, codes[a][:, lo:hi], lo, hi, a == 0, a == K_PASSES - 1)
            make_factor(first_factors[e], first_banks[e], 0)
        for e in range(2):
            nc.vector.tensor_tensor(first_rows[e], first_banks[e], wgs_first[:, STEP * e : STEP * (e + 1)], MULT)
        for e in range(2):
            nc.vector.tensor_tensor(first_rows[e], first_rows[e], first_factors[e], MULT)
        gain_first = place("gain_first", [P, BANK], F32, AT_GAIN_FIRST)
        w4_high_raw = load_w4("w4_high_raw", 1, AT_W4_HIGH_RAW)

        def product(u, factor):
            i, h = divmod(u, 2)
            acc = bank("p%d" % u, BANK_OF[u])
            lo, hi = BANK * h, BANK * (h + 1)
            for a in (1, 0):
                first_pass(acc[:], i, a, codes[a][:, lo:hi], lo, hi, a == 1, a == 0)
            make_factor(factor, acc[:], i)
            if u >= OWN:
                nc.scalar.copy(held[:, BANK * (u - OWN) : BANK * (u - OWN + 1)], acc[:])
            banks[u] = acc

        def gains(first, count, host, gain):
            for e in range(count):
                product(first + e, host[:, BANK * e : BANK * (e + 1)])
            at = BANK * ((first + 1) % 8 if first == 7 else first % 8 + 1)
            nc.gpsimd.tensor_tensor(gain, host[:, : BANK * count], wgs_all[:, at : at + BANK * count], MULT)

        def features(first, count):
            for u in range(first, first + count):
                nc.vector.tensor_tensor(feature_cols(u, 1), banks[u][:], feature_cols(u, 1), MULT)

        def shelve(i, lo=0, hi=S):
            nc.vector.tensor_copy(pages[i % PAGES][:].indirect(part(shelved, lo, hi)), feature_cols(2 * i, 2)[:, lo:hi])

        def shelf_product(i, lo=0, hi=T2):
            nc.gpsimd.tensor_tensor(z_of(i, lo, hi), pages[i % PAGES][:, lo:hi], shelf_sb[i][:, lo:hi], MULT)

        grouped = {}

        def merge(b, lo, hi):
            if b not in grouped:
                grouped[b] = place("grouped%d" % b, [P, PACK * T2], BF16, AT_GROUPED[b])
            nc.scalar.copy(
                grouped[b][:, PACK * lo : PACK * hi].bitcast(U32).rearrange("q (c w) -> q c w", w=2),
                pairs[b][:, : 2 * T2].bitcast(U32).rearrange("q (w c) -> q c w", w=2)[:, lo:hi, :],
            )

        shelve(0, 0, BANK)
        gains(2, 1, place("host2", [P, BANK], F32, AT_HOSTS[0])[:], gain_first[:])
        nc.vector.tensor_tensor(feature_cols(2, 1)[:, :STEP], banks[2][:, :STEP], gain_first[:, :STEP], MULT)
        gains(1, 1, feature_cols(2, 2)[:, STEP : STEP + BANK], feature_cols(1, 1))
        gains(3, 2, place("host3", [P, S], F32, AT_HOSTS[1])[:], feature_cols(3, 2))
        features(1, 1)
        nc.vector.tensor_tensor(feature_cols(2, 1)[:, STEP:], banks[2][:, STEP:], gain_first[:, STEP:], MULT)
        load_shelf(0)
        shelve(0, BANK, S)
        base_sb = place("base_sb", [P, N_TILES], F32, AT_BASE)
        with nc.allow_non_contiguous_dma(reason="one bias value a partition"):
            nc.sync.dma_start(base_sb[:], base.rearrange("(c q) -> q c", q=P))
        gains(5, 2, place("host5", [P, S], F32, AT_HOSTS[2])[:], feature_cols(5, 2))
        deal(nc.scalar.copy, "w4_mid", w4_high_raw, PACK, 2, AT_W4[1])
        features(3, 2)
        shelve(1)
        shelf_product(0)
        load_shelf(1)
        gains(7, 5, pairs[0][:, T2:], feature_cols(7, 5))
        load_shelf(2)
        features(5, 2)
        shelve(2)
        features(7, 2)
        shelve(3)
        shelf_product(1)
        load_shelf(3)
        deal(nc.scalar.copy, "w4_high", w4_high_raw, PACK + 2, 2, AT_W4[2])
        gains(12, 4, shelf_sb[4], feature_cols(12, 4))
        load_shelf(LAST)
        w2_raw = place("w2_raw", [P, H_PASSES, PACK * N], F32, AT_W2_RAW)
        nc.sync.dma_start(w2_raw[:], w2.rearrange("(b q t) n -> q b (t n)", b=H_PASSES, t=PACK))
        load_shelf(4)
        load_shelf(5)
        features(9, 3)
        shelve(4)
        shelf_product(2)
        shelve(5)
        nc.gpsimd.tensor_tensor(feature_cols(OWN, 4), feature_cols(OWN, 4), held, MULT)
        load_shelf(6)

        turned = place("turned", [P, SHARED], F32, AT_TURNED)
        spans = [(lo, min(lo + BANK, SHARED)) for lo in range(0, SHARED, BANK)]
        for c, (lo, hi) in enumerate(spans):
            there = bank("there%d" % c, 5 + c)
            for at in range(lo, hi, P):
                nc.tensor.transpose(there[:, at - lo : at - lo + P], shelf_sb[LAST][:, at : at + P], identity[:])
            nc.scalar.copy(turned[:, lo:hi], there[:, : hi - lo])
        shelf_banks = []
        for c, (lo, hi) in enumerate(spans):
            back = bank("back%d" % c, 5 + c)
            for at in range(lo, hi, P):
                nc.tensor.transpose(back[:, at - lo : at - lo + P], turned[:, at : at + P], identity[:])
            shelf_banks.append(back)

        shelf_product(3)
        shelve(6)
        w2_grouped = place("w2_grouped", [P, N_TILES * H_PASSES * P * PACK], BF16, AT_W2_GROUPED)
        for b in range(H_PASSES):
            nc.scalar.copy(
                w2_grouped[:].rearrange("q (n b c i t) -> q b n c t i", b=H_PASSES, n=N_TILES, i=RUN, t=PACK)[:, b],
                w2_raw[:, b, :].rearrange("q (t n c i) -> q n c t i", t=PACK, n=N_TILES, i=RUN),
            )
        wgo_sb = place("wgo_sb", [P, PICKS], F32, AT_WGO)
        nc.sync.dma_start(wgo_sb[:], wgo)
        for lo in range(0, T2, S):
            merge(0, lo, lo + S)
        shelf_product(4)
        shelve(LAST)
        shelf_product(5)
        nc.scalar.copy(
            pairs[1][:, :T2].bitcast(BF16).rearrange("q (c i t) -> q c t i", i=RUN, t=2),
            z_rows[:].rearrange("q (t c i) -> q c t i", t=2, i=RUN),
        )
        shelf_product(6)
        shelf_product(LAST, SHARED, T2)

        z_tiles = [place("z_codes%d" % b, [P, T2], U32, AT_Z_CODES[b]) for b in range(H_PASSES)]
        z_tail = place("z_tail", [P, BANK], U32, AT_Z_TAIL)

        def z_codes(b, lo, hi):
            if b == 0 and lo >= T2 - BANK:
                return z_tail[:, lo - T2 + BANK : hi - T2 + BANK]
            return z_tiles[b][:, lo:hi]

        z_scale = [place("z_scale%d" % b, [P, T2], U8, AT_Z_SCALE[b]) for b in range(H_PASSES)]
        w2_parts = ((0, 1), (1, 2), (2, N_TILES))
        w2_tiles = {
            first: place("w2_codes%d" % first, [P, (last - first) * H_PASSES * P], U32, AT_W2_CODES[first])
            for first, last in w2_parts
        }
        first_cols = H_PASSES * P
        scale_tiles = [
            place("w2_scale%d" % e, [P, width], U8, AT_W2_SCALE[e])
            for e, width in enumerate((first_cols, (N_TILES - 1) * first_cols))
        ]

        def w2_scale(lo, hi):
            return scale_tiles[0][:, lo:hi] if hi <= first_cols else scale_tiles[1][:, lo - first_cols : hi - first_cols]

        def quantise_w2(first, last):
            lo, hi = H_PASSES * P * first, H_PASSES * P * last
            nc.vector.quantize_mx(
                out=w2_tiles[first][:].bitcast(FP8X4), scales=w2_scale(lo, hi), in_=w2_grouped[:, PACK * lo : PACK * hi]
            )

        def quantise_z(b, lo, hi):
            nc.vector.quantize_mx(
                out=z_codes(b, lo, hi).bitcast(FP8X4), scales=z_scale[b][:, lo:hi], in_=grouped[b][:, PACK * lo : PACK * hi]
            )

        def second_pass(acc, n, b, lo, hi):
            at = P * (H_PASSES * n + b)
            first = min(n, w2_parts[-1][0])
            within = at - P * H_PASSES * first
            nc.tensor.matmul_mx(
                out=acc[:, : hi - lo],
                lhsT=w2_tiles[first][:, within : within + P].bitcast(FP8X4),
                lhsT_scale=w2_scale(at, at + P),
                rhs=z_codes(b, lo, hi).bitcast(FP8X4),
                rhs_scale=z_scale[b][:, lo:hi],
                start=(b == 0),
                stop=(b == H_PASSES - 1),
            )

        chunks = range(0, T2, BANK)
        pieces = (0, BANK, 2 * BANK, 3 * BANK, T2 - BANK // 2, T2)
        spans_first = list(zip(pieces, pieces[1:]))
        accs_first = [bank("y0_%d" % c, c) for c in range(len(spans_first))]
        quantise_w2(0, 1)
        cuts = (0, BANK // 2, BANK, 2 * BANK, 3 * BANK, T2 - BANK // 2, T2)
        for lo, hi in zip(cuts, cuts[1:]):
            if lo < SHARED:
                end = min(hi, SHARED)
                rows_last = shelf_banks[lo // BANK][:, lo % BANK : lo % BANK + end - lo]
                nc.vector.tensor_tensor(z_of(LAST, lo, end), rows_last, pages[LAST % PAGES][:, lo:end], MULT)
            merge(1, lo, hi)

        ahead = {0: S, S: 3 * BANK, 3 * BANK: T2}
        for acc, (lo, hi) in zip(accs_first, spans_first):
            if lo in ahead:
                quantise_z(0, lo, ahead[lo])
            second_pass(acc, 0, 0, lo, hi)
            quantise_z(1, lo, hi)
            second_pass(acc, 0, 1, lo, hi)
        quantise_w2(1, 2)
        quantise_w2(2, N_TILES)
        banner = place("banner1", [P, T2], F32, AT_BANNER[1])
        nc.gpsimd.memset(banner[:], 0.0)
        banners.append(banner)

        both = {}

        def picked(n, width):
            y = place("y%d" % n, [P, T2], F32, AT_Y[n])
            accs, cols = accs_first, spans_first
            if n > 0:
                cols = [(lo, lo + BANK) for lo in chunks]
                accs = [bank("y%d_%d" % (n, c), PACK * (n % 2) + c) for c in range(len(chunks))]
                for b in range(H_PASSES):
                    for acc, lo in zip(accs, chunks):
                        second_pass(acc, n, b, lo, lo + BANK)
            for acc, (lo, hi) in zip(accs, cols):
                nc.scalar.copy(y[:, lo:hi], acc[:, : hi - lo])
            both[n] = place("picks%d" % n, [P, PICKS], F32, AT_PICKS[n])
            for lo in range(0, PICKS, width):
                nc.vector.tensor_copy(both[n][:, lo : lo + width], y[:].indirect(part(promoted, lo, lo + width)))

        def show(n, lo, hi):
            score = place("score%d_%d" % (n, lo), [P, hi - lo], F32, AT_SCORE[n + (hi == PICKS)])[:]
            nc.scalar.activation(score, both[n][:, lo:hi], ACT.Sigmoid, bias=base_sb[:, n : n + 1])
            nc.vector.tensor_tensor(banners[n % 2][:].indirect(part(banner_slots, lo, hi)), score, wgo_sb[:, lo:hi], MULT)
            if hi == PICKS:
                queues = (nc.sync, nc.scalar) if n == N_TILES - 1 else (nc.sync,)
                width = T2 // len(queues)
                for k, queue in enumerate(queues):
                    cols = slice(width * k, width * (k + 1))
                    queue.dma_start(out[P * n : P * (n + 1), cols], banners[n % 2][:, cols])

        picked(0, PICKS // 2)
        show(0, 0, PICKS // 2)
        picked(1, PICKS)
        show(0, PICKS // 2, PICKS)
        for n in range(1, N_TILES):
            if n + 1 < N_TILES:
                picked(n + 1, PICKS)
            show(n, 0, PICKS)
